import numpy as np
import ml_dtypes


def mxq(x, axis, fmt="e4m3"):
    dtype, down = {"e4m3": (ml_dtypes.float8_e4m3fn, 7), "e5m2": (ml_dtypes.float8_e5m2, 14)}[fmt]
    v = np.moveaxis(np.asarray(x, np.float32).astype(ml_dtypes.bfloat16).astype(np.float64), axis, -1)
    blocks = v.reshape(v.shape[:-1] + (-1, 32))
    amax = np.abs(blocks).max(-1, keepdims=True)
    byte = np.maximum(np.where(amax > 0, np.frexp(amax)[1] - 1 + 127, 0) - down, 1)
    scale = np.exp2(byte - 127.0)
    codes = (blocks / scale).astype(np.float32).astype(dtype).astype(np.float64)
    return np.moveaxis((codes * scale).reshape(v.shape), -1, axis)


WIDE = False


def mx_kscale(k):
    if not WIDE:
        return np.ones(k)
    levels = np.array([10, -10, 5, -5, 0])
    if k % 512:
        return np.exp2(np.random.permutation(np.resize(levels, k // 32))).repeat(32)
    a = np.empty((k // 512, 16))
    for p in range(k // 512):
        a[p, :8] = np.random.permutation(np.resize(levels, 8))
        for g in range(8):
            far = levels[np.abs(levels - a[p, g]) >= 10]
            a[p, g + 8] = far[np.random.randint(len(far))]
    return np.exp2(a.ravel()).repeat(32)


def f64(x):
    return np.asarray(x).astype(np.float64)


def striped(idx):
    return np.tile(idx.reshape(-1, 16).T, (8, 1)).astype(np.uint16)


def unstriped(offs):
    return offs[:16].T.reshape(-1).astype(np.int64)


def striped8(idx):
    return np.concatenate([x.reshape(-1, 16).T for x in idx]).astype(np.uint16)


def runs(offs, k):
    lists = np.stack([offs[16 * r : 16 * r + 16].T.reshape(-1) for r in range(8)]).astype(np.int64)
    return lists[np.arange(k) % 512 // 64]


def pack_weight(w):
    k, n = w.shape
    w = f64(np.asarray(w, np.float32).astype(ml_dtypes.bfloat16)).reshape(k // 32, 32, n)
    amax = np.abs(w).max(1)
    byte = np.clip(np.where(amax > 0, np.frexp(amax)[1] - 1 + 127 - 7, 1), 1, 254)
    scaled = (w * np.exp2(127.0 - byte)[:, None, :]).reshape(k, n).astype(np.float32)
    words = np.ascontiguousarray(scaled.reshape(k // 512, 128, 4, n).transpose(0, 1, 3, 2)).astype(ml_dtypes.float8_e4m3fn).view(np.uint8)
    return words, np.ascontiguousarray(byte.astype(np.uint8).reshape(k // 512, 16, n))


def unpack_weight(words, scales):
    g, p, n, _ = words.shape
    vals = np.ascontiguousarray(words).view(ml_dtypes.float8_e4m3fn).astype(np.float64) * np.repeat(np.exp2(scales.astype(np.float64) - 127.0), 8, axis=1)[..., None]
    return vals.transpose(0, 1, 3, 2).reshape(g * 512, n)


def sigmoid(v):
    return 1.0 / (1.0 + np.exp(-np.maximum(v, -700.0)))


K, T, S, N = 512, 2048, 512, 512


def setup_inputs():
    n = np.random.standard_normal
    s = mx_kscale(K)[:, None]
    packed_xT = pack_weight(n((K, T)) * s)
    return {
        "x_words": packed_xT[0],
        "x_scales": packed_xT[1],
        "w1": (n((K, N)) / np.sqrt(K) / s).astype(np.float32),
        "w2": (n((K, N)) / np.sqrt(K) / s).astype(np.float32),
        "w3": (n((K, N)) / np.sqrt(K) / s).astype(np.float32),
        "num": n((N, S)).astype(np.float32),
        "den": np.random.uniform(0.5, 2.0, (N, S)).astype(np.float32),
        "offs": striped(np.random.permutation(T)[:S]),
        "par": striped8(np.random.randint(0, S, (8, S))),
    }


def reference(x_words, x_scales, w1, w2, w3, num, den, offs, par):
    xq = unpack_weight(x_words, x_scales)[:, unstriped(offs)]
    q = sigmoid(mxq(f64(w3), 0, "e4m3").T @ xq)
    ek = np.exp(0.5 * ((mxq(f64(w1), 0, "e4m3").T @ xq)))
    val = mxq(f64(w2), 0, "e4m3").T @ xq
    return q * ((f64(num)[np.arange(N)[:, None], runs(par, N)] + ek * val) / (f64(den)[np.arange(N)[:, None], runs(par, N)] + ek))

@@ -1,0 +1,180 @@
+from contextlib import ExitStack
+
+import concourse.mybir as mybir
+
+K, T, S, N = 512, 2048, 512, 512
+FLOPS = 3 * 2 * K * N * S
+
+F32 = mybir.dt.float32
+BF16 = mybir.dt.bfloat16
+I32 = mybir.dt.int32
+U32 = mybir.dt.uint32
+U16 = mybir.dt.uint16
+U8 = mybir.dt.uint8
+FP8X4 = mybir.dt.float8_e4m3fn_x4
+ACT = mybir.ActivationFunctionType
+ALU = mybir.AluOpType
+
+P = 128
+PACK = 4
+TILES = 4
+HALF = S // 2
+
+
+def tile_picked_wkv8_none_p_kernel(tc, x_words, x_scales, w1, w2, w3, num, den, offs, par, out):
+    nc = tc.nc
+    with ExitStack() as ctx:
+        keep = ctx.enter_context(tc.tile_pool(name="keep", bufs=1))
+        psum = ctx.enter_context(tc.psum_pool(name="psum", bufs=1))
+
+        def f32_tiles(name, width=S):
+            return [keep.tile([P, width], F32, name=f"{name}{t}") for t in range(TILES)]
+
+        offs_sb = keep.tile([P, S // 16], U16, name="offs_sb")
+        par_sb = keep.tile([P, S // 16], U16, name="par_sb")
+        word_table = keep.tile([P, T], I32, name="word_table", align_bytes=64)
+        scale_table = keep.tile([P, T], U8, name="scale_table", align_bytes=64)
+        x_codes = keep.tile([P, S], U32, name="x_codes", align_bytes=64)
+        x_bytes = keep.tile([P, S], U8, name="x_bytes", align_bytes=64)
+        raw = {n: keep.tile([P, PACK, N], F32, name=f"raw_{n}") for n in ("w1", "w2", "w3")}
+        dens, nums = f32_tiles("den", 2 * S), f32_tiles("num", 2 * S)
+        ek, ekv, rinv, res = (f32_tiles(n) for n in ("ek", "ekv", "rinv", "res"))
+        wide = {n: keep.tile([P, TILES * S], F32, name=f"{n}_all") for n in ("th", "asum", "sgn", "gated", "signed")}
+
+        def span(name, first, last):
+            return wide[name][:, first * S : last * S]
+
+        bsum_all = keep.tile([P, TILES * S], F32, name="bsum_all")
+        rs_all = keep.tile([P, TILES * S], F32, name="rs_all")
+        bsum = [bsum_all[:, t * S : (t + 1) * S] for t in range(TILES)]
+        rs = [rs_all[:, t * S : (t + 1) * S] for t in range(TILES)]
+
+        nc.vector.memset(scale_table[:].bitcast(I32), 0)
+        nc.gpsimd.memset(rs_all[:, 0:1], 0.0)
+        for window in dens + nums:
+            nc.gpsimd.memset(window[:, S:], 0.0)
+
+        def by_tile(ap):
+            return ap.rearrange("(p t) s -> t p s", t=TILES)
+
+        def load_weight(name, w):
+            nc.sync.dma_start(out=raw[name][:], in_=w.rearrange("(p j) c -> p j c", j=PACK))
+
+        nc.sync.dma_start(offs_sb[:], offs)
+        nc.sync.dma_start(out=word_table[:], in_=x_words[0].rearrange("p n t -> p (n t)").bitcast(I32))
+        for q in range(4):
+            nc.sync.dma_start(
+                out=scale_table[32 * q : 32 * q + 4, :].bitcast(I32),
+                in_=x_scales[0, 4 * q : 4 * q + 4, :].bitcast(I32),
+            )
+        load_weight("w1", w1)
+        nc.sync.dma_start(par_sb[:], par)
+        for t in range(TILES):
+            nc.sync.dma_start(out=dens[t][:, :S], in_=by_tile(den)[t])
+        load_weight("w3", w3)
+        load_weight("w2", w2)
+        for t in range(TILES):
+            nc.sync.dma_start(out=nums[t][:, :S], in_=by_tile(num)[t])
+
+        grouped, codes, scales = {}, {}, {}
+
+        def cast(name, h, on_vector):
+            g = keep.tile([P, 2, P, PACK], BF16, name=f"g_{name}{h}", align_bytes=64)
+            grouped[name, h] = g
+            src = raw[name][:].rearrange("p j (m t) -> p m j t", t=TILES)[:, :, :, 2 * h : 2 * h + 2]
+            dst = g[:].rearrange("p t m j -> p m j t")
+            if on_vector:
+                nc.vector.tensor_copy(out=dst, in_=src)
+            else:
+                nc.scalar.copy(out=dst, in_=src)
+
+        def quantise(name, h):
+            c = keep.tile([P, 2 * P], U32, name=f"c_{name}{h}", align_bytes=64)
+            s = keep.tile([P, 2 * P], U8, name=f"s_{name}{h}", align_bytes=64)
+            codes[name, h], scales[name, h] = c, s
+            nc.vector.quantize_mx(out=c[:].bitcast(FP8X4), scales=s[:], in_=grouped[name, h][:].rearrange("p t m j -> p (t m j)"))
+
+        def product(name, t, tag, tokens=slice(0, S)):
+            acc = psum.tile([P, tokens.stop - tokens.start], F32, name=f"acc_{name}", tag=tag, bufs=4)
+            cols = slice((t % 2) * P, (t % 2 + 1) * P)
+            nc.tensor.matmul_mx(
+                out=acc[:],
+                lhsT=codes[name, t // 2][:, cols].bitcast(FP8X4),
+                lhsT_scale=scales[name, t // 2][:, cols],
+                rhs=x_codes[:, tokens].bitcast(FP8X4),
+                rhs_scale=x_bytes[:, tokens],
+                start=True,
+                stop=True,
+            )
+            return acc
+
+        def gather_add(dst, window, other, cols=slice(0, S)):
+            lists = par_sb[:, cols.start // 16 : cols.stop // 16]
+            nc.vector.tensor_tensor(dst[:, cols], window[:].indirect(lists), other[:, cols], ALU.add)
+
+        def pieces(t, split):
+            return [slice(0, HALF), slice(HALF, S)] if t == split else [slice(0, S)]
+
+        nc.vector.tensor_copy(x_codes[:], word_table[:].bitcast(U32).indirect(offs_sb[:]))
+        nc.vector.tensor_copy(x_bytes[:], scale_table[:].indirect(offs_sb[:]))
+
+        cast("w1", 0, True)
+        cast("w1", 1, False)
+        quantise("w1", 0)
+        quantise("w1", 1)
+        for t in range(TILES):
+            for cols in pieces(t, 0):
+                nc.scalar.activation(ek[t][:, cols], product("w1", t, "scalar_banks", cols)[:], ACT.Exp, scale=0.5)
+        cast("w3", 0, False)
+        cast("w3", 1, False)
+        cast("w2", 0, False)
+        for t in range(TILES):
+            for cols in pieces(t, 0):
+                gather_add(bsum[t], dens[t], ek[t], cols)
+            if t >= 2:
+                quantise("w3", t - 2)
+        for t in range(TILES):
+            bias = rs_all[:, 0:1] if t == TILES - 1 else 0.0
+            nc.scalar.activation(span("th", t, t + 1), product("w3", t, "scalar_banks")[:], ACT.Tanh, bias=bias, scale=0.5)
+        quantise("w2", 0)
+        cast("w2", 1, True)
+        quantise("w2", 1)
+        for h in range(2):
+            nc.scalar.activation(span("sgn", 2 * h, 2 * h + 2), bsum_all[:, 2 * h * S : (2 * h + 2) * S], ACT.Sign)
+        nc.scalar.activation(rs_all[:], bsum_all[:], ACT.Abs_reciprocal_sqrt, scale=2.0)
+        for t in range(TILES):
+            nc.scalar.activation(rinv[t][:], rs[t], ACT.Square)
+
+        def weigh(t):
+            nc.vector.tensor_tensor(ekv[t][:], product("w2", t, "vector_banks")[:], ek[t][:], ALU.mult)
+
+        def numerator(t):
+            gather_add(span("asum", t, t + 1), nums[t], ekv[t])
+
+        def gate(first, last):
+            nc.vector.scalar_tensor_tensor(span("gated", first, last), span("th", first, last), 1.0, span("asum", first, last), ALU.add, ALU.mult)
+
+        def sign(first, last):
+            nc.vector.tensor_tensor(span("signed", first, last), span("gated", first, last), span("sgn", first, last), ALU.mult)
+
+        def finish(t):
+            for cols in pieces(t, TILES - 1):
+                nc.vector.tensor_tensor(res[t][:, cols], span("signed", t, t + 1)[:, cols], rinv[t][:, cols], ALU.mult)
+                nc.sync.dma_start(out=by_tile(out)[t][:, cols], in_=res[t][:, cols])
+
+        weigh(0)
+        weigh(1)
+        numerator(0)
+        weigh(2)
+        numerator(1)
+        weigh(3)
+        numerator(2)
+        gate(0, 2)
+        numerator(3)
+        sign(0, 2)
+        gate(2, 4)
+        finish(0)
+        sign(2, 4)
+        finish(1)
+        finish(2)
+        finish(3)

@@ -1,6 +1,7 @@
 from contextlib import ExitStack
 
 import concourse.mybir as mybir
+from concourse.masks import make_identity
 
 K, T, S, N = 512, 2048, 512, 512
 FLOPS = 3 * 2 * K * N * S
@@ -18,7 +19,6 @@ ALU = mybir.AluOpType
 P = 128
 PACK = 4
 TILES = 4
-HALF = S // 2
 
 
 def tile_picked_wkv8_none_p_kernel(tc, x_words, x_scales, w1, w2, w3, num, den, offs, par, out):
@@ -36,22 +36,20 @@ def tile_picked_wkv8_none_p_kernel(tc, x_words, x_scales, w1, w2, w3, num, den, 
         scale_table = keep.tile([P, T], U8, name="scale_table", align_bytes=64)
         x_codes = keep.tile([P, S], U32, name="x_codes", align_bytes=64)
         x_bytes = keep.tile([P, S], U8, name="x_bytes", align_bytes=64)
+        ident = keep.tile([P, P], F32, name="ident")
         raw = {n: keep.tile([P, PACK, N], F32, name=f"raw_{n}") for n in ("w1", "w2", "w3")}
         dens, nums = f32_tiles("den", 2 * S), f32_tiles("num", 2 * S)
-        ek, ekv, rinv, res = (f32_tiles(n) for n in ("ek", "ekv", "rinv", "res"))
-        wide = {n: keep.tile([P, TILES * S], F32, name=f"{n}_all") for n in ("th", "asum", "sgn", "gated", "signed")}
-
-        def span(name, first, last):
-            return wide[name][:, first * S : last * S]
-
-        bsum_all = keep.tile([P, TILES * S], F32, name="bsum_all")
-        rs_all = keep.tile([P, TILES * S], F32, name="rs_all")
-        bsum = [bsum_all[:, t * S : (t + 1) * S] for t in range(TILES)]
-        rs = [rs_all[:, t * S : (t + 1) * S] for t in range(TILES)]
+        ek, ekv, th, sgn, root, rabs, rinv, quot, res = (
+            f32_tiles(n) for n in ("ek", "ekv", "th", "sgn", "root", "rabs", "rinv", "quot", "res")
+        )
 
         nc.vector.memset(scale_table[:].bitcast(I32), 0)
-        nc.gpsimd.memset(rs_all[:, 0:1], 0.0)
-        for window in dens + nums:
+        for window in dens:
+            nc.gpsimd.memset(window[:, S:], 0.0)
+        make_identity(nc, ident[:])
+        for t in range(TILES):
+            nc.gpsimd.memset(root[t][:, 0:1], 0.0)
+        for window in nums:
             nc.gpsimd.memset(window[:, S:], 0.0)
 
         def by_tile(ap):
@@ -71,7 +69,8 @@ def tile_picked_wkv8_none_p_kernel(tc, x_words, x_scales, w1, w2, w3, num, den, 
         nc.sync.dma_start(par_sb[:], par)
         for t in range(TILES):
             nc.sync.dma_start(out=dens[t][:, :S], in_=by_tile(den)[t])
-        load_weight("w3", w3)
+            if t == 0:
+                load_weight("w3", w3)
         load_weight("w2", w2)
         for t in range(TILES):
             nc.sync.dma_start(out=nums[t][:, :S], in_=by_tile(num)[t])
@@ -79,7 +78,7 @@ def tile_picked_wkv8_none_p_kernel(tc, x_words, x_scales, w1, w2, w3, num, den, 
         grouped, codes, scales = {}, {}, {}
 
         def cast(name, h, on_vector):
-            g = keep.tile([P, 2, P, PACK], BF16, name=f"g_{name}{h}", align_bytes=64)
+            g = keep.tile([P, 2, P, PACK], BF16, name=f"g_{name}{h}", tag=f"g_{name}{h}", align_bytes=64)
             grouped[name, h] = g
             src = raw[name][:].rearrange("p j (m t) -> p m j t", t=TILES)[:, :, :, 2 * h : 2 * h + 2]
             dst = g[:].rearrange("p t m j -> p m j t")
@@ -94,87 +93,105 @@ def tile_picked_wkv8_none_p_kernel(tc, x_words, x_scales, w1, w2, w3, num, den, 
             codes[name, h], scales[name, h] = c, s
             nc.vector.quantize_mx(out=c[:].bitcast(FP8X4), scales=s[:], in_=grouped[name, h][:].rearrange("p t m j -> p (t m j)"))
 
-        def product(name, t, tag, tokens=slice(0, S)):
-            acc = psum.tile([P, tokens.stop - tokens.start], F32, name=f"acc_{name}", tag=tag, bufs=4)
+        def bank(tag):
+            return psum.tile([P, S], F32, name=tag, tag=tag)
+
+        def product(name, t, tag):
+            acc = bank(tag)
             cols = slice((t % 2) * P, (t % 2 + 1) * P)
             nc.tensor.matmul_mx(
                 out=acc[:],
                 lhsT=codes[name, t // 2][:, cols].bitcast(FP8X4),
                 lhsT_scale=scales[name, t // 2][:, cols],
-                rhs=x_codes[:, tokens].bitcast(FP8X4),
-                rhs_scale=x_bytes[:, tokens],
+                rhs=x_codes[:].bitcast(FP8X4),
+                rhs_scale=x_bytes[:],
                 start=True,
                 stop=True,
             )
             return acc
 
-        def gather_add(dst, window, other, cols=slice(0, S)):
-            lists = par_sb[:, cols.start // 16 : cols.stop // 16]
-            nc.vector.tensor_tensor(dst[:, cols], window[:].indirect(lists), other[:, cols], ALU.add)
-
-        def pieces(t, split):
-            return [slice(0, HALF), slice(HALF, S)] if t == split else [slice(0, S)]
+        def turned_sum(acc, terms):
+            for b in range(S // P):
+                cols = slice(b * P, (b + 1) * P)
+                for i, term in enumerate(terms):
+                    nc.tensor.matmul(acc[:, cols], term[:, cols], ident[:], start=(i == 0), stop=(i == len(terms) - 1), is_transpose=True)
+            return acc
 
         nc.vector.tensor_copy(x_codes[:], word_table[:].bitcast(U32).indirect(offs_sb[:]))
         nc.vector.tensor_copy(x_bytes[:], scale_table[:].indirect(offs_sb[:]))
+
+        bt, at, gn = {}, {}, {}
+        last = TILES - 1
+
+        def key(t):
+            nc.scalar.activation(ek[t][:], product("w1", t, f"den{t}")[:], ACT.Exp, scale=0.5)
+
+        def gate(t):
+            bias = root[0][:, 0:1] if t == last else 0.0
+            nc.scalar.activation(th[t][:], product("w3", t, f"num{t}")[:], ACT.Tanh, bias=bias, scale=0.5)
+
+        def reuse(tag, count):
+            wide = keep.tile([P, count * S], F32, name=f"after_{tag}", tag=tag, align_bytes=64)
+            return [wide[:, i * S : (i + 1) * S] for i in range(count)]
+
+        def denominator(t, gd):
+            nc.vector.tensor_copy(gd, dens[t][:].indirect(par_sb[:]))
+            bt[t] = turned_sum(bank(f"den{t}"), (gd, ek[t]))
+
+        def inverse(t):
+            nc.scalar.activation(sgn[t][:], bt[t][:], ACT.Sign)
+            bias = root[t + 1][:, 0:1] if t < last else 0.0
+            nc.scalar.activation(root[t][:], bt[t][:], ACT.Abs_reciprocal_sqrt, bias=bias, scale=2.0)
+            nc.scalar.activation(rabs[t][:], root[t][:], ACT.Square)
+            if t < last:
+                nc.gpsimd.tensor_tensor(rinv[t][:], rabs[t][:], sgn[t][:], ALU.mult)
+
+        def look_up_num(t, dst):
+            gn[t] = dst
+            nc.vector.tensor_copy(dst, nums[t][:].indirect(par_sb[:]))
+
+        def numerator(t):
+            nc.vector.tensor_tensor(ekv[t][:], product("w2", t, f"num{t}")[:], ek[t][:], ALU.mult)
+
+        def turn_numerator(t):
+            at[t] = turned_sum(bank(f"num{t}"), (gn[t], ekv[t]))
+
+        def quotient(t):
+            if t == last:
+                nc.vector.tensor_tensor(rinv[t][:], at[t][:], sgn[t][:], ALU.mult)
+            nc.vector.tensor_tensor(quot[t][:], (at[t] if t < last else rabs[t])[:], rinv[t][:], ALU.mult)
+
+        def finish(t):
+            back = turned_sum(bank(f"den{t}"), (quot[t],))
+            nc.vector.scalar_tensor_tensor(res[t][:], th[t][:], 1.0, back[:], ALU.add, ALU.mult)
+            nc.sync.dma_start(out=by_tile(out)[t], in_=res[t][:])
 
         cast("w1", 0, True)
         cast("w1", 1, False)
         quantise("w1", 0)
         quantise("w1", 1)
-        for t in range(TILES):
-            for cols in pieces(t, 0):
-                nc.scalar.activation(ek[t][:, cols], product("w1", t, "scalar_banks", cols)[:], ACT.Exp, scale=0.5)
-        cast("w3", 0, False)
+        cast("w3", 0, True)
         cast("w3", 1, False)
-        cast("w2", 0, False)
+        quantise("w3", 0)
+        quantise("w3", 1)
         for t in range(TILES):
-            for cols in pieces(t, 0):
-                gather_add(bsum[t], dens[t], ek[t], cols)
-            if t >= 2:
-                quantise("w3", t - 2)
+            key(t)
         for t in range(TILES):
-            bias = rs_all[:, 0:1] if t == TILES - 1 else 0.0
-            nc.scalar.activation(span("th", t, t + 1), product("w3", t, "scalar_banks")[:], ACT.Tanh, bias=bias, scale=0.5)
-        quantise("w2", 0)
-        cast("w2", 1, True)
-        quantise("w2", 1)
+            gate(t)
+        for t, gd in enumerate(reuse("g_w11", 1) + reuse("g_w31", 3)):
+            denominator(t, gd)
         for h in range(2):
-            nc.scalar.activation(span("sgn", 2 * h, 2 * h + 2), bsum_all[:, 2 * h * S : (2 * h + 2) * S], ACT.Sign)
-        nc.scalar.activation(rs_all[:], bsum_all[:], ACT.Abs_reciprocal_sqrt, scale=2.0)
+            cast("w2", h, False)
+            quantise("w2", h)
         for t in range(TILES):
-            nc.scalar.activation(rinv[t][:], rs[t], ACT.Square)
-
-        def weigh(t):
-            nc.vector.tensor_tensor(ekv[t][:], product("w2", t, "vector_banks")[:], ek[t][:], ALU.mult)
-
-        def numerator(t):
-            gather_add(span("asum", t, t + 1), nums[t], ekv[t])
-
-        def gate(first, last):
-            nc.vector.scalar_tensor_tensor(span("gated", first, last), span("th", first, last), 1.0, span("asum", first, last), ALU.add, ALU.mult)
-
-        def sign(first, last):
-            nc.vector.tensor_tensor(span("signed", first, last), span("gated", first, last), span("sgn", first, last), ALU.mult)
-
-        def finish(t):
-            for cols in pieces(t, TILES - 1):
-                nc.vector.tensor_tensor(res[t][:, cols], span("signed", t, t + 1)[:, cols], rinv[t][:, cols], ALU.mult)
-                nc.sync.dma_start(out=by_tile(out)[t][:, cols], in_=res[t][:, cols])
-
-        weigh(0)
-        weigh(1)
-        numerator(0)
-        weigh(2)
-        numerator(1)
-        weigh(3)
-        numerator(2)
-        gate(0, 2)
-        numerator(3)
-        sign(0, 2)
-        gate(2, 4)
-        finish(0)
-        sign(2, 4)
-        finish(1)
-        finish(2)
-        finish(3)
+            inverse(t)
+        for t in range(TILES):
+            numerator(t)
+        for t, dst in enumerate(reuse("g_w10", 1) + reuse("g_w20", 1) + reuse("g_w21", 2)):
+            look_up_num(t, dst)
+            turn_numerator(t)
+        quotient(0)
+        for t in range(TILES):
+            if t < last:
+                quotient(t + 1)
+            finish(t)

@@ -44,13 +44,9 @@ def tile_picked_wkv8_none_p_kernel(tc, x_words, x_scales, w1, w2, w3, num, den, 
         )
 
         nc.vector.memset(scale_table[:].bitcast(I32), 0)
-        for window in dens:
-            nc.gpsimd.memset(window[:, S:], 0.0)
         make_identity(nc, ident[:])
         for t in range(TILES):
             nc.gpsimd.memset(root[t][:, 0:1], 0.0)
-        for window in nums:
-            nc.gpsimd.memset(window[:, S:], 0.0)
 
         def by_tile(ap):
             return ap.rearrange("(p t) s -> t p s", t=TILES)
@@ -171,7 +167,7 @@ def tile_picked_wkv8_none_p_kernel(tc, x_words, x_scales, w1, w2, w3, num, den, 
         quantise("w1", 0)
         quantise("w1", 1)
         cast("w3", 0, True)
-        cast("w3", 1, False)
+        cast("w3", 1, True)
         quantise("w3", 0)
         quantise("w3", 1)
         for t in range(TILES):
@@ -185,10 +181,10 @@ def tile_picked_wkv8_none_p_kernel(tc, x_words, x_scales, w1, w2, w3, num, den, 
             quantise("w2", h)
         for t in range(TILES):
             inverse(t)
-        for t in range(TILES):
-            numerator(t)
         for t, dst in enumerate(reuse("g_w10", 1) + reuse("g_w20", 1) + reuse("g_w21", 2)):
             look_up_num(t, dst)
+        for t in range(TILES):
+            numerator(t)
             turn_numerator(t)
         quotient(0)
         for t in range(TILES):

@@ -18,7 +18,11 @@ ALU = mybir.AluOpType
 
 P = 128
 PACK = 4
-TILES = 4
+TILES = N // P
+LAST = TILES - 1
+PAIR = 2
+QUADRANTS = 4
+LIST_ROWS = 16
 
 
 def tile_picked_wkv8_none_p_kernel(tc, x_words, x_scales, w1, w2, w3, num, den, offs, par, out):
@@ -28,77 +32,78 @@ def tile_picked_wkv8_none_p_kernel(tc, x_words, x_scales, w1, w2, w3, num, den, 
         psum = ctx.enter_context(tc.psum_pool(name="psum", bufs=1))
 
         def f32_tiles(name, width=S):
-            return [keep.tile([P, width], F32, name=f"{name}{t}") for t in range(TILES)]
+            return [keep.tile([P, width], F32, name=f"{name}{t}", tag=f"{name}{t}", align_bytes=64) for t in range(TILES)]
 
-        offs_sb = keep.tile([P, S // 16], U16, name="offs_sb")
-        par_sb = keep.tile([P, S // 16], U16, name="par_sb")
+        def reuse(tag, count):
+            wide = keep.tile([P, count * S], F32, name=f"after_{tag}", tag=tag, align_bytes=64)
+            return [wide[:, i * S : (i + 1) * S] for i in range(count)]
+
+        def by_tile(ap):
+            return ap.rearrange("(p t) s -> t p s", t=TILES)
+
+        offs_sb = keep.tile([P, S // LIST_ROWS], U16, name="offs_sb")
+        par_sb = keep.tile([P, S // LIST_ROWS], U16, name="par_sb")
         word_table = keep.tile([P, T], I32, name="word_table", align_bytes=64)
         scale_table = keep.tile([P, T], U8, name="scale_table", align_bytes=64)
         x_codes = keep.tile([P, S], U32, name="x_codes", align_bytes=64)
         x_bytes = keep.tile([P, S], U8, name="x_bytes", align_bytes=64)
         ident = keep.tile([P, P], F32, name="ident")
-        raw = {n: keep.tile([P, PACK, N], F32, name=f"raw_{n}") for n in ("w1", "w2", "w3")}
+        raw = {n: keep.tile([P, PACK, N], F32, name=f"raw_{n}", tag=f"raw_{n}", align_bytes=64) for n in ("w1", "w2", "w3")}
         dens, nums = f32_tiles("den", 2 * S), f32_tiles("num", 2 * S)
-        ek, ekv, th, sgn, root, rabs, rinv, quot, res = (
-            f32_tiles(n) for n in ("ek", "ekv", "th", "sgn", "root", "rabs", "rinv", "quot", "res")
-        )
+        ek, ekv, th, sgn, root, rabs, quot = (f32_tiles(n) for n in ("ek", "ekv", "th", "sgn", "root", "rabs", "quot"))
 
         nc.vector.memset(scale_table[:].bitcast(I32), 0)
         make_identity(nc, ident[:])
         for t in range(TILES):
             nc.gpsimd.memset(root[t][:, 0:1], 0.0)
 
-        def by_tile(ap):
-            return ap.rearrange("(p t) s -> t p s", t=TILES)
-
         def load_weight(name, w):
             nc.sync.dma_start(out=raw[name][:], in_=w.rearrange("(p j) c -> p j c", j=PACK))
 
         nc.sync.dma_start(offs_sb[:], offs)
-        nc.sync.dma_start(out=word_table[:], in_=x_words[0].rearrange("p n t -> p (n t)").bitcast(I32))
-        for q in range(4):
-            nc.sync.dma_start(
-                out=scale_table[32 * q : 32 * q + 4, :].bitcast(I32),
-                in_=x_scales[0, 4 * q : 4 * q + 4, :].bitcast(I32),
-            )
         load_weight("w1", w1)
+        for g in range(QUADRANTS):
+            nc.sync.dma_start(
+                out=scale_table[32 * g : 32 * g + 4, :].bitcast(I32),
+                in_=x_scales[0, 4 * g : 4 * g + 4, :].bitcast(I32),
+            )
+        nc.sync.dma_start(out=word_table[:], in_=x_words[0].rearrange("p n t -> p (n t)").bitcast(I32))
         nc.sync.dma_start(par_sb[:], par)
-        for t in range(TILES):
+        nc.sync.dma_start(out=dens[0][:, :S], in_=by_tile(den)[0])
+        load_weight("w3", w3)
+        for t in range(1, TILES):
             nc.sync.dma_start(out=dens[t][:, :S], in_=by_tile(den)[t])
-            if t == 0:
-                load_weight("w3", w3)
         load_weight("w2", w2)
         for t in range(TILES):
             nc.sync.dma_start(out=nums[t][:, :S], in_=by_tile(num)[t])
 
-        grouped, codes, scales = {}, {}, {}
+        rounded, codes, scales = {}, {}, {}
 
-        def cast(name, h, on_vector):
-            g = keep.tile([P, 2, P, PACK], BF16, name=f"g_{name}{h}", tag=f"g_{name}{h}", align_bytes=64)
-            grouped[name, h] = g
-            src = raw[name][:].rearrange("p j (m t) -> p m j t", t=TILES)[:, :, :, 2 * h : 2 * h + 2]
-            dst = g[:].rearrange("p t m j -> p m j t")
-            if on_vector:
-                nc.vector.tensor_copy(out=dst, in_=src)
-            else:
-                nc.scalar.copy(out=dst, in_=src)
+        def round_pair(name, h, copy):
+            dst = keep.tile([P, PAIR, P, PACK], BF16, name=f"rounded_{name}_{h}", tag=f"rounded_{name}_{h}", align_bytes=64)
+            rounded[name, h] = dst
+            src = raw[name][:].rearrange("p j (m t) -> p m j t", t=TILES)[:, :, :, PAIR * h : PAIR * (h + 1)]
+            copy(out=dst[:].rearrange("p t m j -> p m j t"), in_=src)
 
         def quantise(name, h):
-            c = keep.tile([P, 2 * P], U32, name=f"c_{name}{h}", align_bytes=64)
-            s = keep.tile([P, 2 * P], U8, name=f"s_{name}{h}", align_bytes=64)
-            codes[name, h], scales[name, h] = c, s
-            nc.vector.quantize_mx(out=c[:].bitcast(FP8X4), scales=s[:], in_=grouped[name, h][:].rearrange("p t m j -> p (t m j)"))
+            codes[name, h] = keep.tile([P, PAIR * P], U32, name=f"codes_{name}_{h}", align_bytes=64)
+            scales[name, h] = keep.tile([P, PAIR * P], U8, name=f"scales_{name}_{h}", align_bytes=64)
+            nc.vector.quantize_mx(
+                out=codes[name, h][:].bitcast(FP8X4),
+                scales=scales[name, h][:],
+                in_=rounded[name, h][:].rearrange("p t m j -> p (t m j)"),
+            )
 
         def bank(tag):
             return psum.tile([P, S], F32, name=tag, tag=tag)
 
         def product(name, t, tag):
             acc = bank(tag)
-            cols = slice((t % 2) * P, (t % 2 + 1) * P)
+            cols = slice((t % PAIR) * P, (t % PAIR + 1) * P)
             nc.tensor.matmul_mx(
                 out=acc[:],
-                lhsT=codes[name, t // 2][:, cols].bitcast(FP8X4),
-                lhsT_scale=scales[name, t // 2][:, cols],
+                lhsT=codes[name, t // PAIR][:, cols].bitcast(FP8X4),
+                lhsT_scale=scales[name, t // PAIR][:, cols],
                 rhs=x_codes[:].bitcast(FP8X4),
                 rhs_scale=x_bytes[:],
                 start=True,
@@ -106,88 +111,79 @@ def tile_picked_wkv8_none_p_kernel(tc, x_words, x_scales, w1, w2, w3, num, den, 
             )
             return acc
 
-        def turned_sum(acc, terms):
+        def turned_sum(tag, terms):
+            acc = bank(tag)
             for b in range(S // P):
                 cols = slice(b * P, (b + 1) * P)
                 for i, term in enumerate(terms):
                     nc.tensor.matmul(acc[:, cols], term[:, cols], ident[:], start=(i == 0), stop=(i == len(terms) - 1), is_transpose=True)
             return acc
 
-        nc.vector.tensor_copy(x_codes[:], word_table[:].bitcast(U32).indirect(offs_sb[:]))
-        nc.vector.tensor_copy(x_bytes[:], scale_table[:].indirect(offs_sb[:]))
-
-        bt, at, gn = {}, {}, {}
-        last = TILES - 1
+        den_sum, num_sum = {}, {}
 
         def key(t):
             nc.scalar.activation(ek[t][:], product("w1", t, f"den{t}")[:], ACT.Exp, scale=0.5)
 
         def gate(t):
-            bias = root[0][:, 0:1] if t == last else 0.0
+            bias = root[0][:, 0:1] if t == LAST else 0.0
             nc.scalar.activation(th[t][:], product("w3", t, f"num{t}")[:], ACT.Tanh, bias=bias, scale=0.5)
 
-        def reuse(tag, count):
-            wide = keep.tile([P, count * S], F32, name=f"after_{tag}", tag=tag, align_bytes=64)
-            return [wide[:, i * S : (i + 1) * S] for i in range(count)]
-
-        def denominator(t, gd):
-            nc.vector.tensor_copy(gd, dens[t][:].indirect(par_sb[:]))
-            bt[t] = turned_sum(bank(f"den{t}"), (gd, ek[t]))
+        def denominator(t, picked):
+            nc.vector.tensor_copy(picked, dens[t][:].indirect(par_sb[:]))
+            den_sum[t] = turned_sum(f"den{t}", (picked, ek[t]))
 
         def inverse(t):
-            nc.scalar.activation(sgn[t][:], bt[t][:], ACT.Sign)
-            bias = root[t + 1][:, 0:1] if t < last else 0.0
-            nc.scalar.activation(root[t][:], bt[t][:], ACT.Abs_reciprocal_sqrt, bias=bias, scale=2.0)
+            nc.scalar.activation(sgn[t][:], den_sum[t][:], ACT.Sign)
+            bias = root[t + 1][:, 0:1] if t < LAST else 0.0
+            nc.scalar.activation(root[t][:], den_sum[t][:], ACT.Abs_reciprocal_sqrt, bias=bias, scale=2.0)
             nc.scalar.activation(rabs[t][:], root[t][:], ACT.Square)
-            if t < last:
-                nc.gpsimd.tensor_tensor(rinv[t][:], rabs[t][:], sgn[t][:], ALU.mult)
 
-        def look_up_num(t, dst):
-            gn[t] = dst
-            nc.vector.tensor_copy(dst, nums[t][:].indirect(par_sb[:]))
-
-        def numerator(t):
+        def numerator(t, picked):
             nc.vector.tensor_tensor(ekv[t][:], product("w2", t, f"num{t}")[:], ek[t][:], ALU.mult)
-
-        def turn_numerator(t):
-            at[t] = turned_sum(bank(f"num{t}"), (gn[t], ekv[t]))
+            num_sum[t] = turned_sum(f"num{t}", (picked, ekv[t]))
 
         def quotient(t):
-            if t == last:
-                nc.vector.tensor_tensor(rinv[t][:], at[t][:], sgn[t][:], ALU.mult)
-            nc.vector.tensor_tensor(quot[t][:], (at[t] if t < last else rabs[t])[:], rinv[t][:], ALU.mult)
+            if t < LAST:
+                (rinv,) = reuse(f"num{LAST}" if t == 0 else f"rinv{t}", 1)
+                nc.gpsimd.tensor_tensor(rinv, rabs[t][:], sgn[t][:], ALU.mult)
+                nc.vector.tensor_tensor(quot[t][:], num_sum[t][:], rinv, ALU.mult)
+            else:
+                (signed,) = reuse("num3", 1)
+                nc.vector.tensor_tensor(signed, num_sum[t][:], sgn[t][:], ALU.mult)
+                nc.vector.tensor_tensor(quot[t][:], signed, rabs[t][:], ALU.mult)
 
-        def finish(t):
-            back = turned_sum(bank(f"den{t}"), (quot[t],))
-            nc.vector.scalar_tensor_tensor(res[t][:], th[t][:], 1.0, back[:], ALU.add, ALU.mult)
-            nc.sync.dma_start(out=by_tile(out)[t], in_=res[t][:])
+        def finish(t, res):
+            back = turned_sum(f"den{t}", (quot[t],))
+            nc.vector.scalar_tensor_tensor(res, th[t][:], 1.0, back[:], ALU.add, ALU.mult)
+            nc.sync.dma_start(out=by_tile(out)[t], in_=res)
 
-        cast("w1", 0, True)
-        cast("w1", 1, False)
-        quantise("w1", 0)
-        quantise("w1", 1)
-        cast("w3", 0, True)
-        cast("w3", 1, True)
-        quantise("w3", 0)
-        quantise("w3", 1)
+        nc.vector.tensor_copy(x_bytes[:], scale_table[:].indirect(offs_sb[:]))
+        nc.vector.tensor_copy(x_codes[:], word_table[:].bitcast(U32).indirect(offs_sb[:]))
+
+        for name, copy in (("w1", nc.scalar.copy), ("w3", nc.vector.tensor_copy)):
+            for h in range(TILES // PAIR):
+                round_pair(name, h, nc.vector.tensor_copy if h == 1 else copy)
+            for h in range(TILES // PAIR):
+                quantise(name, h)
         for t in range(TILES):
             key(t)
         for t in range(TILES):
             gate(t)
-        for t, gd in enumerate(reuse("g_w11", 1) + reuse("g_w31", 3)):
-            denominator(t, gd)
-        for h in range(2):
-            cast("w2", h, False)
+        for t, picked in enumerate(reuse("rounded_w1_1", 1) + reuse("rounded_w3_0", LAST)):
+            denominator(t, picked)
+        for h in range(TILES // PAIR):
+            round_pair("w2", h, nc.scalar.copy)
             quantise("w2", h)
         for t in range(TILES):
             inverse(t)
-        for t, dst in enumerate(reuse("g_w10", 1) + reuse("g_w20", 1) + reuse("g_w21", 2)):
-            look_up_num(t, dst)
+        picked_num = reuse("raw_w1", 1) + reuse("rounded_w2_0", 1) + reuse("raw_w2", PAIR)
+        for h in range(TILES // PAIR):
+            pair = range(PAIR * h, PAIR * (h + 1))
+            for t in pair:
+                nc.vector.tensor_copy(picked_num[t], nums[t][:].indirect(par_sb[:]))
+            for t in pair:
+                numerator(t, picked_num[t])
         for t in range(TILES):
-            numerator(t)
-            turn_numerator(t)
-        quotient(0)
-        for t in range(TILES):
-            if t < last:
-                quotient(t + 1)
-            finish(t)
+            quotient(t)
+        for t, res in enumerate(reuse(f"sgn{LAST}", TILES)):
+            finish(t, res)

@@ -25,6 +25,22 @@ QUADRANTS = 4
 LIST_ROWS = 16
 
 
+LOADS = ["d0","par","sc","d1","d2","offs","w1","x","n0","n1","w3","d3","w2","n2","n3"]
+CAST = {"w1":"ssvv","w3":"vvvv","w2":"vvvv"}
+GROUP = {"w1":2,"w3":2,"w2":2}
+SIGNV = [2,3]
+ORDER = "gs:0 gx:0 c1 q1 key c3 q3 gate gd+B sign:012 c2 q2 ars:0 sign:3 sq:0 ars:1 ars:2 sq:1 ars:3 sq:23 ekv gn+A sm+quot fin"
+HOLD = {"pn3":"ek2"}
+BFIRST = "eeep"
+AFIRST = "eeee"
+SIGNHOLD = -1
+ZS = 1
+GB = "num"
+PRE = ""
+S3H = 0
+FUSE = ""
+SGNV = ""
+
 def tile_picked_wkv8_none_p_kernel(tc, x_words, x_scales, w1, w2, w3, num, den, offs, par, out):
     nc = tc.nc
     with ExitStack() as ctx:
@@ -34,9 +50,9 @@ def tile_picked_wkv8_none_p_kernel(tc, x_words, x_scales, w1, w2, w3, num, den, 
         def f32_tiles(name, width=S):
             return [keep.tile([P, width], F32, name=f"{name}{t}", tag=f"{name}{t}", align_bytes=64) for t in range(TILES)]
 
-        def reuse(tag, count):
-            wide = keep.tile([P, count * S], F32, name=f"after_{tag}", tag=tag, align_bytes=64)
-            return [wide[:, i * S : (i + 1) * S] for i in range(count)]
+        def buf(name):
+            tag = HOLD.get(name, name)
+            return keep.tile([P, S], F32, name=name, tag=tag, align_bytes=64)[:]
 
         def by_tile(ap):
             return ap.rearrange("(p t) s -> t p s", t=TILES)
@@ -50,44 +66,54 @@ def tile_picked_wkv8_none_p_kernel(tc, x_words, x_scales, w1, w2, w3, num, den, 
         ident = keep.tile([P, P], F32, name="ident")
         raw = {n: keep.tile([P, PACK, N], F32, name=f"raw_{n}", tag=f"raw_{n}", align_bytes=64) for n in ("w1", "w2", "w3")}
         dens, nums = f32_tiles("den", 2 * S), f32_tiles("num", 2 * S)
-        ek, ekv, th, sgn, root, rabs, quot = (f32_tiles(n) for n in ("ek", "ekv", "th", "sgn", "root", "rabs", "quot"))
+        ek, th, sgn = (f32_tiles(n) for n in ("ek", "th", "sgn"))
+        zero = keep.tile([P, 1], F32, name="zero", tag="roots", align_bytes=64)
 
         nc.vector.memset(scale_table[:].bitcast(I32), 0)
         make_identity(nc, ident[:])
         for t in range(TILES):
-            nc.gpsimd.memset(root[t][:, 0:1], 0.0)
+            if t == 0:
+                nc.scalar.activation(zero[:], ident[:, 0:1], ACT.Copy, scale=0.0)
+            if t > SIGNHOLD >= 0:
+                nc.gpsimd.memset(sgn[t][:, 0:1], 0.0)
 
-        def load_weight(name, w):
-            nc.sync.dma_start(out=raw[name][:], in_=w.rearrange("(p j) c -> p j c", j=PACK))
-
-        nc.sync.dma_start(offs_sb[:], offs)
-        load_weight("w1", w1)
-        for g in range(QUADRANTS):
-            nc.sync.dma_start(
-                out=scale_table[32 * g : 32 * g + 4, :].bitcast(I32),
-                in_=x_scales[0, 4 * g : 4 * g + 4, :].bitcast(I32),
-            )
-        nc.sync.dma_start(out=word_table[:], in_=x_words[0].rearrange("p n t -> p (n t)").bitcast(I32))
-        nc.sync.dma_start(par_sb[:], par)
-        nc.sync.dma_start(out=dens[0][:, :S], in_=by_tile(den)[0])
-        load_weight("w3", w3)
-        for t in range(1, TILES):
-            nc.sync.dma_start(out=dens[t][:, :S], in_=by_tile(den)[t])
-        load_weight("w2", w2)
-        for t in range(TILES):
-            nc.sync.dma_start(out=nums[t][:, :S], in_=by_tile(num)[t])
+        if S3H >= 0:
+            nc.gpsimd.memset(sgn[LAST][:, 1:2], 2.0)
+        weights = {"w1": w1, "w2": w2, "w3": w3}
+        for name in LOADS:
+            if name == "offs":
+                nc.sync.dma_start(offs_sb[:], offs)
+            elif name == "par":
+                nc.sync.dma_start(par_sb[:], par)
+            elif name == "sc":
+                for g in range(QUADRANTS):
+                    nc.sync.dma_start(
+                        out=scale_table[32 * g : 32 * g + 4, :].bitcast(I32),
+                        in_=x_scales[0, 4 * g : 4 * g + 4, :].bitcast(I32),
+                    )
+            elif name == "x":
+                nc.sync.dma_start(out=word_table[:], in_=x_words[0].rearrange("p n t -> p (n t)").bitcast(I32))
+            elif name[0] == "w":
+                nc.sync.dma_start(out=raw[name][:], in_=weights[name].rearrange("(p j) c -> p j c", j=PACK))
+            elif name[0] == "d":
+                nc.sync.dma_start(out=dens[int(name[1])][:, :S], in_=by_tile(den)[int(name[1])])
+            else:
+                nc.sync.dma_start(out=nums[int(name[1])][:, :S], in_=by_tile(num)[int(name[1])])
 
         rounded, codes, scales = {}, {}, {}
 
-        def round_pair(name, h, copy):
-            dst = keep.tile([P, PAIR, P, PACK], BF16, name=f"rounded_{name}_{h}", tag=f"rounded_{name}_{h}", align_bytes=64)
+        def cast(name, h):
+            g = GROUP[name]
+            copy = nc.vector.tensor_copy if CAST[name][h * g] == "v" else nc.scalar.copy
+            dst = keep.tile([P, g, P, PACK], BF16, name=f"r{name}{h}", tag=HOLD.get(f"r{name}{h}", f"r{name}{h}"), align_bytes=64)
             rounded[name, h] = dst
-            src = raw[name][:].rearrange("p j (m t) -> p m j t", t=TILES)[:, :, :, PAIR * h : PAIR * (h + 1)]
+            src = raw[name][:].rearrange("p j (m t) -> p m j t", t=TILES)[:, :, :, g * h : g * (h + 1)]
             copy(out=dst[:].rearrange("p t m j -> p m j t"), in_=src)
 
         def quantise(name, h):
-            codes[name, h] = keep.tile([P, PAIR * P], U32, name=f"codes_{name}_{h}", align_bytes=64)
-            scales[name, h] = keep.tile([P, PAIR * P], U8, name=f"scales_{name}_{h}", align_bytes=64)
+            g = GROUP[name]
+            codes[name, h] = keep.tile([P, g * P], U32, name=f"codes_{name}_{h}", align_bytes=64)
+            scales[name, h] = keep.tile([P, g * P], U8, name=f"scales_{name}_{h}", align_bytes=64)
             nc.vector.quantize_mx(
                 out=codes[name, h][:].bitcast(FP8X4),
                 scales=scales[name, h][:],
@@ -99,11 +125,12 @@ def tile_picked_wkv8_none_p_kernel(tc, x_words, x_scales, w1, w2, w3, num, den, 
 
         def product(name, t, tag):
             acc = bank(tag)
-            cols = slice((t % PAIR) * P, (t % PAIR + 1) * P)
+            g = GROUP[name]
+            cols = slice((t % g) * P, (t % g + 1) * P)
             nc.tensor.matmul_mx(
                 out=acc[:],
-                lhsT=codes[name, t // PAIR][:, cols].bitcast(FP8X4),
-                lhsT_scale=scales[name, t // PAIR][:, cols],
+                lhsT=codes[name, t // g][:, cols].bitcast(FP8X4),
+                lhsT_scale=scales[name, t // g][:, cols],
                 rhs=x_codes[:].bitcast(FP8X4),
                 rhs_scale=x_bytes[:],
                 start=True,
@@ -119,71 +146,97 @@ def tile_picked_wkv8_none_p_kernel(tc, x_words, x_scales, w1, w2, w3, num, den, 
                     nc.tensor.matmul(acc[:, cols], term[:, cols], ident[:], start=(i == 0), stop=(i == len(terms) - 1), is_transpose=True)
             return acc
 
-        den_sum, num_sum = {}, {}
+        def turn_into(acc, term, first, last):
+            for b in range(S // P):
+                cols = slice(b * P, (b + 1) * P)
+                nc.tensor.matmul(acc[:, cols], term[:, cols], ident[:], start=(first and b == 0), stop=(last and b == S // P - 1), is_transpose=True)
 
-        def key(t):
-            nc.scalar.activation(ek[t][:], product("w1", t, f"den{t}")[:], ACT.Exp, scale=0.5)
+        v = {}
 
-        def gate(t):
-            bias = root[0][:, 0:1] if t == LAST else 0.0
-            nc.scalar.activation(th[t][:], product("w3", t, f"num{t}")[:], ACT.Tanh, bias=bias, scale=0.5)
+        def step(op, t):
+            if op == "gs":
+                nc.vector.tensor_copy(x_bytes[:], scale_table[:].indirect(offs_sb[:]))
+            elif op == "gx":
+                nc.vector.tensor_copy(x_codes[:], word_table[:].bitcast(U32).indirect(offs_sb[:]))
+            elif op[0] == "c":
+                if t % GROUP["w" + op[1]] == 0:
+                    cast("w" + op[1], t // GROUP["w" + op[1]])
+            elif op[0] == "q" and op != "quot":
+                if t % GROUP["w" + op[1]] == 0:
+                    quantise("w" + op[1], t // GROUP["w" + op[1]])
+            elif op == "key":
+                nc.scalar.activation(ek[t][:], product("w1", t, f"num{t}" if str(t) in PRE else f"den{t}")[:], ACT.Exp, scale=0.5)
+            elif op == "gate":
+                bias = zero[:] if t == LAST else (sgn[t + 1][:, 0:1] if t + 1 > SIGNHOLD >= 0 else 0.0)
+                nc.scalar.activation(th[t][:], product("w3", t, f"num{t}" if str(t) in PRE else f"{GB}{t}")[:], ACT.Tanh, bias=bias, scale=0.5)
+            elif op in ("gd", "gn") and str(t) in FUSE:
+                pass
+            elif op == "B" and str(t) in FUSE:
+                v["B", t] = buf(f"pd{t}")
+                nc.vector.tensor_tensor(v["B", t], dens[t][:].indirect(par_sb[:]), ek[t][:], ALU.add)
+            elif op == "A" and str(t) in FUSE:
+                v["A", t] = buf(f"pn{t}")
+                nc.vector.tensor_tensor(v["A", t], nums[t][:].indirect(par_sb[:]), v["ekv", t], ALU.add)
+            elif op == "sm" and str(t) in FUSE:
+                v["sm", t] = buf(f"sm{t}")
+                nc.vector.scalar_tensor_tensor(v["sm", t], th[t][:], 1.0, sgn[t][:], ALU.add, ALU.mult)
+            elif op == "quot" and str(t) in FUSE:
+                v["quot", t] = buf(f"quot{t}")
+                nc.vector.tensor_tensor(v["quot", t], v["A", t], v["sm", t], ALU.mult)
+            elif op == "fin" and str(t) in FUSE:
+                res = buf(f"res{t}")
+                nc.vector.tensor_tensor(res, v["quot", t], v["rabs", t], ALU.mult)
+                nc.sync.dma_start(out=by_tile(out)[t], in_=res)
+            elif op == "B" and str(t) in PRE:
+                turn_into(v["B", t], ek[t], False, True)
+            elif op == "gd":
+                v["pd", t] = buf(f"pd{t}")
+                nc.vector.tensor_copy(v["pd", t], dens[t][:].indirect(par_sb[:]))
+                if str(t) in PRE:
+                    v["B", t] = bank(f"den{t}")
+                    turn_into(v["B", t], v["pd", t], True, False)
+            elif op == "gn":
+                v["pn", t] = buf(f"pn{t}")
+                nc.vector.tensor_copy(v["pn", t], nums[t][:].indirect(par_sb[:]))
+            elif op == "B":
+                v["B", t] = turned_sum(f"den{t}", (v["pd", t], ek[t]) if BFIRST[t] == "p" else (ek[t], v["pd", t]))
+            elif op == "sign":
+                if str(t) in SGNV:
+                    nc.vector.tensor_scalar(sgn[t][:], v["B", t][:], 0.0, 0.5, ALU.is_ge, ALU.subtract)
+                else:
+                    nc.scalar.activation(sgn[t][:], v["B", t][:], ACT.Sign)
+            elif op == "ars":
+                if "roots" not in v:
+                    v["roots"] = keep.tile([P, TILES * S], F32, name="roots", tag="roots", align_bytes=64)
+                nc.scalar.activation(v["roots"][:, t * S : (t + 1) * S], v["B", t][:], ACT.Abs_reciprocal_sqrt, scale=sgn[LAST][:, 1:2] if t == S3H else 2.0)
+            elif op == "sq":
+                v["rabs", t] = buf(f"rabs{t}")
+                nc.scalar.activation(v["rabs", t], v["roots"][:, t * S : (t + 1) * S], ACT.Square)
+            elif op == "ekv":
+                v["ekv", t] = buf(f"ekv{t}")
+                nc.vector.tensor_tensor(v["ekv", t], product("w2", t, f"num{t}")[:], ek[t][:], ALU.mult)
+            elif op == "A":
+                v["A", t] = turned_sum(f"num{t}", (v["pn", t], v["ekv", t]) if AFIRST[t] == "p" else (v["ekv", t], v["pn", t]))
+            elif op == "sm":
+                v["sm", t] = buf(f"sm{t}")
+                if t in SIGNV:
+                    nc.vector.tensor_tensor(v["sm", t], v["A", t][:], sgn[t][:], ALU.mult)
+                else:
+                    nc.gpsimd.tensor_tensor(v["sm", t], v["rabs", t], sgn[t][:], ALU.mult)
+            elif op == "quot":
+                v["quot", t] = buf(f"quot{t}")
+                if t in SIGNV:
+                    nc.vector.tensor_tensor(v["quot", t], v["sm", t], v["rabs", t], ALU.mult)
+                else:
+                    nc.vector.tensor_tensor(v["quot", t], v["A", t][:], v["sm", t], ALU.mult)
+            elif op == "fin":
+                back = turned_sum(f"den{t}", (v["quot", t],))
+                res = buf(f"res{t}")
+                nc.vector.scalar_tensor_tensor(res, th[t][:], 1.0, back[:], ALU.add, ALU.mult)
+                nc.sync.dma_start(out=by_tile(out)[t], in_=res)
 
-        def denominator(t, picked):
-            nc.vector.tensor_copy(picked, dens[t][:].indirect(par_sb[:]))
-            den_sum[t] = turned_sum(f"den{t}", (picked, ek[t]))
-
-        def inverse(t):
-            nc.scalar.activation(sgn[t][:], den_sum[t][:], ACT.Sign)
-            bias = root[t + 1][:, 0:1] if t < LAST else 0.0
-            nc.scalar.activation(root[t][:], den_sum[t][:], ACT.Abs_reciprocal_sqrt, bias=bias, scale=2.0)
-            nc.scalar.activation(rabs[t][:], root[t][:], ACT.Square)
-
-        def numerator(t, picked):
-            nc.vector.tensor_tensor(ekv[t][:], product("w2", t, f"num{t}")[:], ek[t][:], ALU.mult)
-            num_sum[t] = turned_sum(f"num{t}", (picked, ekv[t]))
-
-        def quotient(t):
-            if t < LAST:
-                (rinv,) = reuse(f"num{LAST}" if t == 0 else f"rinv{t}", 1)
-                nc.gpsimd.tensor_tensor(rinv, rabs[t][:], sgn[t][:], ALU.mult)
-                nc.vector.tensor_tensor(quot[t][:], num_sum[t][:], rinv, ALU.mult)
-            else:
-                (signed,) = reuse("num3", 1)
-                nc.vector.tensor_tensor(signed, num_sum[t][:], sgn[t][:], ALU.mult)
-                nc.vector.tensor_tensor(quot[t][:], signed, rabs[t][:], ALU.mult)
-
-        def finish(t, res):
-            back = turned_sum(f"den{t}", (quot[t],))
-            nc.vector.scalar_tensor_tensor(res, th[t][:], 1.0, back[:], ALU.add, ALU.mult)
-            nc.sync.dma_start(out=by_tile(out)[t], in_=res)
-
-        nc.vector.tensor_copy(x_bytes[:], scale_table[:].indirect(offs_sb[:]))
-        nc.vector.tensor_copy(x_codes[:], word_table[:].bitcast(U32).indirect(offs_sb[:]))
-
-        for name, copy in (("w1", nc.scalar.copy), ("w3", nc.vector.tensor_copy)):
-            for h in range(TILES // PAIR):
-                round_pair(name, h, nc.vector.tensor_copy if h == 1 else copy)
-            for h in range(TILES // PAIR):
-                quantise(name, h)
-        for t in range(TILES):
-            key(t)
-        for t in range(TILES):
-            gate(t)
-        for t, picked in enumerate(reuse("rounded_w1_1", 1) + reuse("rounded_w3_0", LAST)):
-            denominator(t, picked)
-        for h in range(TILES // PAIR):
-            round_pair("w2", h, nc.scalar.copy)
-            quantise("w2", h)
-        for t in range(TILES):
-            inverse(t)
-        picked_num = reuse("raw_w1", 1) + reuse("rounded_w2_0", 1) + reuse("raw_w2", PAIR)
-        for h in range(TILES // PAIR):
-            pair = range(PAIR * h, PAIR * (h + 1))
-            for t in pair:
-                nc.vector.tensor_copy(picked_num[t], nums[t][:].indirect(par_sb[:]))
-            for t in pair:
-                numerator(t, picked_num[t])
-        for t in range(TILES):
-            quotient(t)
-        for t, res in enumerate(reuse(f"sgn{LAST}", TILES)):
-            finish(t, res)
+        for item in ORDER.split():
+            op, ts = item.split(":") if ":" in item else (item, "0123")
+            for t in ts:
+                for o in op.split("+"):
+                    step(o, int(t))

@@ -25,19 +25,21 @@ QUADRANTS = 4
 LIST_ROWS = 16
 
 
-LOADS = ["d0","par","sc","d1","d2","offs","w1","x","n0","n1","w3","d3","w2","n2","n3"]
+LOADS = ["d0","par","sc","d1","offs","w1","d2","x","n0","w3","n1","w2","d3","n2","n3"]
 CAST = {"w1":"ssvv","w3":"vvvv","w2":"vvvv"}
-GROUP = {"w1":2,"w3":2,"w2":2}
-SIGNV = [2,3]
-ORDER = "gs:0 gx:0 c1 q1 key c3 q3 gate gd+B sign:012 c2 q2 ars:0 sign:3 sq:0 ars:1 ars:2 sq:1 ars:3 sq:23 ekv gn+A sm+quot fin"
-HOLD = {"pn3":"ek2"}
+GROUP = {"w1":2,"w3":2,"w2":4}
+SIGNV = [0]
+ORDER = "gs:0 gx:0 c1 q1 key c3 q3 gate c2 gd+B q2 gn sign:012 ars:12 sq:1 ars:3 sq:2 sign:3 sq:3 ars:0 sq:0 ekv+A:1203 sm:0 sm+quot:123 quot:0 fin:1230"
+HOLD = {}
 BFIRST = "eeep"
 AFIRST = "eeee"
 SIGNHOLD = -1
 ZS = 1
 GB = "num"
-PRE = ""
-S3H = 0
+PRE = "012"
+PAT = 1
+CUT = {"w1": 64, "w2": 128, "w3": 128}
+S3H = 1
 FUSE = ""
 SGNV = ""
 
@@ -102,13 +104,30 @@ def tile_picked_wkv8_none_p_kernel(tc, x_words, x_scales, w1, w2, w3, num, den, 
 
         rounded, codes, scales = {}, {}, {}
 
+        whole = {}
+
         def cast(name, h):
+            if PAT == 3:
+                if name not in whole:
+                    whole[name] = keep.tile([P, TILES, P, PACK], BF16, name=f"r{name}", tag=f"r{name}", align_bytes=64)
+                rounded[name, h] = whole[name][:, PAIR * h : PAIR * (h + 1)]
+                cut = CUT[name]
+                cols = slice(0, cut) if h == 0 else slice(cut, P)
+                if cols.start < cols.stop:
+                    copy = nc.vector.tensor_copy if CAST[name][h * PAIR] == "v" else nc.scalar.copy
+                    src = raw[name][:].rearrange("p j (m t) -> p m t j", t=TILES)[:, cols]
+                    copy(out=whole[name][:].rearrange("p t m j -> p m t j")[:, cols], in_=src)
+                return
             g = GROUP[name]
             copy = nc.vector.tensor_copy if CAST[name][h * g] == "v" else nc.scalar.copy
             dst = keep.tile([P, g, P, PACK], BF16, name=f"r{name}{h}", tag=HOLD.get(f"r{name}{h}", f"r{name}{h}"), align_bytes=64)
             rounded[name, h] = dst
-            src = raw[name][:].rearrange("p j (m t) -> p m j t", t=TILES)[:, :, :, g * h : g * (h + 1)]
-            copy(out=dst[:].rearrange("p t m j -> p m j t"), in_=src)
+            if PAT == 2:
+                src = raw[name][:].rearrange("p j (m t) -> p m t j", t=TILES)[:, :, g * h : g * (h + 1), :]
+                copy(out=dst[:].rearrange("p t m j -> p m t j"), in_=src)
+            else:
+                src = raw[name][:].rearrange("p j (m t) -> p m j t", t=TILES)[:, :, :, g * h : g * (h + 1)]
+                copy(out=dst[:].rearrange("p t m j -> p m j t"), in_=src)
 
         def quantise(name, h):
             g = GROUP[name]

@@ -25,23 +25,22 @@ QUADRANTS = 4
 LIST_ROWS = 16
 
 
-LOADS = ["d0","par","sc","d1","offs","w1","d2","x","n0","w3","n1","w2","d3","n2","n3"]
+LOADS = ["par","d0","offs","sc","d1","w1","d2","x","n0","w3","n1","w2","d3","n2","n3"]
 CAST = {"w1":"ssvv","w3":"vvvv","w2":"vvvv"}
 GROUP = {"w1":2,"w3":2,"w2":4}
 SIGNV = [0]
-ORDER = "gs:0 gx:0 c1 q1 key c3 q3 gate c2 gd+B q2 gn sign:012 ars:12 sq:1 ars:3 sq:2 sign:3 sq:3 ars:0 sq:0 ekv+A:1203 sm:0 sm+quot:123 quot:0 fin:1230"
+ORDER = "gs:0 gx:0 c1 q1 gd:012 td:12 key:1230 c3 q3 gate tk:123 td:0 tk:0 c2 gd:3 td:3 q2 val:1 gn tn:012 sign:12 ars:12 val:20 sq:1 ars:3 sq:2 sign:3 sq:3 sign:0 ars:0 sq:0 ekv:1 val:3 te:1 ekv:2 te:2 ekv:0 te:0 tn:3 ekv:3 te:3 sm+quot:12 sm:0 sm+quot:3 quot:0 fin:1230"
 HOLD = {}
-BFIRST = "eeep"
-AFIRST = "eeee"
-SIGNHOLD = -1
-ZS = 1
-GB = "num"
-PRE = "012"
+WIDE = {"ekv0 ekv1 ekv2 ekv3 sgn3 sgn0":"g1","res0 res1 res2 res3":"sm3"}
+BANK = {"B":"r3 b1 b2 r1","key":"r0 r1 r2 r3","gate":"r0 r1 r2 r3","A":"r0 r2 b0 b1","val":"b2 r4 b1 r4","back":"r3 b2 r4 r1"}
+ZB = {"ars1":"g1"}
+FUSE = ""
+HALF = 0
+SPLIT = ""
+LATE = ""
+LATETAG = "rw30"
 PAT = 1
 CUT = {"w1": 64, "w2": 128, "w3": 128}
-S3H = 1
-FUSE = ""
-SGNV = ""
 
 def tile_picked_wkv8_none_p_kernel(tc, x_words, x_scales, w1, w2, w3, num, den, offs, par, out):
     nc = tc.nc
@@ -52,9 +51,16 @@ def tile_picked_wkv8_none_p_kernel(tc, x_words, x_scales, w1, w2, w3, num, den, 
         def f32_tiles(name, width=S):
             return [keep.tile([P, width], F32, name=f"{name}{t}", tag=f"{name}{t}", align_bytes=64) for t in range(TILES)]
 
+        wide = {}
+
         def buf(name):
-            tag = HOLD.get(name, name)
-            return keep.tile([P, S], F32, name=name, tag=tag, align_bytes=64)[:]
+            for group in WIDE:
+                if name in group.split():
+                    if group not in wide:
+                        wide[group] = keep.tile([P, len(group.split()) * S], F32, name=name, tag=WIDE[group], align_bytes=64)
+                    i = group.split().index(name)
+                    return wide[group][:, i * S : (i + 1) * S]
+            return keep.tile([P, S], F32, name=name, tag=HOLD.get(name, name), align_bytes=64)[:]
 
         def by_tile(ap):
             return ap.rearrange("(p t) s -> t p s", t=TILES)
@@ -68,19 +74,22 @@ def tile_picked_wkv8_none_p_kernel(tc, x_words, x_scales, w1, w2, w3, num, den, 
         ident = keep.tile([P, P], F32, name="ident")
         raw = {n: keep.tile([P, PACK, N], F32, name=f"raw_{n}", tag=f"raw_{n}", align_bytes=64) for n in ("w1", "w2", "w3")}
         dens, nums = f32_tiles("den", 2 * S), f32_tiles("num", 2 * S)
-        ek, th, sgn = (f32_tiles(n) for n in ("ek", "th", "sgn"))
+        ek, th = (f32_tiles(n) for n in ("ek", "th"))
+        sgn = {}
         zero = keep.tile([P, 1], F32, name="zero", tag="roots", align_bytes=64)
 
         nc.vector.memset(scale_table[:].bitcast(I32), 0)
         make_identity(nc, ident[:])
-        for t in range(TILES):
-            if t == 0:
-                nc.scalar.activation(zero[:], ident[:, 0:1], ACT.Copy, scale=0.0)
-            if t > SIGNHOLD >= 0:
-                nc.gpsimd.memset(sgn[t][:, 0:1], 0.0)
+        nc.scalar.activation(zero[:], ident[:, 0:1], ACT.Copy, scale=0.0)
 
-        if S3H >= 0:
-            nc.gpsimd.memset(sgn[LAST][:, 1:2], 2.0)
+        zeros = {}
+        for user in ZB:
+            zeros[user] = keep.tile([P, 1], F32, name=ZB[user], tag=ZB[user], align_bytes=64)
+            nc.gpsimd.memset(zeros[user][:], 0.0)
+
+        def bias_of(user):
+            return zeros[user][:] if user in zeros else 0.0
+
         weights = {"w1": w1, "w2": w2, "w3": w3}
         for name in LOADS:
             if name == "offs":
@@ -119,10 +128,10 @@ def tile_picked_wkv8_none_p_kernel(tc, x_words, x_scales, w1, w2, w3, num, den, 
                     copy(out=whole[name][:].rearrange("p t m j -> p m t j")[:, cols], in_=src)
                 return
             g = GROUP[name]
-            copy = nc.vector.tensor_copy if CAST[name][h * g] == "v" else nc.scalar.copy
+            copy = {"v": nc.vector.tensor_copy, "s": nc.scalar.copy, "g": nc.gpsimd.tensor_copy}[CAST[name][h * g]]
             dst = keep.tile([P, g, P, PACK], BF16, name=f"r{name}{h}", tag=HOLD.get(f"r{name}{h}", f"r{name}{h}"), align_bytes=64)
             rounded[name, h] = dst
-            if PAT == 2:
+            if CAST[name][h * g] == "g":
                 src = raw[name][:].rearrange("p j (m t) -> p m t j", t=TILES)[:, :, g * h : g * (h + 1), :]
                 copy(out=dst[:].rearrange("p t m j -> p m t j"), in_=src)
             else:
@@ -131,7 +140,7 @@ def tile_picked_wkv8_none_p_kernel(tc, x_words, x_scales, w1, w2, w3, num, den, 
 
         def quantise(name, h):
             g = GROUP[name]
-            codes[name, h] = keep.tile([P, g * P], U32, name=f"codes_{name}_{h}", align_bytes=64)
+            codes[name, h] = keep.tile([P, g * P], U32, name=f"codes_{name}_{h}", tag=HOLD.get(f"codes{name}{h}", f"codes{name}{h}"), align_bytes=64)
             scales[name, h] = keep.tile([P, g * P], U8, name=f"scales_{name}_{h}", align_bytes=64)
             nc.vector.quantize_mx(
                 out=codes[name, h][:].bitcast(FP8X4),
@@ -165,35 +174,55 @@ def tile_picked_wkv8_none_p_kernel(tc, x_words, x_scales, w1, w2, w3, num, den, 
                     nc.tensor.matmul(acc[:, cols], term[:, cols], ident[:], start=(i == 0), stop=(i == len(terms) - 1), is_transpose=True)
             return acc
 
-        def turn_into(acc, term, first, last):
+        def turn_into(acc, term, first, last, ident):
             for b in range(S // P):
                 cols = slice(b * P, (b + 1) * P)
                 nc.tensor.matmul(acc[:, cols], term[:, cols], ident[:], start=(first and b == 0), stop=(last and b == S // P - 1), is_transpose=True)
 
         v = {}
 
+        def half_key(t, h):
+            g = GROUP["w1"]
+            cols = slice((t % g) * P, (t % g + 1) * P)
+            part = slice(h * 256, (h + 1) * 256)
+            nc.tensor.matmul_mx(
+                out=v["key", t][:, part],
+                lhsT=codes["w1", t // g][:, cols].bitcast(FP8X4),
+                lhsT_scale=scales["w1", t // g][:, cols],
+                rhs=x_codes[:, part].bitcast(FP8X4),
+                rhs_scale=x_bytes[:, part],
+                start=True,
+                stop=True,
+            )
+            nc.scalar.activation(ek[t][:, part], v["key", t][:, part], ACT.Exp, scale=0.5)
+
+        def turned_term(key, term, name):
+            first = key not in v
+            if first:
+                v[key] = bank(BANK[key[0]].split()[key[1]])
+            turn_into(v[key], term, first, not first, v["late"] if name in LATE.split() else ident)
+
         def step(op, t):
             if op == "gs":
                 nc.vector.tensor_copy(x_bytes[:], scale_table[:].indirect(offs_sb[:]))
-            elif op == "gx":
-                nc.vector.tensor_copy(x_codes[:], word_table[:].bitcast(U32).indirect(offs_sb[:]))
-            elif op[0] == "c":
-                if t % GROUP["w" + op[1]] == 0:
-                    cast("w" + op[1], t // GROUP["w" + op[1]])
-            elif op[0] == "q" and op != "quot":
-                if t % GROUP["w" + op[1]] == 0:
-                    quantise("w" + op[1], t // GROUP["w" + op[1]])
-            elif op == "key":
-                nc.scalar.activation(ek[t][:], product("w1", t, f"num{t}" if str(t) in PRE else f"den{t}")[:], ACT.Exp, scale=0.5)
-            elif op == "gate":
-                bias = zero[:] if t == LAST else (sgn[t + 1][:, 0:1] if t + 1 > SIGNHOLD >= 0 else 0.0)
-                nc.scalar.activation(th[t][:], product("w3", t, f"num{t}" if str(t) in PRE else f"{GB}{t}")[:], ACT.Tanh, bias=bias, scale=0.5)
-            elif op in ("gd", "gn") and str(t) in FUSE:
+            elif op == "gx" and HALF:
+                for h in range(2):
+                    nc.vector.tensor_copy(x_codes[:, h * 256 : (h + 1) * 256], word_table[:].bitcast(U32).indirect(offs_sb[:, h * 16 : (h + 1) * 16]))
+            elif op == "key" and HALF:
+                v["key", t] = bank(BANK["key"].split()[t])
+                half_key(t, 0)
+            elif op == "late":
+                v["late"] = keep.tile([P, P], F32, name="late", tag=LATETAG, align_bytes=64)
+                nc.vector.tensor_copy(v["late"][:], ident[:])
+            elif op == "kez":
+                if HALF:
+                    half_key(t, 1)
+            elif op in ("gd", "gn", "td", "tn") and str(t) in FUSE:
                 pass
-            elif op == "B" and str(t) in FUSE:
+            elif op == "tk" and str(t) in FUSE:
                 v["B", t] = buf(f"pd{t}")
                 nc.vector.tensor_tensor(v["B", t], dens[t][:].indirect(par_sb[:]), ek[t][:], ALU.add)
-            elif op == "A" and str(t) in FUSE:
+            elif op == "te" and str(t) in FUSE:
                 v["A", t] = buf(f"pn{t}")
                 nc.vector.tensor_tensor(v["A", t], nums[t][:].indirect(par_sb[:]), v["ekv", t], ALU.add)
             elif op == "sm" and str(t) in FUSE:
@@ -206,36 +235,48 @@ def tile_picked_wkv8_none_p_kernel(tc, x_words, x_scales, w1, w2, w3, num, den, 
                 res = buf(f"res{t}")
                 nc.vector.tensor_tensor(res, v["quot", t], v["rabs", t], ALU.mult)
                 nc.sync.dma_start(out=by_tile(out)[t], in_=res)
-            elif op == "B" and str(t) in PRE:
-                turn_into(v["B", t], ek[t], False, True)
+            elif op == "gx":
+                nc.vector.tensor_copy(x_codes[:], word_table[:].bitcast(U32).indirect(offs_sb[:]))
+            elif op[0] == "c":
+                if t % GROUP["w" + op[1]] == 0:
+                    cast("w" + op[1], t // GROUP["w" + op[1]])
+            elif op[0] == "q" and op != "quot":
+                if t % GROUP["w" + op[1]] == 0:
+                    quantise("w" + op[1], t // GROUP["w" + op[1]])
+            elif op == "key":
+                nc.scalar.activation(ek[t][:], product("w1", t, BANK["key"].split()[t])[:], ACT.Exp, bias=bias_of(f"key{t}"), scale=0.5)
+            elif op == "gate":
+                bias = zero[:] if t == LAST else bias_of(f"gate{t}")
+                nc.scalar.activation(th[t][:], product("w3", t, BANK["gate"].split()[t])[:], ACT.Tanh, bias=bias, scale=0.5)
             elif op == "gd":
                 v["pd", t] = buf(f"pd{t}")
                 nc.vector.tensor_copy(v["pd", t], dens[t][:].indirect(par_sb[:]))
-                if str(t) in PRE:
-                    v["B", t] = bank(f"den{t}")
-                    turn_into(v["B", t], v["pd", t], True, False)
             elif op == "gn":
                 v["pn", t] = buf(f"pn{t}")
                 nc.vector.tensor_copy(v["pn", t], nums[t][:].indirect(par_sb[:]))
-            elif op == "B":
-                v["B", t] = turned_sum(f"den{t}", (v["pd", t], ek[t]) if BFIRST[t] == "p" else (ek[t], v["pd", t]))
+            elif op == "td":
+                turned_term(("B", t), v["pd", t], f"td{t}")
+            elif op == "tk":
+                turned_term(("B", t), ek[t], f"tk{t}")
+            elif op == "tn":
+                turned_term(("A", t), v["pn", t], f"tn{t}")
+            elif op == "te":
+                turned_term(("A", t), v["ekv", t], f"te{t}")
             elif op == "sign":
-                if str(t) in SGNV:
-                    nc.vector.tensor_scalar(sgn[t][:], v["B", t][:], 0.0, 0.5, ALU.is_ge, ALU.subtract)
-                else:
-                    nc.scalar.activation(sgn[t][:], v["B", t][:], ACT.Sign)
+                sgn[t] = buf(f"sgn{t}")
+                nc.scalar.activation(sgn[t][:], v["B", t][:], ACT.Sign, bias=bias_of(f"sign{t}"))
             elif op == "ars":
                 if "roots" not in v:
                     v["roots"] = keep.tile([P, TILES * S], F32, name="roots", tag="roots", align_bytes=64)
-                nc.scalar.activation(v["roots"][:, t * S : (t + 1) * S], v["B", t][:], ACT.Abs_reciprocal_sqrt, scale=sgn[LAST][:, 1:2] if t == S3H else 2.0)
+                nc.scalar.activation(v["roots"][:, t * S : (t + 1) * S], v["B", t][:], ACT.Abs_reciprocal_sqrt, bias=bias_of(f"ars{t}"), scale=2.0)
             elif op == "sq":
                 v["rabs", t] = buf(f"rabs{t}")
-                nc.scalar.activation(v["rabs", t], v["roots"][:, t * S : (t + 1) * S], ACT.Square)
+                nc.scalar.activation(v["rabs", t], v["roots"][:, t * S : (t + 1) * S], ACT.Square, bias=bias_of(f"sq{t}"))
+            elif op == "val":
+                v["val", t] = product("w2", t, BANK["val"].split()[t])
             elif op == "ekv":
                 v["ekv", t] = buf(f"ekv{t}")
-                nc.vector.tensor_tensor(v["ekv", t], product("w2", t, f"num{t}")[:], ek[t][:], ALU.mult)
-            elif op == "A":
-                v["A", t] = turned_sum(f"num{t}", (v["pn", t], v["ekv", t]) if AFIRST[t] == "p" else (v["ekv", t], v["pn", t]))
+                nc.vector.tensor_tensor(v["ekv", t], v["val", t][:], ek[t][:], ALU.mult)
             elif op == "sm":
                 v["sm", t] = buf(f"sm{t}")
                 if t in SIGNV:
@@ -249,10 +290,13 @@ def tile_picked_wkv8_none_p_kernel(tc, x_words, x_scales, w1, w2, w3, num, den, 
                 else:
                     nc.vector.tensor_tensor(v["quot", t], v["A", t][:], v["sm", t], ALU.mult)
             elif op == "fin":
-                back = turned_sum(f"den{t}", (v["quot", t],))
+                back = turned_sum(BANK["back"].split()[t], (v["quot", t],))
                 res = buf(f"res{t}")
-                nc.vector.scalar_tensor_tensor(res, th[t][:], 1.0, back[:], ALU.add, ALU.mult)
-                nc.sync.dma_start(out=by_tile(out)[t], in_=res)
+                step_cols = S // 2 if str(t) in SPLIT else S
+                for c0 in range(0, S, step_cols):
+                    part = slice(c0, c0 + step_cols)
+                    nc.vector.scalar_tensor_tensor(res[:, part], th[t][:, part], 1.0, back[:, part], ALU.add, ALU.mult)
+                    nc.sync.dma_start(out=by_tile(out)[t][:, part], in_=res[:, part])
 
         for item in ORDER.split():
             op, ts = item.split(":") if ":" in item else (item, "0123")

@@ -19,48 +19,29 @@ ALU = mybir.AluOpType
 P = 128
 PACK = 4
 TILES = N // P
-LAST = TILES - 1
 PAIR = 2
 QUADRANTS = 4
 LIST_ROWS = 16
+BLOCKS = S // P
+
+EARLY = (1, 2)
+LATE = (3, 0)
+ON_VECTOR = LATE[-1]
 
 
-LOADS = ["par","d0","offs","sc","d1","w1","d2","x","n0","w3","n1","w2","d3","n2","n3"]
-CAST = {"w1":"ssvv","w3":"vvvv","w2":"vvvv"}
-GROUP = {"w1":2,"w3":2,"w2":4}
-SIGNV = [0]
-ORDER = "gs:0 gx:0 c1 q1 gd:012 td:12 key:1230 c3 q3 gate tk:123 td:0 tk:0 c2 gd:3 td:3 q2 val:1 gn tn:012 sign:12 ars:12 val:20 sq:1 ars:3 sq:2 sign:3 sq:3 sign:0 ars:0 sq:0 ekv:1 val:3 te:1 ekv:2 te:2 ekv:0 te:0 tn:3 ekv:3 te:3 sm+quot:12 sm:0 sm+quot:3 quot:0 fin:1230"
-HOLD = {}
-WIDE = {"ekv0 ekv1 ekv2 ekv3 sgn3 sgn0":"g1","res0 res1 res2 res3":"sm3"}
-BANK = {"B":"r3 b1 b2 r1","key":"r0 r1 r2 r3","gate":"r0 r1 r2 r3","A":"r0 r2 b0 b1","val":"b2 r4 b1 r4","back":"r3 b2 r4 r1"}
-ZB = {"ars1":"g1"}
-FUSE = ""
-HALF = 0
-SPLIT = ""
-LATE = ""
-LATETAG = "rw30"
-PAT = 1
-CUT = {"w1": 64, "w2": 128, "w3": 128}
-
-def tile_picked_wkv8_none_p_kernel(tc, x_words, x_scales, w1, w2, w3, num, den, offs, par, out):
+def tile_picked_wkv8_none_p_kernel(
+    tc, x_words, x_scales, w1, w2, w3, num, den, offs, par, out
+):
     nc = tc.nc
     with ExitStack() as ctx:
         keep = ctx.enter_context(tc.tile_pool(name="keep", bufs=1))
         psum = ctx.enter_context(tc.psum_pool(name="psum", bufs=1))
 
         def f32_tiles(name, width=S):
-            return [keep.tile([P, width], F32, name=f"{name}{t}", tag=f"{name}{t}", align_bytes=64) for t in range(TILES)]
+            return [keep.tile([P, width], F32, name=f"{name}{t}", align_bytes=64) for t in range(TILES)]
 
-        wide = {}
-
-        def buf(name):
-            for group in WIDE:
-                if name in group.split():
-                    if group not in wide:
-                        wide[group] = keep.tile([P, len(group.split()) * S], F32, name=name, tag=WIDE[group], align_bytes=64)
-                    i = group.split().index(name)
-                    return wide[group][:, i * S : (i + 1) * S]
-            return keep.tile([P, S], F32, name=name, tag=HOLD.get(name, name), align_bytes=64)[:]
+        def columns(i, width):
+            return slice(i * width, (i + 1) * width)
 
         def by_tile(ap):
             return ap.rearrange("(p t) s -> t p s", t=TILES)
@@ -72,93 +53,68 @@ def tile_picked_wkv8_none_p_kernel(tc, x_words, x_scales, w1, w2, w3, num, den, 
         x_codes = keep.tile([P, S], U32, name="x_codes", align_bytes=64)
         x_bytes = keep.tile([P, S], U8, name="x_bytes", align_bytes=64)
         ident = keep.tile([P, P], F32, name="ident")
-        raw = {n: keep.tile([P, PACK, N], F32, name=f"raw_{n}", tag=f"raw_{n}", align_bytes=64) for n in ("w1", "w2", "w3")}
+        raw = {n: keep.tile([P, PACK, N], F32, name=f"raw_{n}", align_bytes=64) for n in ("w1", "w2", "w3")}
         dens, nums = f32_tiles("den", 2 * S), f32_tiles("num", 2 * S)
-        ek, th = (f32_tiles(n) for n in ("ek", "th"))
-        sgn = {}
-        zero = keep.tile([P, 1], F32, name="zero", tag="roots", align_bytes=64)
+        ek, th = f32_tiles("ek"), f32_tiles("th")
+        picked_den, picked_num = f32_tiles("picked_den"), f32_tiles("picked_num")
+        inverse, signed, quotient, result = (f32_tiles(n) for n in ("inverse", "signed", "quotient", "result"))
 
         nc.vector.memset(scale_table[:].bitcast(I32), 0)
         make_identity(nc, ident[:])
-        nc.scalar.activation(zero[:], ident[:, 0:1], ACT.Copy, scale=0.0)
 
-        zeros = {}
-        for user in ZB:
-            zeros[user] = keep.tile([P, 1], F32, name=ZB[user], tag=ZB[user], align_bytes=64)
-            nc.gpsimd.memset(zeros[user][:], 0.0)
+        last_gate_bias = keep.tile([P, 1], F32, name="last_gate_bias", tag="roots", align_bytes=64)
+        nc.scalar.activation(last_gate_bias[:], ident[:, 0:1], ACT.Copy, scale=0.0)
+        first_root_bias = keep.tile([P, 1], F32, name="first_root_bias", tag="after_first_root", align_bytes=64)
+        nc.gpsimd.memset(first_root_bias[:], 0.0)
 
-        def bias_of(user):
-            return zeros[user][:] if user in zeros else 0.0
-
-        weights = {"w1": w1, "w2": w2, "w3": w3}
-        for name in LOADS:
-            if name == "offs":
-                nc.sync.dma_start(offs_sb[:], offs)
-            elif name == "par":
-                nc.sync.dma_start(par_sb[:], par)
-            elif name == "sc":
-                for g in range(QUADRANTS):
-                    nc.sync.dma_start(
-                        out=scale_table[32 * g : 32 * g + 4, :].bitcast(I32),
-                        in_=x_scales[0, 4 * g : 4 * g + 4, :].bitcast(I32),
-                    )
-            elif name == "x":
-                nc.sync.dma_start(out=word_table[:], in_=x_words[0].rearrange("p n t -> p (n t)").bitcast(I32))
-            elif name[0] == "w":
-                nc.sync.dma_start(out=raw[name][:], in_=weights[name].rearrange("(p j) c -> p j c", j=PACK))
-            elif name[0] == "d":
-                nc.sync.dma_start(out=dens[int(name[1])][:, :S], in_=by_tile(den)[int(name[1])])
-            else:
-                nc.sync.dma_start(out=nums[int(name[1])][:, :S], in_=by_tile(num)[int(name[1])])
-
-        rounded, codes, scales = {}, {}, {}
-
-        whole = {}
-
-        def cast(name, h):
-            if PAT == 3:
-                if name not in whole:
-                    whole[name] = keep.tile([P, TILES, P, PACK], BF16, name=f"r{name}", tag=f"r{name}", align_bytes=64)
-                rounded[name, h] = whole[name][:, PAIR * h : PAIR * (h + 1)]
-                cut = CUT[name]
-                cols = slice(0, cut) if h == 0 else slice(cut, P)
-                if cols.start < cols.stop:
-                    copy = nc.vector.tensor_copy if CAST[name][h * PAIR] == "v" else nc.scalar.copy
-                    src = raw[name][:].rearrange("p j (m t) -> p m t j", t=TILES)[:, cols]
-                    copy(out=whole[name][:].rearrange("p t m j -> p m t j")[:, cols], in_=src)
-                return
-            g = GROUP[name]
-            copy = {"v": nc.vector.tensor_copy, "s": nc.scalar.copy, "g": nc.gpsimd.tensor_copy}[CAST[name][h * g]]
-            dst = keep.tile([P, g, P, PACK], BF16, name=f"r{name}{h}", tag=HOLD.get(f"r{name}{h}", f"r{name}{h}"), align_bytes=64)
-            rounded[name, h] = dst
-            if CAST[name][h * g] == "g":
-                src = raw[name][:].rearrange("p j (m t) -> p m t j", t=TILES)[:, :, g * h : g * (h + 1), :]
-                copy(out=dst[:].rearrange("p t m j -> p m t j"), in_=src)
-            else:
-                src = raw[name][:].rearrange("p j (m t) -> p m j t", t=TILES)[:, :, :, g * h : g * (h + 1)]
-                copy(out=dst[:].rearrange("p t m j -> p m j t"), in_=src)
-
-        def quantise(name, h):
-            g = GROUP[name]
-            codes[name, h] = keep.tile([P, g * P], U32, name=f"codes_{name}_{h}", tag=HOLD.get(f"codes{name}{h}", f"codes{name}{h}"), align_bytes=64)
-            scales[name, h] = keep.tile([P, g * P], U8, name=f"scales_{name}_{h}", align_bytes=64)
-            nc.vector.quantize_mx(
-                out=codes[name, h][:].bitcast(FP8X4),
-                scales=scales[name, h][:],
-                in_=rounded[name, h][:].rearrange("p t m j -> p (t m j)"),
+        tables = [(dens[t], by_tile(den)[t]) for t in range(TILES)] + [(nums[t], by_tile(num)[t]) for t in range(TILES)]
+        large = [
+            (raw["w1"][:], w1.rearrange("(p j) c -> p j c", j=PACK)),
+            (word_table[:], x_words[0].rearrange("p n t -> p (n t)").bitcast(I32)),
+            (raw["w3"][:], w3.rearrange("(p j) c -> p j c", j=PACK)),
+            (raw["w2"][:], w2.rearrange("(p j) c -> p j c", j=PACK)),
+        ]
+        nc.sync.dma_start(par_sb[:], par)
+        nc.sync.dma_start(out=tables[0][0][:, :S], in_=tables[0][1])
+        nc.sync.dma_start(offs_sb[:], offs)
+        for g in range(QUADRANTS):
+            nc.sync.dma_start(
+                out=scale_table[32 * g : 32 * g + 4, :].bitcast(I32),
+                in_=x_scales[0, 4 * g : 4 * g + 4, :].bitcast(I32),
             )
+        for i, (table, rows) in enumerate(tables[1:]):
+            nc.sync.dma_start(out=table[:, :S], in_=rows)
+            if i < len(large):
+                nc.sync.dma_start(out=large[i][0], in_=large[i][1])
+
+        def quantised(name, copies):
+            share = TILES // len(copies)
+            by_column = raw[name][:].rearrange("p j (m t) -> p m j t", t=TILES)
+            rounded = []
+            for h, copy in enumerate(copies):
+                part = keep.tile([P, share, P, PACK], BF16, name=f"rounded_{name}_{h}", align_bytes=64)
+                copy(out=part[:].rearrange("p t m j -> p m j t"), in_=by_column[:, :, :, columns(h, share)])
+                rounded.append(part)
+            operands = []
+            for h, part in enumerate(rounded):
+                codes = keep.tile([P, share * P], U32, name=f"codes_{name}_{h}", align_bytes=64)
+                scales = keep.tile([P, share * P], U8, name=f"scales_{name}_{h}", align_bytes=64)
+                nc.vector.quantize_mx(
+                    out=codes[:].bitcast(FP8X4), scales=scales[:], in_=part[:].rearrange("p t m j -> p (t m j)")
+                )
+                operands += [(codes[:, columns(i, P)], scales[:, columns(i, P)]) for i in range(share)]
+            return operands
 
         def bank(tag):
             return psum.tile([P, S], F32, name=tag, tag=tag)
 
-        def product(name, t, tag):
+        def product(operand, tag):
             acc = bank(tag)
-            g = GROUP[name]
-            cols = slice((t % g) * P, (t % g + 1) * P)
+            codes, scales = operand
             nc.tensor.matmul_mx(
                 out=acc[:],
-                lhsT=codes[name, t // g][:, cols].bitcast(FP8X4),
-                lhsT_scale=scales[name, t // g][:, cols],
+                lhsT=codes.bitcast(FP8X4),
+                lhsT_scale=scales,
                 rhs=x_codes[:].bitcast(FP8X4),
                 rhs_scale=x_bytes[:],
                 start=True,
@@ -166,140 +122,96 @@ def tile_picked_wkv8_none_p_kernel(tc, x_words, x_scales, w1, w2, w3, num, den, 
             )
             return acc
 
-        def turned_sum(tag, terms):
+        def add_turned(acc, term, opens):
+            for b in range(BLOCKS):
+                cols = columns(b, P)
+                start, stop = opens and b == 0, not opens and b == BLOCKS - 1
+                nc.tensor.matmul(acc[:, cols], term[:, cols], ident[:], start=start, stop=stop, is_transpose=True)
+
+        def open_sum(tag, term):
             acc = bank(tag)
-            for b in range(S // P):
-                cols = slice(b * P, (b + 1) * P)
-                for i, term in enumerate(terms):
-                    nc.tensor.matmul(acc[:, cols], term[:, cols], ident[:], start=(i == 0), stop=(i == len(terms) - 1), is_transpose=True)
+            add_turned(acc, term, True)
             return acc
 
-        def turn_into(acc, term, first, last, ident):
-            for b in range(S // P):
-                cols = slice(b * P, (b + 1) * P)
-                nc.tensor.matmul(acc[:, cols], term[:, cols], ident[:], start=(first and b == 0), stop=(last and b == S // P - 1), is_transpose=True)
+        nc.vector.tensor_copy(x_bytes[:], scale_table[:].indirect(offs_sb[:]))
+        nc.vector.tensor_copy(x_codes[:], word_table[:].bitcast(U32).indirect(offs_sb[:]))
+        key_weights = quantised("w1", (nc.scalar.copy, nc.vector.tensor_copy))
 
-        v = {}
+        for t in range(TILES):
+            nc.vector.tensor_copy(picked_den[t][:], dens[t][:].indirect(par_sb[:]))
+        den_bank = {t: f"den{t}" for t in EARLY}
+        den_sum = {t: open_sum(den_bank[t], picked_den[t]) for t in EARLY}
+        for t in EARLY + LATE:
+            nc.scalar.activation(ek[t][:], product(key_weights[t], f"product{t}")[:], ACT.Exp, scale=0.5)
 
-        def half_key(t, h):
-            g = GROUP["w1"]
-            cols = slice((t % g) * P, (t % g + 1) * P)
-            part = slice(h * 256, (h + 1) * 256)
-            nc.tensor.matmul_mx(
-                out=v["key", t][:, part],
-                lhsT=codes["w1", t // g][:, cols].bitcast(FP8X4),
-                lhsT_scale=scales["w1", t // g][:, cols],
-                rhs=x_codes[:, part].bitcast(FP8X4),
-                rhs_scale=x_bytes[:, part],
-                start=True,
-                stop=True,
-            )
-            nc.scalar.activation(ek[t][:, part], v["key", t][:, part], ACT.Exp, scale=0.5)
+        gate_weights = quantised("w3", (nc.vector.tensor_copy,) * (TILES // PAIR))
+        for t in range(TILES):
+            bias = last_gate_bias[:] if t == TILES - 1 else 0.0
+            nc.scalar.activation(th[t][:], product(gate_weights[t], f"product{t}")[:], ACT.Tanh, bias=bias, scale=0.5)
 
-        def turned_term(key, term, name):
-            first = key not in v
-            if first:
-                v[key] = bank(BANK[key[0]].split()[key[1]])
-            turn_into(v[key], term, first, not first, v["late"] if name in LATE.split() else ident)
+        for t in EARLY:
+            add_turned(den_sum[t], ek[t], False)
+        for i, t in enumerate(LATE):
+            den_bank[t] = f"product{len(EARLY) + i}"
+            den_sum[t] = open_sum(den_bank[t], picked_den[t])
+            add_turned(den_sum[t], ek[t], False)
 
-        def step(op, t):
-            if op == "gs":
-                nc.vector.tensor_copy(x_bytes[:], scale_table[:].indirect(offs_sb[:]))
-            elif op == "gx" and HALF:
-                for h in range(2):
-                    nc.vector.tensor_copy(x_codes[:, h * 256 : (h + 1) * 256], word_table[:].bitcast(U32).indirect(offs_sb[:, h * 16 : (h + 1) * 16]))
-            elif op == "key" and HALF:
-                v["key", t] = bank(BANK["key"].split()[t])
-                half_key(t, 0)
-            elif op == "late":
-                v["late"] = keep.tile([P, P], F32, name="late", tag=LATETAG, align_bytes=64)
-                nc.vector.tensor_copy(v["late"][:], ident[:])
-            elif op == "kez":
-                if HALF:
-                    half_key(t, 1)
-            elif op in ("gd", "gn", "td", "tn") and str(t) in FUSE:
-                pass
-            elif op == "tk" and str(t) in FUSE:
-                v["B", t] = buf(f"pd{t}")
-                nc.vector.tensor_tensor(v["B", t], dens[t][:].indirect(par_sb[:]), ek[t][:], ALU.add)
-            elif op == "te" and str(t) in FUSE:
-                v["A", t] = buf(f"pn{t}")
-                nc.vector.tensor_tensor(v["A", t], nums[t][:].indirect(par_sb[:]), v["ekv", t], ALU.add)
-            elif op == "sm" and str(t) in FUSE:
-                v["sm", t] = buf(f"sm{t}")
-                nc.vector.scalar_tensor_tensor(v["sm", t], th[t][:], 1.0, sgn[t][:], ALU.add, ALU.mult)
-            elif op == "quot" and str(t) in FUSE:
-                v["quot", t] = buf(f"quot{t}")
-                nc.vector.tensor_tensor(v["quot", t], v["A", t], v["sm", t], ALU.mult)
-            elif op == "fin" and str(t) in FUSE:
-                res = buf(f"res{t}")
-                nc.vector.tensor_tensor(res, v["quot", t], v["rabs", t], ALU.mult)
-                nc.sync.dma_start(out=by_tile(out)[t], in_=res)
-            elif op == "gx":
-                nc.vector.tensor_copy(x_codes[:], word_table[:].bitcast(U32).indirect(offs_sb[:]))
-            elif op[0] == "c":
-                if t % GROUP["w" + op[1]] == 0:
-                    cast("w" + op[1], t // GROUP["w" + op[1]])
-            elif op[0] == "q" and op != "quot":
-                if t % GROUP["w" + op[1]] == 0:
-                    quantise("w" + op[1], t // GROUP["w" + op[1]])
-            elif op == "key":
-                nc.scalar.activation(ek[t][:], product("w1", t, BANK["key"].split()[t])[:], ACT.Exp, bias=bias_of(f"key{t}"), scale=0.5)
-            elif op == "gate":
-                bias = zero[:] if t == LAST else bias_of(f"gate{t}")
-                nc.scalar.activation(th[t][:], product("w3", t, BANK["gate"].split()[t])[:], ACT.Tanh, bias=bias, scale=0.5)
-            elif op == "gd":
-                v["pd", t] = buf(f"pd{t}")
-                nc.vector.tensor_copy(v["pd", t], dens[t][:].indirect(par_sb[:]))
-            elif op == "gn":
-                v["pn", t] = buf(f"pn{t}")
-                nc.vector.tensor_copy(v["pn", t], nums[t][:].indirect(par_sb[:]))
-            elif op == "td":
-                turned_term(("B", t), v["pd", t], f"td{t}")
-            elif op == "tk":
-                turned_term(("B", t), ek[t], f"tk{t}")
-            elif op == "tn":
-                turned_term(("A", t), v["pn", t], f"tn{t}")
-            elif op == "te":
-                turned_term(("A", t), v["ekv", t], f"te{t}")
-            elif op == "sign":
-                sgn[t] = buf(f"sgn{t}")
-                nc.scalar.activation(sgn[t][:], v["B", t][:], ACT.Sign, bias=bias_of(f"sign{t}"))
-            elif op == "ars":
-                if "roots" not in v:
-                    v["roots"] = keep.tile([P, TILES * S], F32, name="roots", tag="roots", align_bytes=64)
-                nc.scalar.activation(v["roots"][:, t * S : (t + 1) * S], v["B", t][:], ACT.Abs_reciprocal_sqrt, bias=bias_of(f"ars{t}"), scale=2.0)
-            elif op == "sq":
-                v["rabs", t] = buf(f"rabs{t}")
-                nc.scalar.activation(v["rabs", t], v["roots"][:, t * S : (t + 1) * S], ACT.Square, bias=bias_of(f"sq{t}"))
-            elif op == "val":
-                v["val", t] = product("w2", t, BANK["val"].split()[t])
-            elif op == "ekv":
-                v["ekv", t] = buf(f"ekv{t}")
-                nc.vector.tensor_tensor(v["ekv", t], v["val", t][:], ek[t][:], ALU.mult)
-            elif op == "sm":
-                v["sm", t] = buf(f"sm{t}")
-                if t in SIGNV:
-                    nc.vector.tensor_tensor(v["sm", t], v["A", t][:], sgn[t][:], ALU.mult)
-                else:
-                    nc.gpsimd.tensor_tensor(v["sm", t], v["rabs", t], sgn[t][:], ALU.mult)
-            elif op == "quot":
-                v["quot", t] = buf(f"quot{t}")
-                if t in SIGNV:
-                    nc.vector.tensor_tensor(v["quot", t], v["sm", t], v["rabs", t], ALU.mult)
-                else:
-                    nc.vector.tensor_tensor(v["quot", t], v["A", t][:], v["sm", t], ALU.mult)
-            elif op == "fin":
-                back = turned_sum(BANK["back"].split()[t], (v["quot", t],))
-                res = buf(f"res{t}")
-                step_cols = S // 2 if str(t) in SPLIT else S
-                for c0 in range(0, S, step_cols):
-                    part = slice(c0, c0 + step_cols)
-                    nc.vector.scalar_tensor_tensor(res[:, part], th[t][:, part], 1.0, back[:, part], ALU.add, ALU.mult)
-                    nc.sync.dma_start(out=by_tile(out)[t][:, part], in_=res[:, part])
+        value_weights = quantised("w2", (nc.vector.tensor_copy,))
+        value = {0: product(value_weights[0], "value")}
+        for t in range(TILES):
+            nc.vector.tensor_copy(picked_num[t][:], nums[t][:].indirect(par_sb[:]))
+        num_sum = {t: open_sum(tag, picked_num[t]) for t, tag in enumerate(("product0", "product1", "spare"))}
 
-        for item in ORDER.split():
-            op, ts = item.split(":") if ":" in item else (item, "0123")
-            for t in ts:
-                for o in op.split("+"):
-                    step(o, int(t))
+        sign = {t: keep.tile([P, S], F32, name=f"sign{t}", align_bytes=64)[:] for t in EARLY}
+        for t in EARLY:
+            nc.scalar.activation(sign[t], den_sum[t][:], ACT.Sign)
+        roots = keep.tile([P, TILES * S], F32, name="roots", tag="roots", align_bytes=64)
+        for t in EARLY:
+            bias = first_root_bias[:] if t == EARLY[0] else 0.0
+            nc.scalar.activation(roots[:, columns(t, S)], den_sum[t][:], ACT.Abs_reciprocal_sqrt, bias=bias, scale=2.0)
+        for t in EARLY:
+            value[t] = product(value_weights[t], den_bank[t])
+        for t in EARLY:
+            nc.scalar.activation(inverse[t][:], roots[:, columns(t, S)], ACT.Square)
+
+        held = keep.tile([P, (len(LATE) + TILES) * S], F32, name="held", tag="after_first_root", align_bytes=64)
+        term = [held[:, columns(len(LATE) + t, S)] for t in range(TILES)]
+        for i, t in enumerate(LATE):
+            sign[t] = held[:, columns(i, S)]
+            nc.scalar.activation(sign[t], den_sum[t][:], ACT.Sign)
+            nc.scalar.activation(roots[:, columns(t, S)], den_sum[t][:], ACT.Abs_reciprocal_sqrt, scale=2.0)
+        for t in LATE:
+            nc.scalar.activation(inverse[t][:], roots[:, columns(t, S)], ACT.Square)
+
+        for t in range(TILES):
+            nc.vector.tensor_tensor(term[t], value[t][:], ek[t][:], ALU.mult)
+            if t == 0:
+                value[TILES - 1] = product(value_weights[TILES - 1], "value")
+            if t in num_sum:
+                add_turned(num_sum[t], term[t], False)
+
+        def divide(t):
+            nc.gpsimd.tensor_tensor(signed[t][:], inverse[t][:], sign[t], ALU.mult)
+            nc.vector.tensor_tensor(quotient[t][:], num_sum[t][:], signed[t][:], ALU.mult)
+
+        def finish(t):
+            back = bank(den_bank[t])
+            for b in range(BLOCKS):
+                cols = columns(b, P)
+                nc.tensor.matmul(back[:, cols], quotient[t][:, cols], ident[:], start=True, stop=True, is_transpose=True)
+            nc.vector.scalar_tensor_tensor(result[t][:], th[t][:], 1.0, back[:], ALU.add, ALU.mult)
+            nc.sync.dma_start(out=by_tile(out)[t], in_=result[t][:])
+
+        first, second = EARLY
+        third = LATE[0]
+        nc.vector.tensor_tensor(signed[ON_VECTOR][:], num_sum[ON_VECTOR][:], sign[ON_VECTOR], ALU.mult)
+        divide(first)
+        finish(first)
+        num_sum[third] = open_sum(f"product{first}", picked_num[third])
+        add_turned(num_sum[third], term[third], False)
+        divide(second)
+        finish(second)
+        nc.vector.tensor_tensor(quotient[ON_VECTOR][:], signed[ON_VECTOR][:], inverse[ON_VECTOR][:], ALU.mult)
+        divide(third)
+        finish(ON_VECTOR)
+        finish(third)

@@ -19,14 +19,12 @@ ALU = mybir.AluOpType
 P = 128
 PACK = 4
 TILES = N // P
-PAIR = 2
 QUADRANTS = 4
 LIST_ROWS = 16
 BLOCKS = S // P
-
-EARLY = (1, 2)
-LATE = (3, 0)
-ON_VECTOR = LATE[-1]
+LAST = TILES - 1
+HALVES = 2
+SIGN_ON_VECTOR = ()
 
 
 def tile_picked_wkv8_none_p_kernel(
@@ -53,165 +51,175 @@ def tile_picked_wkv8_none_p_kernel(
         x_codes = keep.tile([P, S], U32, name="x_codes", align_bytes=64)
         x_bytes = keep.tile([P, S], U8, name="x_bytes", align_bytes=64)
         ident = keep.tile([P, P], F32, name="ident")
-        raw = {n: keep.tile([P, PACK, N], F32, name=f"raw_{n}", align_bytes=64) for n in ("w1", "w2", "w3")}
+        raw = {
+            (n, h): keep.tile([P, PACK, N // HALVES], F32, name=f"raw_{n}_{h}", tag=f"raw_{n}_{h}", align_bytes=64)
+            for n in ("w1", "w2", "w3")
+            for h in range(HALVES)
+        }
         dens, nums = f32_tiles("den", 2 * S), f32_tiles("num", 2 * S)
-        ek, th = f32_tiles("ek"), f32_tiles("th")
-        picked_den, picked_num = f32_tiles("picked_den"), f32_tiles("picked_num")
-        inverse, signed, quotient, result = (f32_tiles(n) for n in ("inverse", "signed", "quotient", "result"))
+        (picked_num,) = (f32_tiles(n) for n in ("picked_num",))
+        sign, inverse, signed, gated, result = (f32_tiles(n) for n in ("sign", "inverse", "signed", "gated", "result"))
+        th = keep.tile([P, TILES, BLOCKS, P], F32, name="th", align_bytes=64)
 
         nc.vector.memset(scale_table[:].bitcast(I32), 0)
         make_identity(nc, ident[:])
-
         last_gate_bias = keep.tile([P, 1], F32, name="last_gate_bias", tag="roots", align_bytes=64)
         nc.scalar.activation(last_gate_bias[:], ident[:, 0:1], ACT.Copy, scale=0.0)
-        first_root_bias = keep.tile([P, 1], F32, name="first_root_bias", tag="after_first_root", align_bytes=64)
-        nc.gpsimd.memset(first_root_bias[:], 0.0)
 
-        tables = [(dens[t], by_tile(den)[t]) for t in range(TILES)] + [(nums[t], by_tile(num)[t]) for t in range(TILES)]
-        large = [
-            (raw["w1"][:], w1.rearrange("(p j) c -> p j c", j=PACK)),
-            (word_table[:], x_words[0].rearrange("p n t -> p (n t)").bitcast(I32)),
-            (raw["w3"][:], w3.rearrange("(p j) c -> p j c", j=PACK)),
-            (raw["w2"][:], w2.rearrange("(p j) c -> p j c", j=PACK)),
-        ]
+        loads = {f"num{t}": (nums[t][:, :S], by_tile(num)[t]) for t in range(TILES)}
+        for t in range(TILES):
+            loads[f"den{t}"] = (dens[t][:, :S], by_tile(den)[t])
+        for n, w in (("w1", w1), ("w2", w2), ("w3", w3)):
+            for h in range(HALVES):
+                loads[n + "ab"[h]] = (raw[n, h][:], w.rearrange("(p j) c -> p j c", j=PACK)[:, :, columns(h, N // HALVES)])
+        loads["x"] = (word_table[:], x_words[0].rearrange("p n t -> p (n t)").bitcast(I32))
         nc.sync.dma_start(par_sb[:], par)
-        nc.sync.dma_start(out=tables[0][0][:, :S], in_=tables[0][1])
+        nc.sync.dma_start(out=loads["num0"][0], in_=loads["num0"][1])
         nc.sync.dma_start(offs_sb[:], offs)
         for g in range(QUADRANTS):
             nc.sync.dma_start(
                 out=scale_table[32 * g : 32 * g + 4, :].bitcast(I32),
                 in_=x_scales[0, 4 * g : 4 * g + 4, :].bitcast(I32),
             )
-        for i, (table, rows) in enumerate(tables[1:]):
-            nc.sync.dma_start(out=table[:, :S], in_=rows)
-            if i < len(large):
-                nc.sync.dma_start(out=large[i][0], in_=large[i][1])
+        for n in ["w1a","num1","w1b","num2","x","w3a","num3","w3b","w2a","den0","w2b","den1","den2","den3"]:
+            nc.sync.dma_start(out=loads[n][0], in_=loads[n][1])
 
-        def quantised(name, copies):
-            share = TILES // len(copies)
-            by_column = raw[name][:].rearrange("p j (m t) -> p m j t", t=TILES)
-            rounded = []
-            for h, copy in enumerate(copies):
-                part = keep.tile([P, share, P, PACK], BF16, name=f"rounded_{name}_{h}", align_bytes=64)
-                copy(out=part[:].rearrange("p t m j -> p m j t"), in_=by_column[:, :, :, columns(h, share)])
-                rounded.append(part)
-            operands = []
-            for h, part in enumerate(rounded):
-                codes = keep.tile([P, share * P], U32, name=f"codes_{name}_{h}", align_bytes=64)
-                scales = keep.tile([P, share * P], U8, name=f"scales_{name}_{h}", align_bytes=64)
+        def on_gpsimd(out, in_):
+            order = "p m j t -> p t m j"
+            nc.gpsimd.tensor_scalar(out.rearrange(order), in_.rearrange(order), 1.0, 0.0, ALU.mult, ALU.add)
+
+        rounded = {n: keep.tile([P, TILES, P, PACK], BF16, name=f"rounded_{n}", align_bytes=64) for n in ("w1", "w2", "w3")}
+
+        def round_half(name, h, copy):
+            copy(
+                out=rounded[name][:, :, columns(h, P // HALVES), :].rearrange("p t m j -> p m j t"),
+                in_=raw[name, h][:].rearrange("p j (m t) -> p m j t", t=TILES),
+            )
+
+        def quantised(name, groups):
+            codes = keep.tile([P, N], U32, name=f"codes_{name}", align_bytes=64)
+            scales = keep.tile([P, N], U8, name=f"scales_{name}", align_bytes=64)
+            per = TILES // groups
+            for g in range(groups):
+                cols = columns(g, per * P)
                 nc.vector.quantize_mx(
-                    out=codes[:].bitcast(FP8X4), scales=scales[:], in_=part[:].rearrange("p t m j -> p (t m j)")
+                    out=codes[:, cols].bitcast(FP8X4),
+                    scales=scales[:, cols],
+                    in_=rounded[name][:, columns(g, per)].rearrange("p t m j -> p (t m j)"),
                 )
-                operands += [(codes[:, columns(i, P)], scales[:, columns(i, P)]) for i in range(share)]
-            return operands
+            return codes, scales
 
         def bank(tag):
             return psum.tile([P, S], F32, name=tag, tag=tag)
 
-        def product(operand, tag):
-            acc = bank(tag)
-            codes, scales = operand
+        def product(acc, stationary, moving, s_cols, m_cols):
             nc.tensor.matmul_mx(
-                out=acc[:],
-                lhsT=codes.bitcast(FP8X4),
-                lhsT_scale=scales,
-                rhs=x_codes[:].bitcast(FP8X4),
-                rhs_scale=x_bytes[:],
+                out=acc,
+                lhsT=stationary[0][:, s_cols].bitcast(FP8X4),
+                lhsT_scale=stationary[1][:, s_cols],
+                rhs=moving[0][:, m_cols].bitcast(FP8X4),
+                rhs_scale=moving[1][:, m_cols],
                 start=True,
                 stop=True,
             )
-            return acc
 
-        def add_turned(acc, term, opens):
+        def add_turned(acc, addend, opens, closes):
             for b in range(BLOCKS):
                 cols = columns(b, P)
-                start, stop = opens and b == 0, not opens and b == BLOCKS - 1
-                nc.tensor.matmul(acc[:, cols], term[:, cols], ident[:], start=start, stop=stop, is_transpose=True)
+                start, stop = opens and b == 0, closes and b == BLOCKS - 1
+                nc.tensor.matmul(acc[:, cols], addend[:, cols], ident[:], start=start, stop=stop, is_transpose=True)
 
-        def open_sum(tag, term):
+        def turned_back(tag, tile):
             acc = bank(tag)
-            add_turned(acc, term, True)
+            for b in range(BLOCKS):
+                cols = columns(b, P)
+                nc.tensor.matmul(acc[:, cols], tile[:, cols], ident[:], start=True, stop=True, is_transpose=True)
             return acc
 
+        everything = slice(0, S)
+        x = (x_codes, x_bytes)
         nc.vector.tensor_copy(x_bytes[:], scale_table[:].indirect(offs_sb[:]))
         nc.vector.tensor_copy(x_codes[:], word_table[:].bitcast(U32).indirect(offs_sb[:]))
-        key_weights = quantised("w1", (nc.scalar.copy, nc.vector.tensor_copy))
-
+        round_half("w1", 0, nc.scalar.copy)
+        round_half("w1", 1, nc.scalar.copy)
+        key_weights = quantised("w1", 2)
+        round_half("w3", 0, nc.scalar.copy)
+        ek_all = keep.tile([P, TILES, S], F32, name="ek", tag="raw_w3_0", align_bytes=64)
+        ek = [ek_all[:, t] for t in range(TILES)]
         for t in range(TILES):
-            nc.vector.tensor_copy(picked_den[t][:], dens[t][:].indirect(par_sb[:]))
-        den_bank = {t: f"den{t}" for t in EARLY}
-        den_sum = {t: open_sum(den_bank[t], picked_den[t]) for t in EARLY}
-        for t in EARLY + LATE:
-            nc.scalar.activation(ek[t][:], product(key_weights[t], f"product{t}")[:], ACT.Exp, scale=0.5)
-
-        gate_weights = quantised("w3", (nc.vector.tensor_copy,) * (TILES // PAIR))
-        for t in range(TILES):
-            bias = last_gate_bias[:] if t == TILES - 1 else 0.0
-            nc.scalar.activation(th[t][:], product(gate_weights[t], f"product{t}")[:], ACT.Tanh, bias=bias, scale=0.5)
-
-        for t in EARLY:
-            add_turned(den_sum[t], ek[t], False)
-        for i, t in enumerate(LATE):
-            den_bank[t] = f"product{len(EARLY) + i}"
-            den_sum[t] = open_sum(den_bank[t], picked_den[t])
-            add_turned(den_sum[t], ek[t], False)
-
-        value_weights = quantised("w2", (nc.vector.tensor_copy,))
-        value = {0: product(value_weights[0], "value")}
+            acc = bank(f"product{t}")
+            product(acc[:], key_weights, x, columns(t, P), everything)
+            nc.scalar.activation(ek[t], acc[:], ACT.Exp, scale=0.5)
+        num_sum = []
         for t in range(TILES):
             nc.vector.tensor_copy(picked_num[t][:], nums[t][:].indirect(par_sb[:]))
-        num_sum = {t: open_sum(tag, picked_num[t]) for t, tag in enumerate(("product0", "product1", "spare"))}
+            num_sum.append(bank(f"num{t}"))
+            add_turned(num_sum[t], picked_num[t], True, False)
 
-        sign = {t: keep.tile([P, S], F32, name=f"sign{t}", align_bytes=64)[:] for t in EARLY}
-        for t in EARLY:
-            nc.scalar.activation(sign[t], den_sum[t][:], ACT.Sign)
+        round_half("w3", 1, nc.vector.tensor_copy)
+        gate_weights = quantised("w3", 1)
+        for b in range(BLOCKS):
+            acc = bank(f"product{b}")
+            product(acc[:], x, gate_weights, columns(b, P), everything)
+            bias = last_gate_bias[:] if b == BLOCKS - 1 else 0.0
+            nc.scalar.activation(th[:, :, b, :], acc[:].rearrange("p (t m) -> p t m", t=TILES), ACT.Tanh, bias=bias, scale=0.5)
+
+        round_half("w2", 0, nc.scalar.copy)
+        round_half("w2", 1, nc.vector.tensor_copy)
+        value_weights = quantised("w2", 1)
+        den_sum, term = {}, {}
+
+        def denominator(t, tag):
+            den_sum[t] = keep.tile([P, S], F32, name=f"den_sum{t}", tag=tag, align_bytes=64)
+            nc.vector.tensor_tensor(den_sum[t][:], dens[t][:].indirect(par_sb[:]), ek[t], ALU.add)
+
+        def invert(t):
+            if t in SIGN_ON_VECTOR:
+                nc.vector.tensor_scalar(sign[t][:], den_sum[t][:], 0.0, 0.5, ALU.is_ge, ALU.subtract)
+            else:
+                nc.scalar.activation(sign[t][:], den_sum[t][:], ACT.Sign)
+            scale = 1.0 if t in SIGN_ON_VECTOR else 2.0
+            nc.scalar.activation(roots[:, columns(t, S)], den_sum[t][:], ACT.Abs_reciprocal_sqrt, scale=scale)
+            nc.scalar.activation(inverse[t][:], roots[:, columns(t, S)], ACT.Square)
+
         roots = keep.tile([P, TILES * S], F32, name="roots", tag="roots", align_bytes=64)
-        for t in EARLY:
-            bias = first_root_bias[:] if t == EARLY[0] else 0.0
-            nc.scalar.activation(roots[:, columns(t, S)], den_sum[t][:], ACT.Abs_reciprocal_sqrt, bias=bias, scale=2.0)
-        for t in EARLY:
-            value[t] = product(value_weights[t], den_bank[t])
-        for t in EARLY:
-            nc.scalar.activation(inverse[t][:], roots[:, columns(t, S)], ACT.Square)
 
-        held = keep.tile([P, (len(LATE) + TILES) * S], F32, name="held", tag="after_first_root", align_bytes=64)
-        term = [held[:, columns(len(LATE) + t, S)] for t in range(TILES)]
-        for i, t in enumerate(LATE):
-            sign[t] = held[:, columns(i, S)]
-            nc.scalar.activation(sign[t], den_sum[t][:], ACT.Sign)
-            nc.scalar.activation(roots[:, columns(t, S)], den_sum[t][:], ACT.Abs_reciprocal_sqrt, scale=2.0)
-        for t in LATE:
-            nc.scalar.activation(inverse[t][:], roots[:, columns(t, S)], ACT.Square)
+        back = {}
 
-        for t in range(TILES):
-            nc.vector.tensor_tensor(term[t], value[t][:], ek[t][:], ALU.mult)
-            if t == 0:
-                value[TILES - 1] = product(value_weights[TILES - 1], "value")
-            if t in num_sum:
-                add_turned(num_sum[t], term[t], False)
+        def value_term(t):
+            term[t] = keep.tile([P, S], F32, name=f"term{t}", tag=f"term{t}", align_bytes=64)
+            acc = bank(f"product{t}")
+            product(acc[:], value_weights, x, columns(t, P), everything)
+            nc.vector.tensor_tensor(term[t][:], acc[:], ek[t], ALU.mult)
+            add_turned(num_sum[t], term[t], False, True)
+
+        def gate(t):
+            nc.vector.scalar_tensor_tensor(gated[t][:], th[:, t].rearrange("p b m -> p (b m)"), 1.0, num_sum[t][:], ALU.add, ALU.mult)
+            back[t] = turned_back(f"num{t}", gated[t])
 
         def divide(t):
-            nc.gpsimd.tensor_tensor(signed[t][:], inverse[t][:], sign[t], ALU.mult)
-            nc.vector.tensor_tensor(quotient[t][:], num_sum[t][:], signed[t][:], ALU.mult)
-
-        def finish(t):
-            back = bank(den_bank[t])
-            for b in range(BLOCKS):
-                cols = columns(b, P)
-                nc.tensor.matmul(back[:, cols], quotient[t][:, cols], ident[:], start=True, stop=True, is_transpose=True)
-            nc.vector.scalar_tensor_tensor(result[t][:], th[t][:], 1.0, back[:], ALU.add, ALU.mult)
+            if t == LAST:
+                nc.vector.tensor_tensor(signed[t][:], back[t][:], sign[t][:], ALU.mult)
+                nc.vector.tensor_tensor(result[t][:], signed[t][:], inverse[t][:], ALU.mult)
+            else:
+                nc.gpsimd.tensor_tensor(signed[t][:], inverse[t][:], sign[t][:], ALU.mult)
+                nc.vector.tensor_tensor(result[t][:], back[t][:], signed[t][:], ALU.mult)
             nc.sync.dma_start(out=by_tile(out)[t], in_=result[t][:])
 
-        first, second = EARLY
-        third = LATE[0]
-        nc.vector.tensor_tensor(signed[ON_VECTOR][:], num_sum[ON_VECTOR][:], sign[ON_VECTOR], ALU.mult)
-        divide(first)
-        finish(first)
-        num_sum[third] = open_sum(f"product{first}", picked_num[third])
-        add_turned(num_sum[third], term[third], False)
-        divide(second)
-        finish(second)
-        nc.vector.tensor_tensor(quotient[ON_VECTOR][:], signed[ON_VECTOR][:], inverse[ON_VECTOR][:], ALU.mult)
-        divide(third)
-        finish(ON_VECTOR)
-        finish(third)
+        for t in range(LAST):
+            denominator(t, f"den_sum{t}")
+            invert(t)
+        value_term(0)
+        value_term(1)
+        denominator(LAST, "term0")
+        invert(LAST)
+        value_term(2)
+        gate(0)
+        value_term(3)
+        gate(1)
+        gate(2)
+        divide(0)
+        gate(3)
+        divide(1)
+        divide(2)
+        divide(3)

@@ -22,9 +22,11 @@ TILES = N // P
 QUADRANTS = 4
 LIST_ROWS = 16
 BLOCKS = S // P
-LAST = TILES - 1
+LAST = 0
 HALVES = 2
+PAIR = 2
 SIGN_ON_VECTOR = ()
+LOADS = {"w1": 1, "w2": 1, "w3": 1}
 
 
 def tile_picked_wkv8_none_p_kernel(
@@ -36,7 +38,7 @@ def tile_picked_wkv8_none_p_kernel(
         psum = ctx.enter_context(tc.psum_pool(name="psum", bufs=1))
 
         def f32_tiles(name, width=S):
-            return [keep.tile([P, width], F32, name=f"{name}{t}", align_bytes=64) for t in range(TILES)]
+            return [keep.tile([P, width], F32, name=f"{name}{t}", tag=f"{name}{t}", align_bytes=64) for t in range(TILES)]
 
         def columns(i, width):
             return slice(i * width, (i + 1) * width)
@@ -52,13 +54,21 @@ def tile_picked_wkv8_none_p_kernel(
         x_bytes = keep.tile([P, S], U8, name="x_bytes", align_bytes=64)
         ident = keep.tile([P, P], F32, name="ident")
         raw = {
-            (n, h): keep.tile([P, PACK, N // HALVES], F32, name=f"raw_{n}_{h}", tag=f"raw_{n}_{h}", align_bytes=64)
-            for n in ("w1", "w2", "w3")
+            (n, h): keep.tile([P, PACK, N // parts], F32, name=f"raw_{n}_{h}", tag=f"raw_{n}_{h}", align_bytes=64)
+            for n, parts in LOADS.items()
+            for h in range(parts)
+        }
+        rounded = {
+            (n, h): keep.tile([P, PAIR, P, PACK], BF16, name=f"rounded_{n}_{h}", tag=f"rounded_{n}_{h}", align_bytes=64)
+            for n in LOADS
             for h in range(HALVES)
+            if n not in []
         }
         dens, nums = f32_tiles("den", 2 * S), f32_tiles("num", 2 * S)
-        (picked_num,) = (f32_tiles(n) for n in ("picked_num",))
-        sign, inverse, signed, gated, result = (f32_tiles(n) for n in ("sign", "inverse", "signed", "gated", "result"))
+        picked_num = f32_tiles("picked_num")
+        den_sum, term = {}, {}
+        sign, inverse, gated, result = (f32_tiles(n) for n in ("sign", "inverse", "gated", "result"))
+        signed = {}
         th = keep.tile([P, TILES, BLOCKS, P], F32, name="th", align_bytes=64)
 
         nc.vector.memset(scale_table[:].bitcast(I32), 0)
@@ -70,8 +80,8 @@ def tile_picked_wkv8_none_p_kernel(
         for t in range(TILES):
             loads[f"den{t}"] = (dens[t][:, :S], by_tile(den)[t])
         for n, w in (("w1", w1), ("w2", w2), ("w3", w3)):
-            for h in range(HALVES):
-                loads[n + "ab"[h]] = (raw[n, h][:], w.rearrange("(p j) c -> p j c", j=PACK)[:, :, columns(h, N // HALVES)])
+            for h in range(LOADS[n]):
+                loads[n + "ab"[h]] = (raw[n, h][:], w.rearrange("(p j) c -> p j c", j=PACK)[:, :, columns(h, N // LOADS[n])])
         loads["x"] = (word_table[:], x_words[0].rearrange("p n t -> p (n t)").bitcast(I32))
         nc.sync.dma_start(par_sb[:], par)
         nc.sync.dma_start(out=loads["num0"][0], in_=loads["num0"][1])
@@ -81,38 +91,31 @@ def tile_picked_wkv8_none_p_kernel(
                 out=scale_table[32 * g : 32 * g + 4, :].bitcast(I32),
                 in_=x_scales[0, 4 * g : 4 * g + 4, :].bitcast(I32),
             )
-        for n in ["w1a","num1","w1b","num2","x","w3a","num3","w3b","w2a","den0","w2b","den1","den2","den3"]:
+        for n in ["num1","w1a","num2","x","num3","w3a","den1","w2a","den2","den3","den0"]:
             nc.sync.dma_start(out=loads[n][0], in_=loads[n][1])
 
         def on_gpsimd(out, in_):
             order = "p m j t -> p t m j"
             nc.gpsimd.tensor_scalar(out.rearrange(order), in_.rearrange(order), 1.0, 0.0, ALU.mult, ALU.add)
 
-        rounded = {n: keep.tile([P, TILES, P, PACK], BF16, name=f"rounded_{n}", align_bytes=64) for n in ("w1", "w2", "w3")}
-
         def round_half(name, h, copy):
-            copy(
-                out=rounded[name][:, :, columns(h, P // HALVES), :].rearrange("p t m j -> p m j t"),
-                in_=raw[name, h][:].rearrange("p j (m t) -> p m j t", t=TILES),
-            )
+            by_column = raw[name, 0][:].rearrange("p j (m t) -> p m j t", t=TILES)
+            copy(out=rounded[name, h][:].rearrange("p t m j -> p m j t"), in_=by_column[:, :, :, columns(h, PAIR)])
 
-        def quantised(name, groups):
+        def quantised(name, order):
             codes = keep.tile([P, N], U32, name=f"codes_{name}", align_bytes=64)
             scales = keep.tile([P, N], U8, name=f"scales_{name}", align_bytes=64)
-            per = TILES // groups
-            for g in range(groups):
-                cols = columns(g, per * P)
+            for h in order:
+                cols = columns(h, PAIR * P)
                 nc.vector.quantize_mx(
-                    out=codes[:, cols].bitcast(FP8X4),
-                    scales=scales[:, cols],
-                    in_=rounded[name][:, columns(g, per)].rearrange("p t m j -> p (t m j)"),
+                    out=codes[:, cols].bitcast(FP8X4), scales=scales[:, cols], in_=rounded[name, h][:].rearrange("p t m j -> p (t m j)")
                 )
             return codes, scales
 
         def bank(tag):
             return psum.tile([P, S], F32, name=tag, tag=tag)
 
-        def product(acc, stationary, moving, s_cols, m_cols):
+        def product(acc, stationary, moving, s_cols, m_cols=slice(0, S)):
             nc.tensor.matmul_mx(
                 out=acc,
                 lhsT=stationary[0][:, s_cols].bitcast(FP8X4),
@@ -136,42 +139,48 @@ def tile_picked_wkv8_none_p_kernel(
                 nc.tensor.matmul(acc[:, cols], tile[:, cols], ident[:], start=True, stop=True, is_transpose=True)
             return acc
 
-        everything = slice(0, S)
         x = (x_codes, x_bytes)
         nc.vector.tensor_copy(x_bytes[:], scale_table[:].indirect(offs_sb[:]))
         nc.vector.tensor_copy(x_codes[:], word_table[:].bitcast(U32).indirect(offs_sb[:]))
         round_half("w1", 0, nc.scalar.copy)
-        round_half("w1", 1, nc.scalar.copy)
-        key_weights = quantised("w1", 2)
-        round_half("w3", 0, nc.scalar.copy)
-        ek_all = keep.tile([P, TILES, S], F32, name="ek", tag="raw_w3_0", align_bytes=64)
-        ek = [ek_all[:, t] for t in range(TILES)]
-        for t in range(TILES):
+        round_half("w1", 1, nc.vector.tensor_copy)
+        key_weights = quantised("w1", (1, 0))
+        ek = keep.tile([P, TILES, S], F32, name="ek", tag="ek", align_bytes=64)
+        for t in (2, 3, 1, 0):
             acc = bank(f"product{t}")
-            product(acc[:], key_weights, x, columns(t, P), everything)
-            nc.scalar.activation(ek[t], acc[:], ACT.Exp, scale=0.5)
-        num_sum = []
+            product(acc[:], key_weights, x, columns(t, P))
+            nc.scalar.activation(ek[:, t], acc[:], ACT.Exp, scale=0.5)
+
+        round_half("w3", 0, nc.vector.tensor_copy)
+        round_half("w3", 1, nc.vector.tensor_copy)
+        gate_weights = quantised("w3", (0, 1))
+        for g in range(TILES):
+            h, half = divmod(g, HALVES)
+            acc = bank(f"product{g}")
+            for i in range(PAIR):
+                product(acc[:, columns(i, PAIR * P)], x, gate_weights, columns(PAIR * half + i, P), columns(h, PAIR * P))
+            bias = last_gate_bias[:] if g == TILES - 1 else 0.0
+            nc.scalar.activation(
+                th[:, columns(h, PAIR), columns(half, PAIR), :].rearrange("p t b m -> p b t m"),
+                acc[:].rearrange("p (b t m) -> p b t m", b=PAIR, t=PAIR),
+                ACT.Tanh,
+                bias=bias,
+                scale=0.5,
+            )
+
+        round_half("w2", 0, nc.vector.tensor_copy)
+        round_half("w2", 1, nc.vector.tensor_copy)
+        value_weights = quantised("w2", (0, 1))
+        roots = keep.tile([P, TILES * S], F32, name="roots", tag="roots", align_bytes=64)
+        num_sum, back = {}, {}
         for t in range(TILES):
             nc.vector.tensor_copy(picked_num[t][:], nums[t][:].indirect(par_sb[:]))
-            num_sum.append(bank(f"num{t}"))
+            num_sum[t] = bank(f"num{t}")
             add_turned(num_sum[t], picked_num[t], True, False)
-
-        round_half("w3", 1, nc.vector.tensor_copy)
-        gate_weights = quantised("w3", 1)
-        for b in range(BLOCKS):
-            acc = bank(f"product{b}")
-            product(acc[:], x, gate_weights, columns(b, P), everything)
-            bias = last_gate_bias[:] if b == BLOCKS - 1 else 0.0
-            nc.scalar.activation(th[:, :, b, :], acc[:].rearrange("p (t m) -> p t m", t=TILES), ACT.Tanh, bias=bias, scale=0.5)
-
-        round_half("w2", 0, nc.scalar.copy)
-        round_half("w2", 1, nc.vector.tensor_copy)
-        value_weights = quantised("w2", 1)
-        den_sum, term = {}, {}
 
         def denominator(t, tag):
             den_sum[t] = keep.tile([P, S], F32, name=f"den_sum{t}", tag=tag, align_bytes=64)
-            nc.vector.tensor_tensor(den_sum[t][:], dens[t][:].indirect(par_sb[:]), ek[t], ALU.add)
+            nc.vector.tensor_tensor(den_sum[t][:], dens[t][:].indirect(par_sb[:]), ek[:, t], ALU.add)
 
         def invert(t):
             if t in SIGN_ON_VECTOR:
@@ -182,15 +191,15 @@ def tile_picked_wkv8_none_p_kernel(
             nc.scalar.activation(roots[:, columns(t, S)], den_sum[t][:], ACT.Abs_reciprocal_sqrt, scale=scale)
             nc.scalar.activation(inverse[t][:], roots[:, columns(t, S)], ACT.Square)
 
-        roots = keep.tile([P, TILES * S], F32, name="roots", tag="roots", align_bytes=64)
+        value = {}
 
-        back = {}
+        def value_product(t):
+            value[t] = bank(f"product{t}")
+            product(value[t][:], value_weights, x, columns(t, P))
 
         def value_term(t):
             term[t] = keep.tile([P, S], F32, name=f"term{t}", tag=f"term{t}", align_bytes=64)
-            acc = bank(f"product{t}")
-            product(acc[:], value_weights, x, columns(t, P), everything)
-            nc.vector.tensor_tensor(term[t][:], acc[:], ek[t], ALU.mult)
+            nc.vector.tensor_tensor(term[t][:], value[t][:], ek[:, t], ALU.mult)
             add_turned(num_sum[t], term[t], False, True)
 
         def gate(t):
@@ -198,6 +207,8 @@ def tile_picked_wkv8_none_p_kernel(
             back[t] = turned_back(f"num{t}", gated[t])
 
         def divide(t):
+            tag = "den0" if t == 1 else f"signed{t}"
+            signed[t] = keep.tile([P, S], F32, name=f"signed{t}", tag=tag, align_bytes=64)
             if t == LAST:
                 nc.vector.tensor_tensor(signed[t][:], back[t][:], sign[t][:], ALU.mult)
                 nc.vector.tensor_tensor(result[t][:], signed[t][:], inverse[t][:], ALU.mult)
@@ -206,20 +217,24 @@ def tile_picked_wkv8_none_p_kernel(
                 nc.vector.tensor_tensor(result[t][:], back[t][:], signed[t][:], ALU.mult)
             nc.sync.dma_start(out=by_tile(out)[t], in_=result[t][:])
 
-        for t in range(LAST):
+        for t in range(TILES):
+            value_product(t)
+        for t in (1, 2):
             denominator(t, f"den_sum{t}")
             invert(t)
         value_term(0)
         value_term(1)
-        denominator(LAST, "term0")
-        invert(LAST)
+        denominator(3, "den_sum3")
+        invert(3)
         value_term(2)
         gate(0)
+        denominator(0, "term0")
+        invert(0)
         value_term(3)
         gate(1)
         gate(2)
-        divide(0)
-        gate(3)
         divide(1)
+        gate(3)
         divide(2)
+        divide(0)
         divide(3)

@@ -67,7 +67,8 @@ def tile_picked_wkv8_none_p_kernel(
         dens, nums = f32_tiles("den", 2 * S), f32_tiles("num", 2 * S)
         picked_num = f32_tiles("picked_num")
         den_sum, term = {}, {}
-        sign, inverse, gated, result = (f32_tiles(n) for n in ("sign", "inverse", "gated", "result"))
+        inverse, gated, result = (f32_tiles(n) for n in ("inverse", "gated", "result"))
+        sign = {}
         signed = {}
         th = keep.tile([P, TILES, BLOCKS, P], F32, name="th", align_bytes=64)
 
@@ -91,7 +92,7 @@ def tile_picked_wkv8_none_p_kernel(
                 out=scale_table[32 * g : 32 * g + 4, :].bitcast(I32),
                 in_=x_scales[0, 4 * g : 4 * g + 4, :].bitcast(I32),
             )
-        for n in ["num1","w1a","num2","x","num3","w3a","den1","w2a","den2","den3","den0"]:
+        for n in ["num1","w1a","num2","x","num3","den0","w3a","den1","w2a","den2","den3"]:
             nc.sync.dma_start(out=loads[n][0], in_=loads[n][1])
 
         def on_gpsimd(out, in_):
@@ -102,14 +103,17 @@ def tile_picked_wkv8_none_p_kernel(
             by_column = raw[name, 0][:].rearrange("p j (m t) -> p m j t", t=TILES)
             copy(out=rounded[name, h][:].rearrange("p t m j -> p m j t"), in_=by_column[:, :, :, columns(h, PAIR)])
 
-        def quantised(name, order):
-            codes = keep.tile([P, N], U32, name=f"codes_{name}", align_bytes=64)
-            scales = keep.tile([P, N], U8, name=f"scales_{name}", align_bytes=64)
-            for h in order:
-                cols = columns(h, PAIR * P)
-                nc.vector.quantize_mx(
-                    out=codes[:, cols].bitcast(FP8X4), scales=scales[:, cols], in_=rounded[name, h][:].rearrange("p t m j -> p (t m j)")
-                )
+        def round_part(name, h, part, copy):
+            rows = columns(part, P // HALVES)
+            by_column = raw[name, 0][:].rearrange("p j (m t) -> p m j t", t=TILES)
+            copy(out=rounded[name, h][:, :, rows].rearrange("p t m j -> p m j t"), in_=by_column[:, rows, :, columns(h, PAIR)])
+
+        def quantised(name, h, tag=None):
+            codes = keep.tile([P, PAIR * P], U32, name=f"codes_{name}_{h}", tag=tag or f"codes_{name}_{h}", align_bytes=64)
+            scales = keep.tile([P, PAIR * P], U8, name=f"scales_{name}_{h}", align_bytes=64)
+            nc.vector.quantize_mx(
+                out=codes[:].bitcast(FP8X4), scales=scales[:], in_=rounded[name, h][:].rearrange("p t m j -> p (t m j)")
+            )
             return codes, scales
 
         def bank(tag):
@@ -144,21 +148,33 @@ def tile_picked_wkv8_none_p_kernel(
         nc.vector.tensor_copy(x_codes[:], word_table[:].bitcast(U32).indirect(offs_sb[:]))
         round_half("w1", 0, nc.scalar.copy)
         round_half("w1", 1, nc.vector.tensor_copy)
-        key_weights = quantised("w1", (1, 0))
+        key_weights = {h: quantised("w1", h) for h in (1, 0)}
         ek = keep.tile([P, TILES, S], F32, name="ek", tag="ek", align_bytes=64)
         for t in (2, 3, 1, 0):
             acc = bank(f"product{t}")
-            product(acc[:], key_weights, x, columns(t, P))
+            product(acc[:], key_weights[t // PAIR], x, columns(t % PAIR, P))
             nc.scalar.activation(ek[:, t], acc[:], ACT.Exp, scale=0.5)
 
+        picked_den = keep.tile([P, S], F32, name="picked_den", align_bytes=64)
+        nc.vector.tensor_copy(picked_den[:], dens[LAST][:].indirect(par_sb[:]))
         round_half("w3", 0, nc.vector.tensor_copy)
-        round_half("w3", 1, nc.vector.tensor_copy)
-        gate_weights = quantised("w3", (0, 1))
+        round_part("w3", 1, 0, nc.scalar.copy)
+        round_part("w3", 1, 1, nc.vector.tensor_copy)
+        def denominator(t, tag):
+            den_sum[t] = keep.tile([P, S], F32, name=f"den_sum{t}", tag=tag, align_bytes=64)
+            if t == LAST:
+                nc.gpsimd.tensor_tensor(den_sum[t][:], picked_den[:], ek[:, t], ALU.add)
+            else:
+                nc.vector.tensor_tensor(den_sum[t][:], dens[t][:].indirect(par_sb[:]), ek[:, t], ALU.add)
+
+        gate_weights = {0: quantised("w3", 0)}
+        denominator(1, "den_sum1")
+        gate_weights[1] = quantised("w3", 1, "rounded_w3_0")
         for g in range(TILES):
             h, half = divmod(g, HALVES)
             acc = bank(f"product{g}")
             for i in range(PAIR):
-                product(acc[:, columns(i, PAIR * P)], x, gate_weights, columns(PAIR * half + i, P), columns(h, PAIR * P))
+                product(acc[:, columns(i, PAIR * P)], x, gate_weights[h], columns(PAIR * half + i, P), slice(0, PAIR * P))
             bias = last_gate_bias[:] if g == TILES - 1 else 0.0
             nc.scalar.activation(
                 th[:, columns(h, PAIR), columns(half, PAIR), :].rearrange("p t b m -> p b t m"),
@@ -170,7 +186,7 @@ def tile_picked_wkv8_none_p_kernel(
 
         round_half("w2", 0, nc.vector.tensor_copy)
         round_half("w2", 1, nc.vector.tensor_copy)
-        value_weights = quantised("w2", (0, 1))
+        value_weights = {h: quantised("w2", h) for h in (0, 1)}
         roots = keep.tile([P, TILES * S], F32, name="roots", tag="roots", align_bytes=64)
         num_sum, back = {}, {}
         for t in range(TILES):
@@ -178,11 +194,8 @@ def tile_picked_wkv8_none_p_kernel(
             num_sum[t] = bank(f"num{t}")
             add_turned(num_sum[t], picked_num[t], True, False)
 
-        def denominator(t, tag):
-            den_sum[t] = keep.tile([P, S], F32, name=f"den_sum{t}", tag=tag, align_bytes=64)
-            nc.vector.tensor_tensor(den_sum[t][:], dens[t][:].indirect(par_sb[:]), ek[:, t], ALU.add)
-
         def invert(t):
+            sign[t] = keep.tile([P, S], F32, name=f"sign{t}", tag="rounded_w3_1" if t == 1 else f"sign{t}", align_bytes=64)
             if t in SIGN_ON_VECTOR:
                 nc.vector.tensor_scalar(sign[t][:], den_sum[t][:], 0.0, 0.5, ALU.is_ge, ALU.subtract)
             else:
@@ -195,7 +208,7 @@ def tile_picked_wkv8_none_p_kernel(
 
         def value_product(t):
             value[t] = bank(f"product{t}")
-            product(value[t][:], value_weights, x, columns(t, P))
+            product(value[t][:], value_weights[t // PAIR], x, columns(t % PAIR, P))
 
         def value_term(t):
             term[t] = keep.tile([P, S], F32, name=f"term{t}", tag=f"term{t}", align_bytes=64)
@@ -207,7 +220,7 @@ def tile_picked_wkv8_none_p_kernel(
             back[t] = turned_back(f"num{t}", gated[t])
 
         def divide(t):
-            tag = "den0" if t == 1 else f"signed{t}"
+            tag = f"signed{t}"
             signed[t] = keep.tile([P, S], F32, name=f"signed{t}", tag=tag, align_bytes=64)
             if t == LAST:
                 nc.vector.tensor_tensor(signed[t][:], back[t][:], sign[t][:], ALU.mult)
@@ -219,22 +232,21 @@ def tile_picked_wkv8_none_p_kernel(
 
         for t in range(TILES):
             value_product(t)
-        for t in (1, 2):
+        invert(1)
+        for t in (2, 3):
             denominator(t, f"den_sum{t}")
             invert(t)
+        denominator(0, "den3")
+        invert(0)
         value_term(0)
         value_term(1)
-        denominator(3, "den_sum3")
-        invert(3)
         value_term(2)
         gate(0)
-        denominator(0, "term0")
-        invert(0)
         value_term(3)
         gate(1)
         gate(2)
         divide(1)
         gate(3)
         divide(2)
-        divide(0)
         divide(3)
+        divide(0)

@@ -62,7 +62,7 @@ def tile_picked_wkv8_none_p_kernel(
             (n, h): keep.tile([P, PAIR, P, PACK], BF16, name=f"rounded_{n}_{h}", tag=f"rounded_{n}_{h}", align_bytes=64)
             for n in LOADS
             for h in range(HALVES)
-            if n not in []
+            if n != "w2"
         }
         dens, nums = f32_tiles("den", 2 * S), f32_tiles("num", 2 * S)
         picked_num = f32_tiles("picked_num")
@@ -146,33 +146,41 @@ def tile_picked_wkv8_none_p_kernel(
         x = (x_codes, x_bytes)
         nc.vector.tensor_copy(x_bytes[:], scale_table[:].indirect(offs_sb[:]))
         nc.vector.tensor_copy(x_codes[:], word_table[:].bitcast(U32).indirect(offs_sb[:]))
-        round_half("w1", 0, nc.scalar.copy)
-        round_half("w1", 1, nc.vector.tensor_copy)
-        key_weights = {h: quantised("w1", h) for h in (1, 0)}
-        ek = keep.tile([P, TILES, S], F32, name="ek", tag="ek", align_bytes=64)
-        for t in (2, 3, 1, 0):
-            acc = bank(f"product{t}")
-            product(acc[:], key_weights[t // PAIR], x, columns(t % PAIR, P))
-            nc.scalar.activation(ek[:, t], acc[:], ACT.Exp, scale=0.5)
+        round_half("w1", 1, nc.scalar.copy)
+        round_half("w1", 0, nc.vector.tensor_copy)
+        key_weights = {h: quantised("w1", h) for h in (0, 1)}
+        keys, ek = {}, {}
+        for t in (1, 0, 2, 3):
+            keys[t] = bank(f"product{t}")
+            product(keys[t][:], key_weights[t // PAIR], x, columns(t % PAIR, P))
+
+        def exponentials(h, tag, order):
+            pair = keep.tile([P, PAIR, S], F32, name=f"ek{h}", tag=tag, align_bytes=64)
+            for t in order:
+                ek[t] = pair[:, t % PAIR]
+                nc.scalar.activation(ek[t], keys[t][:], ACT.Exp, scale=0.5)
+
+        exponentials(0, "ek_early", (1, 0))
 
         picked_den = keep.tile([P, S], F32, name="picked_den", align_bytes=64)
         nc.vector.tensor_copy(picked_den[:], dens[LAST][:].indirect(par_sb[:]))
         round_half("w3", 0, nc.vector.tensor_copy)
         round_part("w3", 1, 0, nc.scalar.copy)
         round_part("w3", 1, 1, nc.vector.tensor_copy)
+        exponentials(1, "raw_w3_0", (2, 3))
         def denominator(t, tag):
             den_sum[t] = keep.tile([P, S], F32, name=f"den_sum{t}", tag=tag, align_bytes=64)
             if t == LAST:
-                nc.gpsimd.tensor_tensor(den_sum[t][:], picked_den[:], ek[:, t], ALU.add)
+                nc.gpsimd.tensor_tensor(den_sum[t][:], picked_den[:], ek[t], ALU.add)
             else:
-                nc.vector.tensor_tensor(den_sum[t][:], dens[t][:].indirect(par_sb[:]), ek[:, t], ALU.add)
+                nc.vector.tensor_tensor(den_sum[t][:], dens[t][:].indirect(par_sb[:]), ek[t], ALU.add)
 
         gate_weights = {0: quantised("w3", 0)}
+        gate_weights[1] = quantised("w3", 1)
         denominator(1, "den_sum1")
-        gate_weights[1] = quantised("w3", 1, "rounded_w3_0")
         for g in range(TILES):
             h, half = divmod(g, HALVES)
-            acc = bank(f"product{g}")
+            acc = bank(f"product{(1, 0, 2, 3)[g]}")
             for i in range(PAIR):
                 product(acc[:, columns(i, PAIR * P)], x, gate_weights[h], columns(PAIR * half + i, P), slice(0, PAIR * P))
             bias = last_gate_bias[:] if g == TILES - 1 else 0.0
@@ -184,8 +192,10 @@ def tile_picked_wkv8_none_p_kernel(
                 scale=0.5,
             )
 
-        round_half("w2", 0, nc.vector.tensor_copy)
-        round_half("w2", 1, nc.vector.tensor_copy)
+        whole = keep.tile([P, TILES, P, PACK], BF16, name="rounded_w2", align_bytes=64)
+        nc.vector.tensor_copy(out=whole[:].rearrange("p t m j -> p m j t"), in_=raw["w2", 0][:].rearrange("p j (m t) -> p m j t", t=TILES))
+        for h in range(HALVES):
+            rounded["w2", h] = whole[:, columns(h, PAIR)]
         value_weights = {h: quantised("w2", h) for h in (0, 1)}
         roots = keep.tile([P, TILES * S], F32, name="roots", tag="roots", align_bytes=64)
         num_sum, back = {}, {}
@@ -212,7 +222,7 @@ def tile_picked_wkv8_none_p_kernel(
 
         def value_term(t):
             term[t] = keep.tile([P, S], F32, name=f"term{t}", tag=f"term{t}", align_bytes=64)
-            nc.vector.tensor_tensor(term[t][:], value[t][:], ek[:, t], ALU.mult)
+            nc.vector.tensor_tensor(term[t][:], value[t][:], ek[t], ALU.mult)
             add_turned(num_sum[t], term[t], False, True)
 
         def gate(t):
@@ -233,12 +243,13 @@ def tile_picked_wkv8_none_p_kernel(
         for t in range(TILES):
             value_product(t)
         invert(1)
-        for t in (2, 3):
-            denominator(t, f"den_sum{t}")
-            invert(t)
+        denominator(2, "den_sum2")
+        invert(2)
+        value_term(0)
+        denominator(3, "den_sum3")
+        invert(3)
         denominator(0, "den3")
         invert(0)
-        value_term(0)
         value_term(1)
         value_term(2)
         gate(0)

@@ -25,6 +25,7 @@ BLOCKS = S // P
 LAST = 0
 HALVES = 2
 PAIR = 2
+SCALE_STEP = 8
 SIGN_ON_VECTOR = ()
 LOADS = {"w1": 1, "w2": 1, "w3": 1}
 
@@ -73,9 +74,13 @@ def tile_picked_wkv8_none_p_kernel(
         th = keep.tile([P, TILES, BLOCKS, P], F32, name="th", align_bytes=64)
 
         nc.vector.memset(scale_table[:].bitcast(I32), 0)
+        nc.vector.memset(x_bytes[:].bitcast(I32), 0)
+        picked_bytes = keep.tile([P, S], U8, name="picked_bytes", align_bytes=64)
         make_identity(nc, ident[:])
         last_gate_bias = keep.tile([P, 1], F32, name="last_gate_bias", tag="roots", align_bytes=64)
-        nc.scalar.activation(last_gate_bias[:], ident[:, 0:1], ACT.Copy, scale=0.0)
+        zero = keep.tile([P, 1], F32, name="zero")
+        nc.vector.memset(zero[:], 0.0)
+        nc.scalar.copy(out=last_gate_bias[:], in_=zero[:])
 
         loads = {f"num{t}": (nums[t][:, :S], by_tile(num)[t]) for t in range(TILES)}
         for t in range(TILES):
@@ -84,14 +89,10 @@ def tile_picked_wkv8_none_p_kernel(
             for h in range(LOADS[n]):
                 loads[n + "ab"[h]] = (raw[n, h][:], w.rearrange("(p j) c -> p j c", j=PACK)[:, :, columns(h, N // LOADS[n])])
         loads["x"] = (word_table[:], x_words[0].rearrange("p n t -> p (n t)").bitcast(I32))
-        nc.sync.dma_start(par_sb[:], par)
-        nc.sync.dma_start(out=loads["num0"][0], in_=loads["num0"][1])
         nc.sync.dma_start(offs_sb[:], offs)
-        for g in range(QUADRANTS):
-            nc.sync.dma_start(
-                out=scale_table[32 * g : 32 * g + 4, :].bitcast(I32),
-                in_=x_scales[0, 4 * g : 4 * g + 4, :].bitcast(I32),
-            )
+        nc.sync.dma_start(out=loads["num0"][0], in_=loads["num0"][1])
+        nc.sync.dma_start(out=scale_table[0:P:SCALE_STEP, :].bitcast(I32), in_=x_scales[0].bitcast(I32))
+        nc.sync.dma_start(par_sb[:], par)
         for n in ["num1","w1a","num2","x","num3","den0","w3a","den1","w2a","den2","den3"]:
             nc.sync.dma_start(out=loads[n][0], in_=loads[n][1])
 
@@ -144,7 +145,9 @@ def tile_picked_wkv8_none_p_kernel(
             return acc
 
         x = (x_codes, x_bytes)
-        nc.vector.tensor_copy(x_bytes[:], scale_table[:].indirect(offs_sb[:]))
+        nc.vector.tensor_copy(picked_bytes[:], scale_table[:].indirect(offs_sb[:]))
+        for r in range(PACK):
+            nc.scalar.dma_start(out=x_bytes[r:P:32, :].bitcast(I32), in_=picked_bytes[SCALE_STEP * r : P : 32, :].bitcast(I32))
         nc.vector.tensor_copy(x_codes[:], word_table[:].bitcast(U32).indirect(offs_sb[:]))
         round_half("w1", 1, nc.scalar.copy)
         round_half("w1", 0, nc.vector.tensor_copy)

@@ -68,7 +68,8 @@ def tile_picked_wkv8_none_p_kernel(
         dens, nums = f32_tiles("den", 2 * S), f32_tiles("num", 2 * S)
         picked_num = f32_tiles("picked_num")
         den_sum, term = {}, {}
-        inverse, gated, result = (f32_tiles(n) for n in ("inverse", "gated", "result"))
+        inverse, gated = (f32_tiles(n) for n in ("inverse", "gated"))
+        result = {}
         sign = {}
         signed = {}
         th = keep.tile([P, TILES, BLOCKS, P], F32, name="th", align_bytes=64)
@@ -207,14 +208,14 @@ def tile_picked_wkv8_none_p_kernel(
             num_sum[t] = bank(f"num{t}")
             add_turned(num_sum[t], picked_num[t], True, False)
 
-        def invert(t):
-            sign[t] = keep.tile([P, S], F32, name=f"sign{t}", tag="rounded_w3_1" if t == 1 else f"sign{t}", align_bytes=64)
-            if t in SIGN_ON_VECTOR:
-                nc.vector.tensor_scalar(sign[t][:], den_sum[t][:], 0.0, 0.5, ALU.is_ge, ALU.subtract)
-            else:
-                nc.scalar.activation(sign[t][:], den_sum[t][:], ACT.Sign)
-            scale = 1.0 if t in SIGN_ON_VECTOR else 2.0
-            nc.scalar.activation(roots[:, columns(t, S)], den_sum[t][:], ACT.Abs_reciprocal_sqrt, scale=scale)
+        def take_sign(t):
+            sign[t] = keep.tile([P, S], F32, name=f"sign{t}", align_bytes=64)
+            nc.scalar.activation(sign[t][:], den_sum[t][:], ACT.Sign)
+
+        def root(t):
+            nc.scalar.activation(roots[:, columns(t, S)], den_sum[t][:], ACT.Abs_reciprocal_sqrt, scale=2.0)
+
+        def square(t):
             nc.scalar.activation(inverse[t][:], roots[:, columns(t, S)], ACT.Square)
 
         value = {}
@@ -233,26 +234,35 @@ def tile_picked_wkv8_none_p_kernel(
             back[t] = turned_back(f"num{t}", gated[t])
 
         def divide(t):
-            tag = f"signed{t}"
-            signed[t] = keep.tile([P, S], F32, name=f"signed{t}", tag=tag, align_bytes=64)
+            result[t] = keep.tile([P, S], F32, name=f"result{t}", tag="den3" if t == 3 else f"result{t}", align_bytes=64)
             if t == LAST:
-                nc.vector.tensor_tensor(signed[t][:], back[t][:], sign[t][:], ALU.mult)
-                nc.vector.tensor_tensor(result[t][:], signed[t][:], inverse[t][:], ALU.mult)
+                factors = signed[t], inverse[t]
             else:
+                signed[t] = keep.tile([P, S], F32, name=f"signed{t}", align_bytes=64)
                 nc.gpsimd.tensor_tensor(signed[t][:], inverse[t][:], sign[t][:], ALU.mult)
-                nc.vector.tensor_tensor(result[t][:], back[t][:], signed[t][:], ALU.mult)
-            nc.sync.dma_start(out=by_tile(out)[t], in_=result[t][:])
+                factors = back[t], signed[t]
+            parts = HALVES if t in (3, LAST) else 1
+            for h in range(parts):
+                cols = columns(h, S // parts)
+                nc.vector.tensor_tensor(result[t][:, cols], factors[0][:, cols], factors[1][:, cols], ALU.mult)
+                nc.sync.dma_start(out=by_tile(out)[t][:, cols], in_=result[t][:, cols])
 
         for t in range(TILES):
             value_product(t)
-        invert(1)
+        take_sign(1)
         denominator(2, "den_sum2")
-        invert(2)
+        root(1)
+        root(2)
+        square(1)
+        take_sign(2)
+        square(2)
         value_term(0)
         denominator(3, "den_sum3")
-        invert(3)
         denominator(0, "den3")
-        invert(0)
+        for t in (3, 0):
+            root(t)
+            take_sign(t)
+            square(t)
         value_term(1)
         value_term(2)
         gate(0)
@@ -262,5 +272,7 @@ def tile_picked_wkv8_none_p_kernel(
         divide(1)
         gate(3)
         divide(2)
+        signed[LAST] = keep.tile([P, S], F32, name="signed_numerator", align_bytes=64)
+        nc.vector.tensor_tensor(signed[LAST][:], back[LAST][:], sign[LAST][:], ALU.mult)
         divide(3)
         divide(0)

@@ -19,15 +19,12 @@ ALU = mybir.AluOpType
 P = 128
 PACK = 4
 TILES = N // P
-QUADRANTS = 4
+QUADRANT = 32
 LIST_ROWS = 16
 BLOCKS = S // P
-LAST = 0
 HALVES = 2
 PAIR = 2
-SCALE_STEP = 8
-SIGN_ON_VECTOR = ()
-LOADS = {"w1": 1, "w2": 1, "w3": 1}
+HALF_SIGNED = (0,)
 
 
 def tile_picked_wkv8_none_p_kernel(
@@ -38,8 +35,11 @@ def tile_picked_wkv8_none_p_kernel(
         keep = ctx.enter_context(tc.tile_pool(name="keep", bufs=1))
         psum = ctx.enter_context(tc.psum_pool(name="psum", bufs=1))
 
-        def f32_tiles(name, width=S):
-            return [keep.tile([P, width], F32, name=f"{name}{t}", tag=f"{name}{t}", align_bytes=64) for t in range(TILES)]
+        def sbuf(name, shape=(P, S), dtype=F32, tag=None):
+            return keep.tile(list(shape), dtype, name=name, tag=tag or name, align_bytes=64)
+
+        def bank(tag):
+            return psum.tile([P, S], F32, name=tag, tag=tag)
 
         def columns(i, width):
             return slice(i * width, (i + 1) * width)
@@ -49,77 +49,54 @@ def tile_picked_wkv8_none_p_kernel(
 
         offs_sb = keep.tile([P, S // LIST_ROWS], U16, name="offs_sb")
         par_sb = keep.tile([P, S // LIST_ROWS], U16, name="par_sb")
-        word_table = keep.tile([P, T], I32, name="word_table", align_bytes=64)
-        scale_table = keep.tile([P, T], U8, name="scale_table", align_bytes=64)
-        x_codes = keep.tile([P, S], U32, name="x_codes", align_bytes=64)
-        x_bytes = keep.tile([P, S], U8, name="x_bytes", align_bytes=64)
-        ident = keep.tile([P, P], F32, name="ident")
-        raw = {
-            (n, h): keep.tile([P, PACK, N // parts], F32, name=f"raw_{n}_{h}", tag=f"raw_{n}_{h}", align_bytes=64)
-            for n, parts in LOADS.items()
-            for h in range(parts)
-        }
-        rounded = {
-            (n, h): keep.tile([P, PAIR, P, PACK], BF16, name=f"rounded_{n}_{h}", tag=f"rounded_{n}_{h}", align_bytes=64)
-            for n in LOADS
-            for h in range(HALVES)
-            if n != "w2"
-        }
-        dens, nums = f32_tiles("den", 2 * S), f32_tiles("num", 2 * S)
-        picked_num = f32_tiles("picked_num")
-        den_sum, term = {}, {}
-        inverse, gated = (f32_tiles(n) for n in ("inverse", "gated"))
-        result = {}
-        sign = {}
-        signed = {}
-        th = keep.tile([P, TILES, BLOCKS, P], F32, name="th", align_bytes=64)
+        word_table = sbuf("word_table", (P, T), I32)
+        scale_table = sbuf("scale_table", (P, T), U8)
+        x_codes = sbuf("x_codes", dtype=U32)
+        x_bytes = sbuf("x_bytes", dtype=U8)
+        two = sbuf("two", (P, 1))
+        root_scale = sbuf("root_scale", (P, 1))
+        ident = sbuf("ident", (P, P))
+        weights = {"w1": w1, "w2": w2, "w3": w3}
+        raw = {n: sbuf(f"raw_{n}", (P, PACK, N)) for n in weights}
+        tables = {"den": den, "num": num}
+        window = {(n, t): sbuf(f"{n}{t}", (P, 2 * S)) for n in tables for t in range(TILES)}
+        th = sbuf("th", (P, BLOCKS, TILES, P))
 
-        nc.vector.memset(scale_table[:].bitcast(I32), 0)
-        nc.vector.memset(x_bytes[:].bitcast(I32), 0)
-        picked_bytes = keep.tile([P, S], U8, name="picked_bytes", align_bytes=64)
-        make_identity(nc, ident[:])
-        last_gate_bias = keep.tile([P, 1], F32, name="last_gate_bias", tag="roots", align_bytes=64)
-        zero = keep.tile([P, 1], F32, name="zero")
-        nc.vector.memset(zero[:], 0.0)
-        nc.scalar.copy(out=last_gate_bias[:], in_=zero[:])
+        def load_table(n, t):
+            nc.sync.dma_start(out=window[n, t][:, :S], in_=by_tile(tables[n])[t])
 
-        loads = {f"num{t}": (nums[t][:, :S], by_tile(num)[t]) for t in range(TILES)}
-        for t in range(TILES):
-            loads[f"den{t}"] = (dens[t][:, :S], by_tile(den)[t])
-        for n, w in (("w1", w1), ("w2", w2), ("w3", w3)):
-            for h in range(LOADS[n]):
-                loads[n + "ab"[h]] = (raw[n, h][:], w.rearrange("(p j) c -> p j c", j=PACK)[:, :, columns(h, N // LOADS[n])])
-        loads["x"] = (word_table[:], x_words[0].rearrange("p n t -> p (n t)").bitcast(I32))
-        nc.sync.dma_start(offs_sb[:], offs)
-        nc.sync.dma_start(out=loads["num0"][0], in_=loads["num0"][1])
-        nc.sync.dma_start(out=scale_table[0:P:SCALE_STEP, :].bitcast(I32), in_=x_scales[0].bitcast(I32))
-        nc.sync.dma_start(par_sb[:], par)
-        for n in ["num1","w1a","num2","x","num3","den0","w3a","den1","w2a","den2","den3"]:
-            nc.sync.dma_start(out=loads[n][0], in_=loads[n][1])
+        def load_weight(n):
+            nc.sync.dma_start(out=raw[n][:], in_=weights[n].rearrange("(p j) c -> p j c", j=PACK))
 
-        def on_gpsimd(out, in_):
-            order = "p m j t -> p t m j"
-            nc.gpsimd.tensor_scalar(out.rearrange(order), in_.rearrange(order), 1.0, 0.0, ALU.mult, ALU.add)
+        def load_words():
+            nc.sync.dma_start(out=word_table[:], in_=x_words[0].rearrange("p n t -> p (n t)").bitcast(I32))
 
-        def round_half(name, h, copy):
-            by_column = raw[name, 0][:].rearrange("p j (m t) -> p m j t", t=TILES)
-            copy(out=rounded[name, h][:].rearrange("p t m j -> p m j t"), in_=by_column[:, :, :, columns(h, PAIR)])
+        def load_scales():
+            for q in range(P // QUADRANT):
+                rows = slice(QUADRANT * q, QUADRANT * q + PACK)
+                nc.scalar.dma_start(out=scale_table[rows, :].bitcast(I32), in_=x_scales[0][columns(q, PACK), :].bitcast(I32))
 
-        def round_part(name, h, part, copy):
-            rows = columns(part, P // HALVES)
-            by_column = raw[name, 0][:].rearrange("p j (m t) -> p m j t", t=TILES)
-            copy(out=rounded[name, h][:, :, rows].rearrange("p t m j -> p m j t"), in_=by_column[:, rows, :, columns(h, PAIR)])
+        rounded = {}
 
-        def quantised(name, h, tag=None):
-            codes = keep.tile([P, PAIR * P], U32, name=f"codes_{name}_{h}", tag=tag or f"codes_{name}_{h}", align_bytes=64)
-            scales = keep.tile([P, PAIR * P], U8, name=f"scales_{name}_{h}", align_bytes=64)
+        def round_half(n, h, copy=nc.vector.tensor_copy, tag=None):
+            rounded[n, h] = sbuf(f"rounded_{n}_{h}", (P, PAIR, P, PACK), BF16, tag)
+            by_column = raw[n][:].rearrange("p j (m t) -> p m j t", t=TILES)
+            copy(out=rounded[n, h][:].rearrange("p t m j -> p m j t"), in_=by_column[:, :, :, columns(h, PAIR)])
+
+        def round_whole(n, tag=None):
+            whole = sbuf(f"rounded_{n}", (P, TILES, P, PACK), BF16, tag)
+            nc.vector.tensor_copy(out=whole[:].rearrange("p t m j -> p m j t"), in_=raw[n][:].rearrange("p j (m t) -> p m j t", t=TILES))
+            for h in range(HALVES):
+                rounded[n, h] = whole[:, columns(h, PAIR)]
+
+        quant = {n: (sbuf(f"codes_{n}", (P, N), U32), sbuf(f"scales_{n}", (P, N), U8)) for n in weights}
+
+        def quantise(n, h):
+            codes, scales = quant[n]
+            cols = columns(h, PAIR * P)
             nc.vector.quantize_mx(
-                out=codes[:].bitcast(FP8X4), scales=scales[:], in_=rounded[name, h][:].rearrange("p t m j -> p (t m j)")
+                out=codes[:, cols].bitcast(FP8X4), scales=scales[:, cols], in_=rounded[n, h][:].rearrange("p t m j -> p (t m j)")
             )
-            return codes, scales
-
-        def bank(tag):
-            return psum.tile([P, S], F32, name=tag, tag=tag)
 
         def product(acc, stationary, moving, s_cols, m_cols=slice(0, S)):
             nc.tensor.matmul_mx(
@@ -146,133 +123,166 @@ def tile_picked_wkv8_none_p_kernel(
             return acc
 
         x = (x_codes, x_bytes)
-        nc.vector.tensor_copy(picked_bytes[:], scale_table[:].indirect(offs_sb[:]))
-        for r in range(PACK):
-            nc.scalar.dma_start(out=x_bytes[r:P:32, :].bitcast(I32), in_=picked_bytes[SCALE_STEP * r : P : 32, :].bitcast(I32))
-        nc.vector.tensor_copy(x_codes[:], word_table[:].bitcast(U32).indirect(offs_sb[:]))
-        round_half("w1", 1, nc.scalar.copy)
-        round_half("w1", 0, nc.vector.tensor_copy)
-        key_weights = {h: quantised("w1", h) for h in (0, 1)}
-        keys, ek = {}, {}
-        for t in (1, 0, 2, 3):
-            keys[t] = bank(f"product{t}")
-            product(keys[t][:], key_weights[t // PAIR], x, columns(t % PAIR, P))
+        picked, keys, ek, den_sum, num_sum, value, term = {}, {}, {}, {}, {}, {}, {}
+        root, inverse, sign, signed, gated, back = {}, {}, {}, {}, {}, {}
 
-        def exponentials(h, tag, order):
-            pair = keep.tile([P, PAIR, S], F32, name=f"ek{h}", tag=tag, align_bytes=64)
-            for t in order:
-                ek[t] = pair[:, t % PAIR]
-                nc.scalar.activation(ek[t], keys[t][:], ACT.Exp, scale=0.5)
-
-        exponentials(0, "ek_early", (1, 0))
-
-        picked_den = keep.tile([P, S], F32, name="picked_den", align_bytes=64)
-        nc.vector.tensor_copy(picked_den[:], dens[LAST][:].indirect(par_sb[:]))
-        round_half("w3", 0, nc.vector.tensor_copy)
-        round_part("w3", 1, 0, nc.scalar.copy)
-        round_part("w3", 1, 1, nc.vector.tensor_copy)
-        exponentials(1, "raw_w3_0", (2, 3))
-        def denominator(t, tag):
-            den_sum[t] = keep.tile([P, S], F32, name=f"den_sum{t}", tag=tag, align_bytes=64)
-            if t == LAST:
-                nc.gpsimd.tensor_tensor(den_sum[t][:], picked_den[:], ek[t], ALU.add)
+        def pick(n, t, engine, tag=None):
+            picked[n, t] = sbuf(f"picked_{n}{t}", tag=tag)
+            looked_up = window[n, t][:].indirect(par_sb[:])
+            if engine is nc.scalar:
+                nc.scalar.activation(picked[n, t][:], looked_up, ACT.Copy)
             else:
-                nc.vector.tensor_tensor(den_sum[t][:], dens[t][:].indirect(par_sb[:]), ek[t], ALU.add)
+                nc.vector.tensor_copy(picked[n, t][:], looked_up)
 
-        gate_weights = {0: quantised("w3", 0)}
-        gate_weights[1] = quantised("w3", 1)
-        denominator(1, "den_sum1")
-        for g in range(TILES):
-            h, half = divmod(g, HALVES)
-            acc = bank(f"product{(1, 0, 2, 3)[g]}")
-            for i in range(PAIR):
-                product(acc[:, columns(i, PAIR * P)], x, gate_weights[h], columns(PAIR * half + i, P), slice(0, PAIR * P))
-            bias = last_gate_bias[:] if g == TILES - 1 else 0.0
-            nc.scalar.activation(
-                th[:, columns(h, PAIR), columns(half, PAIR), :].rearrange("p t b m -> p b t m"),
-                acc[:].rearrange("p (b t m) -> p b t m", b=PAIR, t=PAIR),
-                ACT.Tanh,
-                bias=bias,
-                scale=0.5,
-            )
-
-        whole = keep.tile([P, TILES, P, PACK], BF16, name="rounded_w2", align_bytes=64)
-        nc.vector.tensor_copy(out=whole[:].rearrange("p t m j -> p m j t"), in_=raw["w2", 0][:].rearrange("p j (m t) -> p m j t", t=TILES))
-        for h in range(HALVES):
-            rounded["w2", h] = whole[:, columns(h, PAIR)]
-        value_weights = {h: quantised("w2", h) for h in (0, 1)}
-        roots = keep.tile([P, TILES * S], F32, name="roots", tag="roots", align_bytes=64)
-        num_sum, back = {}, {}
-        for t in range(TILES):
-            nc.vector.tensor_copy(picked_num[t][:], nums[t][:].indirect(par_sb[:]))
+        def open_numerator(t):
             num_sum[t] = bank(f"num{t}")
-            add_turned(num_sum[t], picked_num[t], True, False)
+            add_turned(num_sum[t], picked["num", t], True, False)
 
-        def take_sign(t):
-            sign[t] = keep.tile([P, S], F32, name=f"sign{t}", align_bytes=64)
+        def key(t):
+            keys[t] = bank(f"product{t}")
+            product(keys[t][:], quant["w1"], x, columns(t, P))
+
+        def exponential(t, tag=None):
+            ek[t] = sbuf(f"ek{t}", tag=tag)
+            nc.scalar.activation(ek[t][:], keys[t][:], ACT.Exp, scale=0.5)
+
+        def denominator(t, engine, tag=None):
+            den_sum[t] = sbuf(f"den_sum{t}", tag=tag)
+            looked_up = picked["den", t][:] if ("den", t) in picked else window["den", t][:].indirect(par_sb[:])
+            engine.tensor_tensor(den_sum[t][:], looked_up, ek[t][:], ALU.add)
+
+        def gate_values(b):
+            acc = bank(f"num{b}")
+            product(acc[:], x, quant["w3"], columns(b, P))
+            nc.scalar.activation(th[:, b].rearrange("p t m -> p (t m)"), acc[:], ACT.Tanh, scale=0.5)
+
+        def take_sign(t, tag=None):
+            sign[t] = sbuf(f"sign{t}", tag=tag)
             nc.scalar.activation(sign[t][:], den_sum[t][:], ACT.Sign)
 
-        def root(t):
-            nc.scalar.activation(roots[:, columns(t, S)], den_sum[t][:], ACT.Abs_reciprocal_sqrt, scale=2.0)
+        def half_sign(t, tag=None):
+            sign[t] = sbuf(f"sign{t}", tag=tag)
+            nc.vector.tensor_scalar(sign[t][:], den_sum[t][:], 0.0, 0.5, ALU.is_ge, ALU.subtract)
 
-        def square(t):
-            nc.scalar.activation(inverse[t][:], roots[:, columns(t, S)], ACT.Square)
+        def take_root(t, tag=None):
+            root[t] = sbuf(f"root{t}", tag=tag)
+            scale = 1.0 if t in HALF_SIGNED else root_scale[:]
+            nc.scalar.activation(root[t][:], den_sum[t][:], ACT.Abs_reciprocal_sqrt, scale=scale)
 
-        value = {}
+        def square(t, tag=None):
+            inverse[t] = sbuf(f"inverse{t}", tag=tag)
+            nc.scalar.activation(inverse[t][:], root[t][:], ACT.Square)
 
         def value_product(t):
             value[t] = bank(f"product{t}")
-            product(value[t][:], value_weights[t // PAIR], x, columns(t % PAIR, P))
+            product(value[t][:], quant["w2"], x, columns(t, P))
 
-        def value_term(t):
-            term[t] = keep.tile([P, S], F32, name=f"term{t}", tag=f"term{t}", align_bytes=64)
-            nc.vector.tensor_tensor(term[t][:], value[t][:], ek[t], ALU.mult)
+        def value_term(t, tag=None):
+            term[t] = sbuf(f"term{t}", tag=tag)
+            nc.vector.tensor_tensor(term[t][:], value[t][:], ek[t][:], ALU.mult)
             add_turned(num_sum[t], term[t], False, True)
 
-        def gate(t):
-            nc.vector.scalar_tensor_tensor(gated[t][:], th[:, t].rearrange("p b m -> p (b m)"), 1.0, num_sum[t][:], ALU.add, ALU.mult)
+        def gate(t, tag=None):
+            gated[t] = sbuf(f"gated{t}", tag=tag)
+            by_block = "p (b m) -> p b m"
+            nc.vector.scalar_tensor_tensor(
+                gated[t][:].rearrange(by_block, m=P), th[:, :, t, :], 1.0, num_sum[t][:].rearrange(by_block, m=P), ALU.add, ALU.mult
+            )
             back[t] = turned_back(f"num{t}", gated[t])
 
-        def divide(t):
-            result[t] = keep.tile([P, S], F32, name=f"result{t}", tag="den3" if t == 3 else f"result{t}", align_bytes=64)
-            if t == LAST:
-                factors = signed[t], inverse[t]
-            else:
-                signed[t] = keep.tile([P, S], F32, name=f"signed{t}", align_bytes=64)
-                nc.gpsimd.tensor_tensor(signed[t][:], inverse[t][:], sign[t][:], ALU.mult)
-                factors = back[t], signed[t]
-            parts = HALVES if t in (3, LAST) else 1
+        def sign_inverse(t, tag=None):
+            signed[t] = sbuf(f"signed{t}", tag=tag)
+            nc.gpsimd.tensor_tensor(signed[t][:], inverse[t][:], sign[t][:], ALU.mult)
+
+        def sign_numerator(t, tag=None):
+            signed[t] = sbuf(f"signed{t}", tag=tag)
+            nc.vector.tensor_tensor(signed[t][:], back[t][:], sign[t][:], ALU.mult)
+            back[t], signed[t] = signed[t], inverse[t]
+
+        def divide(t, parts=1, tag=None):
+            result = sbuf(f"result{t}", tag=tag)
             for h in range(parts):
                 cols = columns(h, S // parts)
-                nc.vector.tensor_tensor(result[t][:, cols], factors[0][:, cols], factors[1][:, cols], ALU.mult)
-                nc.sync.dma_start(out=by_tile(out)[t][:, cols], in_=result[t][:, cols])
+                nc.vector.tensor_tensor(result[:, cols], back[t][:, cols], signed[t][:, cols], ALU.mult)
+                nc.sync.dma_start(out=by_tile(out)[t][:, cols], in_=result[:, cols])
 
+        nc.gpsimd.memset(scale_table[:].bitcast(I32), 0)
+        nc.vector.memset(two[:], 2.0)
+        nc.scalar.copy(out=root_scale[:], in_=two[:])
+        make_identity(nc, ident[:])
+        nc.sync.dma_start(par_sb[:], par)
+        load_table("den", 0)
+        nc.sync.dma_start(offs_sb[:], offs)
+        load_weight("w1")
+        load_scales()
+        load_table("den", 1)
+        load_table("den", 2)
+        load_words()
+        load_table("den", 3)
+        load_table("num", 0)
+        load_weight("w3")
+        load_table("num", 1)
+        load_weight("w2")
+        load_table("num", 2)
+        load_table("num", 3)
+
+        nc.vector.tensor_copy(x_bytes[:], scale_table[:].indirect(offs_sb[:]))
+        for t in range(TILES):
+            pick("den", t, nc.scalar)
+        for h in range(HALVES):
+            round_half("w1", h)
+        for h in range(HALVES):
+            quantise("w1", h)
+        nc.vector.tensor_copy(x_codes[:], word_table[:].bitcast(U32).indirect(offs_sb[:]))
+        for t in range(TILES):
+            key(t)
+        pick("num", 0, nc.vector)
+        exponential(0, "den3")
+        for t in range(1, TILES):
+            exponential(t)
+        for h in range(HALVES):
+            round_half("w3", h)
+        for h in range(HALVES):
+            quantise("w3", h)
+        for g in range(TILES):
+            gate_values(g)
+        pick("num", 1, nc.scalar)
+        denominator(0, nc.vector, "rounded_w3_0")
+        half_sign(0)
+        for h in range(HALVES):
+            round_half("w2", h)
+        for h in range(HALVES):
+            quantise("w2", h)
+        denominator(1, nc.gpsimd, "rounded_w2_1")
+        denominator(2, nc.gpsimd, "picked_den1")
+        denominator(3, nc.gpsimd, "picked_den2")
         for t in range(TILES):
             value_product(t)
+        open_numerator(0)
+        open_numerator(1)
+        pick("num", 2, nc.vector, "rounded_w2_0")
+        open_numerator(2)
+        pick("num", 3, nc.vector)
+        open_numerator(3)
+        take_root(0, "codes_w3")
+        take_root(1)
+        square(0)
         take_sign(1)
-        denominator(2, "den_sum2")
-        root(1)
-        root(2)
         square(1)
+        take_root(2)
         take_sign(2)
         square(2)
-        value_term(0)
-        denominator(3, "den_sum3")
-        denominator(0, "den3")
-        for t in (3, 0):
-            root(t)
-            take_sign(t)
-            square(t)
-        value_term(1)
-        value_term(2)
-        gate(0)
-        value_term(3)
-        gate(1)
-        gate(2)
-        divide(1)
-        gate(3)
-        divide(2)
-        signed[LAST] = keep.tile([P, S], F32, name="signed_numerator", align_bytes=64)
-        nc.vector.tensor_tensor(signed[LAST][:], back[LAST][:], sign[LAST][:], ALU.mult)
-        divide(3)
+        take_sign(3)
+        take_root(3)
+        square(3)
+        for t in range(TILES):
+            value_term(t)
+        for t in (0, 1, 2):
+            sign_inverse(t)
+        for t in range(TILES):
+            gate(t)
         divide(0)
+        divide(1)
+        sign_numerator(3)
+        divide(2, 2, "picked_den2")
+        divide(3, 2)

@@ -211,24 +211,24 @@ def tile_picked_wkv8_none_p_kernel(
         nc.scalar.copy(out=root_scale[:], in_=two[:])
         make_identity(nc, ident[:])
         nc.sync.dma_start(par_sb[:], par)
-        load_table("den", 0)
+        load_table("num", 0)
         nc.sync.dma_start(offs_sb[:], offs)
         load_weight("w1")
         load_scales()
-        load_table("den", 1)
-        load_table("den", 2)
-        load_words()
-        load_table("den", 3)
-        load_table("num", 0)
-        load_weight("w3")
         load_table("num", 1)
-        load_weight("w2")
         load_table("num", 2)
+        load_words()
         load_table("num", 3)
+        load_table("den", 0)
+        load_weight("w3")
+        load_table("den", 1)
+        load_weight("w2")
+        load_table("den", 2)
+        load_table("den", 3)
 
         nc.vector.tensor_copy(x_bytes[:], scale_table[:].indirect(offs_sb[:]))
         for t in range(TILES):
-            pick("den", t, nc.scalar)
+            pick("num", t, nc.scalar)
         for h in range(HALVES):
             round_half("w1", h)
         for h in range(HALVES):
@@ -236,8 +236,8 @@ def tile_picked_wkv8_none_p_kernel(
         nc.vector.tensor_copy(x_codes[:], word_table[:].bitcast(U32).indirect(offs_sb[:]))
         for t in range(TILES):
             key(t)
-        pick("num", 0, nc.vector)
-        exponential(0, "den3")
+        pick("den", 0, nc.vector)
+        exponential(0, "num3")
         for t in range(1, TILES):
             exponential(t)
         for h in range(HALVES):
@@ -246,43 +246,39 @@ def tile_picked_wkv8_none_p_kernel(
             quantise("w3", h)
         for g in range(TILES):
             gate_values(g)
-        pick("num", 1, nc.scalar)
+        pick("den", 1, nc.scalar)
         denominator(0, nc.vector, "rounded_w3_0")
         half_sign(0)
         for h in range(HALVES):
             round_half("w2", h)
         for h in range(HALVES):
             quantise("w2", h)
-        denominator(1, nc.gpsimd, "rounded_w2_1")
-        denominator(2, nc.gpsimd, "picked_den1")
-        denominator(3, nc.gpsimd, "picked_den2")
         for t in range(TILES):
             value_product(t)
-        open_numerator(0)
-        open_numerator(1)
-        pick("num", 2, nc.vector, "rounded_w2_0")
-        open_numerator(2)
-        pick("num", 3, nc.vector)
-        open_numerator(3)
+        for t in range(TILES):
+            open_numerator(t)
+        denominator(2, nc.vector, "rounded_w2_0")
+        denominator(3, nc.vector)
+        denominator(1, nc.gpsimd, "den3")
         take_root(0, "codes_w3")
-        take_root(1)
-        square(0)
-        take_sign(1)
-        square(1)
         take_root(2)
+        square(0)
         take_sign(2)
         square(2)
-        take_sign(3)
         take_root(3)
+        take_sign(3)
         square(3)
-        for t in range(TILES):
+        take_sign(1)
+        take_root(1)
+        square(1)
+        for t in (0, 2, 3, 1):
             value_term(t)
-        for t in (0, 1, 2):
+        for t in (0, 2, 3):
             sign_inverse(t)
-        for t in range(TILES):
+        for t in (0, 2, 3, 1):
             gate(t)
         divide(0)
-        divide(1)
-        sign_numerator(3)
-        divide(2, 2, "picked_den2")
-        divide(3, 2)
+        divide(2)
+        sign_numerator(1)
+        divide(3, 2, "den3")
+        divide(1, 2)

@@ -152,7 +152,7 @@ def tile_picked_wkv8_none_p_kernel(
             engine.tensor_tensor(den_sum[t][:], looked_up, ek[t][:], ALU.add)
 
         def gate_values(b):
-            acc = bank(f"num{b}")
+            acc = bank(f"product{b}")
             product(acc[:], x, quant["w3"], columns(b, P))
             nc.scalar.activation(th[:, b].rearrange("p t m -> p (t m)"), acc[:], ACT.Tanh, scale=0.5)
 
@@ -236,6 +236,8 @@ def tile_picked_wkv8_none_p_kernel(
         nc.vector.tensor_copy(x_codes[:], word_table[:].bitcast(U32).indirect(offs_sb[:]))
         for t in range(TILES):
             key(t)
+        for t in range(TILES):
+            open_numerator(t)
         pick("den", 0, nc.vector)
         exponential(0, "num3")
         for t in range(1, TILES):
@@ -255,8 +257,6 @@ def tile_picked_wkv8_none_p_kernel(
             quantise("w2", h)
         for t in range(TILES):
             value_product(t)
-        for t in range(TILES):
-            open_numerator(t)
         denominator(2, nc.vector, "rounded_w2_0")
         denominator(3, nc.vector)
         denominator(1, nc.gpsimd, "den3")

@@ -24,7 +24,7 @@ LIST_ROWS = 16
 BLOCKS = S // P
 HALVES = 2
 PAIR = 2
-HALF_SIGNED = (0,)
+HALF_SIGNED = ()
 
 
 def tile_picked_wkv8_none_p_kernel(
@@ -57,7 +57,8 @@ def tile_picked_wkv8_none_p_kernel(
         root_scale = sbuf("root_scale", (P, 1))
         ident = sbuf("ident", (P, P))
         weights = {"w1": w1, "w2": w2, "w3": w3}
-        raw = {n: sbuf(f"raw_{n}", (P, PACK, N)) for n in weights}
+        raw = {n: sbuf(f"raw_{n}", (P, PACK, N)) for n in ("w1", "w2")}
+        paired = {("w3", u): sbuf(f"raw_w3_{u}", (P, PAIR, N)) for u in range(HALVES)}
         tables = {"den": den, "num": num}
         window = {(n, t): sbuf(f"{n}{t}", (P, 2 * S)) for n in tables for t in range(TILES)}
         th = sbuf("th", (P, BLOCKS, TILES, P))
@@ -67,6 +68,9 @@ def tile_picked_wkv8_none_p_kernel(
 
         def load_weight(n):
             nc.sync.dma_start(out=raw[n][:], in_=weights[n].rearrange("(p j) c -> p j c", j=PACK))
+
+        def load_weight_rows(n, u):
+            nc.sync.dma_start(out=paired[n, u][:], in_=weights[n].rearrange("(p j) c -> p j c", j=PACK)[:, columns(u, PAIR)])
 
         def load_words():
             nc.sync.dma_start(out=word_table[:], in_=x_words[0].rearrange("p n t -> p (n t)").bitcast(I32))
@@ -82,6 +86,14 @@ def tile_picked_wkv8_none_p_kernel(
             rounded[n, h] = sbuf(f"rounded_{n}_{h}", (P, PAIR, P, PACK), BF16, tag)
             by_column = raw[n][:].rearrange("p j (m t) -> p m j t", t=TILES)
             copy(out=rounded[n, h][:].rearrange("p t m j -> p m j t"), in_=by_column[:, :, :, columns(h, PAIR)])
+
+        def round_rows(n, u, h):
+            if u == 0:
+                rounded[n, h] = sbuf(f"rounded_{n}_{h}", (P, PAIR, P, PACK), BF16)
+            by_column = paired[n, u][:].rearrange("p j (m t) -> p m t j", t=TILES)
+            nc.vector.tensor_copy(
+                out=rounded[n, h][:, :, :, columns(u, PAIR)].rearrange("p t m j -> p m t j"), in_=by_column[:, :, columns(h, PAIR)]
+            )
 
         def round_whole(n, tag=None):
             whole = sbuf(f"rounded_{n}", (P, TILES, P, PACK), BF16, tag)
@@ -138,9 +150,16 @@ def tile_picked_wkv8_none_p_kernel(
             num_sum[t] = bank(f"num{t}")
             add_turned(num_sum[t], picked["num", t], True, False)
 
-        def key(t):
+        def pick_words(parts):
+            for h in range(parts):
+                entries = offs_sb[:, columns(h, S // LIST_ROWS // parts)]
+                nc.vector.tensor_copy(x_codes[:, columns(h, S // parts)], word_table[:].bitcast(U32).indirect(entries))
+
+        def key(t, parts=1):
             keys[t] = bank(f"product{t}")
-            product(keys[t][:], quant["w1"], x, columns(t, P))
+            for h in range(parts):
+                cols = columns(h, S // parts)
+                product(keys[t][:, cols], quant["w1"], x, columns(t, P), cols)
 
         def exponential(t, tag=None):
             ek[t] = sbuf(f"ek{t}", tag=tag)
@@ -164,14 +183,18 @@ def tile_picked_wkv8_none_p_kernel(
             sign[t] = sbuf(f"sign{t}", tag=tag)
             nc.vector.tensor_scalar(sign[t][:], den_sum[t][:], 0.0, 0.5, ALU.is_ge, ALU.subtract)
 
-        def take_root(t, tag=None):
+        def take_root(t, tag=None, parts=1):
             root[t] = sbuf(f"root{t}", tag=tag)
             scale = 1.0 if t in HALF_SIGNED else root_scale[:]
-            nc.scalar.activation(root[t][:], den_sum[t][:], ACT.Abs_reciprocal_sqrt, scale=scale)
+            for h in range(parts):
+                cols = columns(h, S // parts)
+                nc.scalar.activation(root[t][:, cols], den_sum[t][:, cols], ACT.Abs_reciprocal_sqrt, scale=scale)
 
-        def square(t, tag=None):
+        def square(t, tag=None, parts=1):
             inverse[t] = sbuf(f"inverse{t}", tag=tag)
-            nc.scalar.activation(inverse[t][:], root[t][:], ACT.Square)
+            for h in range(parts):
+                cols = columns(h, S // parts)
+                nc.scalar.activation(inverse[t][:, cols], root[t][:, cols], ACT.Square)
 
         def value_product(t):
             value[t] = bank(f"product{t}")
@@ -190,9 +213,11 @@ def tile_picked_wkv8_none_p_kernel(
             )
             back[t] = turned_back(f"num{t}", gated[t])
 
-        def sign_inverse(t, tag=None):
+        def sign_inverse(t, tag=None, parts=1):
             signed[t] = sbuf(f"signed{t}", tag=tag)
-            nc.gpsimd.tensor_tensor(signed[t][:], inverse[t][:], sign[t][:], ALU.mult)
+            for h in range(parts):
+                cols = columns(h, S // parts)
+                nc.gpsimd.tensor_tensor(signed[t][:, cols], inverse[t][:, cols], sign[t][:, cols], ALU.mult)
 
         def sign_numerator(t, tag=None):
             signed[t] = sbuf(f"signed{t}", tag=tag)
@@ -220,10 +245,11 @@ def tile_picked_wkv8_none_p_kernel(
         load_words()
         load_table("num", 3)
         load_table("den", 0)
-        load_weight("w3")
+        for u in range(HALVES):
+            load_weight_rows("w3", u)
         load_table("den", 1)
-        load_weight("w2")
         load_table("den", 2)
+        load_weight("w2")
         load_table("den", 3)
 
         nc.vector.tensor_copy(x_bytes[:], scale_table[:].indirect(offs_sb[:]))
@@ -233,8 +259,9 @@ def tile_picked_wkv8_none_p_kernel(
             round_half("w1", h)
         for h in range(HALVES):
             quantise("w1", h)
-        nc.vector.tensor_copy(x_codes[:], word_table[:].bitcast(U32).indirect(offs_sb[:]))
-        for t in range(TILES):
+        pick_words(HALVES)
+        key(0, HALVES)
+        for t in range(1, TILES):
             key(t)
         for t in range(TILES):
             open_numerator(t)
@@ -242,26 +269,27 @@ def tile_picked_wkv8_none_p_kernel(
         exponential(0, "num3")
         for t in range(1, TILES):
             exponential(t)
-        for h in range(HALVES):
-            round_half("w3", h)
+        for u in range(HALVES):
+            for h in range(HALVES):
+                round_rows("w3", u, h)
         for h in range(HALVES):
             quantise("w3", h)
         for g in range(TILES):
             gate_values(g)
         pick("den", 1, nc.scalar)
         denominator(0, nc.vector, "rounded_w3_0")
-        half_sign(0)
+        denominator(2, nc.vector, "rounded_w3_1")
         for h in range(HALVES):
             round_half("w2", h)
         for h in range(HALVES):
             quantise("w2", h)
         for t in range(TILES):
             value_product(t)
-        denominator(2, nc.vector, "rounded_w2_0")
-        denominator(3, nc.vector)
+        denominator(3, nc.vector, "rounded_w2_0")
         denominator(1, nc.gpsimd, "den3")
         take_root(0, "codes_w3")
-        take_root(2)
+        take_root(2, "scales_w3")
+        take_sign(0)
         square(0)
         take_sign(2)
         square(2)
@@ -269,12 +297,13 @@ def tile_picked_wkv8_none_p_kernel(
         take_sign(3)
         square(3)
         take_sign(1)
-        take_root(1)
-        square(1)
+        take_root(1, parts=HALVES)
+        square(1, parts=HALVES)
         for t in (0, 2, 3, 1):
             value_term(t)
-        for t in (0, 2, 3):
+        for t in (0, 2):
             sign_inverse(t)
+        sign_inverse(3, parts=HALVES)
         for t in (0, 2, 3, 1):
             gate(t)
         divide(0)

@@ -24,6 +24,7 @@ LIST_ROWS = 16
 BLOCKS = S // P
 HALVES = 2
 PAIR = 2
+SCALE_STEP = 8
 HALF_SIGNED = ()
 
 
@@ -53,12 +54,12 @@ def tile_picked_wkv8_none_p_kernel(
         scale_table = sbuf("scale_table", (P, T), U8)
         x_codes = sbuf("x_codes", dtype=U32)
         x_bytes = sbuf("x_bytes", dtype=U8)
+        picked_bytes = sbuf("picked_bytes", dtype=U8)
         two = sbuf("two", (P, 1))
         root_scale = sbuf("root_scale", (P, 1))
         ident = sbuf("ident", (P, P))
         weights = {"w1": w1, "w2": w2, "w3": w3}
-        raw = {n: sbuf(f"raw_{n}", (P, PACK, N)) for n in ("w1", "w2")}
-        paired = {("w3", u): sbuf(f"raw_w3_{u}", (P, PAIR, N)) for u in range(HALVES)}
+        raw = {n: sbuf(f"raw_{n}", (P, PACK, N)) for n in weights}
         tables = {"den": den, "num": num}
         window = {(n, t): sbuf(f"{n}{t}", (P, 2 * S)) for n in tables for t in range(TILES)}
         th = sbuf("th", (P, BLOCKS, TILES, P))
@@ -69,16 +70,17 @@ def tile_picked_wkv8_none_p_kernel(
         def load_weight(n):
             nc.sync.dma_start(out=raw[n][:], in_=weights[n].rearrange("(p j) c -> p j c", j=PACK))
 
-        def load_weight_rows(n, u):
-            nc.sync.dma_start(out=paired[n, u][:], in_=weights[n].rearrange("(p j) c -> p j c", j=PACK)[:, columns(u, PAIR)])
-
         def load_words():
             nc.sync.dma_start(out=word_table[:], in_=x_words[0].rearrange("p n t -> p (n t)").bitcast(I32))
 
         def load_scales():
-            for q in range(P // QUADRANT):
-                rows = slice(QUADRANT * q, QUADRANT * q + PACK)
-                nc.scalar.dma_start(out=scale_table[rows, :].bitcast(I32), in_=x_scales[0][columns(q, PACK), :].bitcast(I32))
+            nc.sync.dma_start(out=scale_table[0:P:SCALE_STEP, :].bitcast(I32), in_=x_scales[0].bitcast(I32))
+
+        def place_scales():
+            for r in range(PACK):
+                nc.scalar.dma_start(
+                    out=x_bytes[r:P:QUADRANT, :].bitcast(I32), in_=picked_bytes[SCALE_STEP * r : P : QUADRANT, :].bitcast(I32)
+                )
 
         rounded = {}
 
@@ -87,13 +89,12 @@ def tile_picked_wkv8_none_p_kernel(
             by_column = raw[n][:].rearrange("p j (m t) -> p m j t", t=TILES)
             copy(out=rounded[n, h][:].rearrange("p t m j -> p m j t"), in_=by_column[:, :, :, columns(h, PAIR)])
 
-        def round_rows(n, u, h):
-            if u == 0:
-                rounded[n, h] = sbuf(f"rounded_{n}_{h}", (P, PAIR, P, PACK), BF16)
-            by_column = paired[n, u][:].rearrange("p j (m t) -> p m t j", t=TILES)
-            nc.vector.tensor_copy(
-                out=rounded[n, h][:, :, :, columns(u, PAIR)].rearrange("p t m j -> p m t j"), in_=by_column[:, :, columns(h, PAIR)]
-            )
+        def round_quarters(n, h):
+            rounded[n, h] = sbuf(f"rounded_{n}_{h}", (P, PAIR, P, PACK), BF16)
+            by_column = raw[n][:].rearrange("p j (m t) -> p m j t", t=TILES)
+            for part, copy in enumerate((nc.scalar.copy, nc.vector.tensor_copy)):
+                rows = columns(part, P // HALVES)
+                copy(out=rounded[n, h][:, :, rows].rearrange("p t m j -> p m j t"), in_=by_column[:, rows, :, columns(h, PAIR)])
 
         def round_whole(n, tag=None):
             whole = sbuf(f"rounded_{n}", (P, TILES, P, PACK), BF16, tag)
@@ -234,26 +235,28 @@ def tile_picked_wkv8_none_p_kernel(
         nc.gpsimd.memset(scale_table[:].bitcast(I32), 0)
         nc.vector.memset(two[:], 2.0)
         nc.scalar.copy(out=root_scale[:], in_=two[:])
+        nc.vector.memset(x_bytes[:].bitcast(I32), 0)
         make_identity(nc, ident[:])
         nc.sync.dma_start(par_sb[:], par)
         load_table("num", 0)
         nc.sync.dma_start(offs_sb[:], offs)
-        load_weight("w1")
         load_scales()
         load_table("num", 1)
+        load_weight("w1")
         load_table("num", 2)
         load_words()
         load_table("num", 3)
         load_table("den", 0)
-        for u in range(HALVES):
-            load_weight_rows("w3", u)
         load_table("den", 1)
+        load_weight("w3")
         load_table("den", 2)
         load_weight("w2")
         load_table("den", 3)
 
-        nc.vector.tensor_copy(x_bytes[:], scale_table[:].indirect(offs_sb[:]))
-        for t in range(TILES):
+        nc.vector.tensor_copy(picked_bytes[:], scale_table[:].indirect(offs_sb[:]))
+        pick("num", 0, nc.scalar)
+        place_scales()
+        for t in range(1, TILES):
             pick("num", t, nc.scalar)
         for h in range(HALVES):
             round_half("w1", h)
@@ -266,19 +269,20 @@ def tile_picked_wkv8_none_p_kernel(
         for t in range(TILES):
             open_numerator(t)
         pick("den", 0, nc.vector)
+        pick("den", 1, nc.vector)
         exponential(0, "num3")
-        for t in range(1, TILES):
-            exponential(t)
-        for u in range(HALVES):
-            for h in range(HALVES):
-                round_rows("w3", u, h)
+        exponential(1)
+        exponential(2)
+        denominator(0, nc.vector)
+        round_half("w3", 0)
+        round_quarters("w3", 1)
+        exponential(3, "raw_w3")
         for h in range(HALVES):
             quantise("w3", h)
+        take_sign(0, "rounded_w3_1")
         for g in range(TILES):
             gate_values(g)
-        pick("den", 1, nc.scalar)
-        denominator(0, nc.vector, "rounded_w3_0")
-        denominator(2, nc.vector, "rounded_w3_1")
+        denominator(2, nc.vector, "rounded_w3_0")
         for h in range(HALVES):
             round_half("w2", h)
         for h in range(HALVES):
@@ -289,7 +293,6 @@ def tile_picked_wkv8_none_p_kernel(
         denominator(1, nc.gpsimd, "den3")
         take_root(0, "codes_w3")
         take_root(2, "scales_w3")
-        take_sign(0)
         square(0)
         take_sign(2)
         square(2)

@@ -62,7 +62,7 @@ def tile_picked_wkv8_none_p_kernel(
         raw = {n: sbuf(f"raw_{n}", (P, PACK, N)) for n in weights}
         tables = {"den": den, "num": num}
         window = {(n, t): sbuf(f"{n}{t}", (P, 2 * S)) for n in tables for t in range(TILES)}
-        th = sbuf("th", (P, BLOCKS, TILES, P))
+        th = sbuf("th", (P, TILES, PAIR, PAIR, P))
 
         def load_table(n, t):
             nc.sync.dma_start(out=window[n, t][:, :S], in_=by_tile(tables[n])[t])
@@ -139,8 +139,8 @@ def tile_picked_wkv8_none_p_kernel(
         picked, keys, ek, den_sum, num_sum, value, term = {}, {}, {}, {}, {}, {}, {}
         root, inverse, sign, signed, gated, back = {}, {}, {}, {}, {}, {}
 
-        def pick(n, t, engine, tag=None):
-            picked[n, t] = sbuf(f"picked_{n}{t}", tag=tag)
+        def pick(n, t, engine, tag=None, into=None):
+            picked[n, t] = sbuf(f"picked_{n}{t}", tag=tag) if into is None else into
             looked_up = window[n, t][:].indirect(par_sb[:])
             if engine is nc.scalar:
                 nc.scalar.activation(picked[n, t][:], looked_up, ACT.Copy)
@@ -171,13 +171,15 @@ def tile_picked_wkv8_none_p_kernel(
             looked_up = picked["den", t][:] if ("den", t) in picked else window["den", t][:].indirect(par_sb[:])
             engine.tensor_tensor(den_sum[t][:], looked_up, ek[t][:], ALU.add)
 
-        def gate_values(b):
-            acc = bank(f"product{b}")
-            product(acc[:], x, quant["w3"], columns(b, P))
-            nc.scalar.activation(th[:, b].rearrange("p t m -> p (t m)"), acc[:], ACT.Tanh, scale=0.5)
+        def gate_values(g):
+            h, half = divmod(g, HALVES)
+            acc = bank(f"product{g}")
+            for i in range(PAIR):
+                product(acc[:, columns(i, PAIR * P)], x, quant["w3"], columns(PAIR * half + i, P), columns(h, PAIR * P))
+            nc.scalar.activation(th[:, g].rearrange("p b t m -> p (b t m)"), acc[:], ACT.Tanh, scale=0.5)
 
-        def take_sign(t, tag=None):
-            sign[t] = sbuf(f"sign{t}", tag=tag)
+        def take_sign(t, into=None):
+            sign[t] = sbuf(f"sign{t}") if into is None else into
             nc.scalar.activation(sign[t][:], den_sum[t][:], ACT.Sign)
 
         def half_sign(t, tag=None):
@@ -209,8 +211,9 @@ def tile_picked_wkv8_none_p_kernel(
         def gate(t, tag=None):
             gated[t] = sbuf(f"gated{t}", tag=tag)
             by_block = "p (b m) -> p b m"
+            gates = th[:, columns(t // PAIR, HALVES)].rearrange("p g b t m -> p (g b) t m")[:, :, t % PAIR, :]
             nc.vector.scalar_tensor_tensor(
-                gated[t][:].rearrange(by_block, m=P), th[:, :, t, :], 1.0, num_sum[t][:].rearrange(by_block, m=P), ALU.add, ALU.mult
+                gated[t][:].rearrange(by_block, m=P), gates, 1.0, num_sum[t][:].rearrange(by_block, m=P), ALU.add, ALU.mult
             )
             back[t] = turned_back(f"num{t}", gated[t])
 
@@ -225,12 +228,13 @@ def tile_picked_wkv8_none_p_kernel(
             nc.vector.tensor_tensor(signed[t][:], back[t][:], sign[t][:], ALU.mult)
             back[t], signed[t] = signed[t], inverse[t]
 
-        def divide(t, parts=1, tag=None):
-            result = sbuf(f"result{t}", tag=tag)
-            for h in range(parts):
-                cols = columns(h, S // parts)
-                nc.vector.tensor_tensor(result[:, cols], back[t][:, cols], signed[t][:, cols], ALU.mult)
-                nc.sync.dma_start(out=by_tile(out)[t][:, cols], in_=result[:, cols])
+        result = {}
+
+        def divide(t, cols=slice(0, S), tag=None):
+            if t not in result:
+                result[t] = sbuf(f"result{t}", tag=tag)
+            nc.vector.tensor_tensor(result[t][:, cols], back[t][:, cols], signed[t][:, cols], ALU.mult)
+            nc.sync.dma_start(out=by_tile(out)[t][:, cols], in_=result[t][:, cols])
 
         nc.gpsimd.memset(scale_table[:].bitcast(I32), 0)
         nc.vector.memset(two[:], 2.0)
@@ -270,7 +274,7 @@ def tile_picked_wkv8_none_p_kernel(
             open_numerator(t)
         pick("den", 0, nc.vector)
         pick("den", 1, nc.vector)
-        exponential(0, "num3")
+        exponential(0)
         exponential(1)
         exponential(2)
         denominator(0, nc.vector)
@@ -279,38 +283,42 @@ def tile_picked_wkv8_none_p_kernel(
         exponential(3, "raw_w3")
         for h in range(HALVES):
             quantise("w3", h)
-        take_sign(0, "rounded_w3_1")
+        behind_w3 = sbuf("behind_w3", (P, PAIR, S), tag="rounded_w3_0")
+        take_sign(0, behind_w3[:, 0])
         for g in range(TILES):
             gate_values(g)
-        denominator(2, nc.vector, "rounded_w3_0")
+        pick("den", 2, nc.vector, into=behind_w3[:, 1])
+        denominator(1, nc.gpsimd, "rounded_w3_1")
         for h in range(HALVES):
             round_half("w2", h)
         for h in range(HALVES):
             quantise("w2", h)
         for t in range(TILES):
             value_product(t)
-        denominator(3, nc.vector, "rounded_w2_0")
-        denominator(1, nc.gpsimd, "den3")
+        pick("den", 3, nc.vector, "rounded_w2_0")
+        denominator(2, nc.gpsimd, "rounded_w2_1")
+        denominator(3, nc.gpsimd)
         take_root(0, "codes_w3")
-        take_root(2, "scales_w3")
+        take_root(1, "scales_w3")
         square(0)
+        take_sign(1)
+        square(1)
+        take_root(2)
         take_sign(2)
         square(2)
-        take_root(3)
         take_sign(3)
-        square(3)
-        take_sign(1)
-        take_root(1, parts=HALVES)
-        square(1, parts=HALVES)
-        for t in (0, 2, 3, 1):
+        take_root(3, parts=HALVES)
+        square(3, parts=HALVES)
+        for t in range(TILES):
             value_term(t)
-        for t in (0, 2):
+        for t in (0, 1):
             sign_inverse(t)
-        sign_inverse(3, parts=HALVES)
-        for t in (0, 2, 3, 1):
+        sign_inverse(2, parts=HALVES)
+        for t in range(TILES):
             gate(t)
         divide(0)
-        divide(2)
-        sign_numerator(1)
-        divide(3, 2, "den3")
-        divide(1, 2)
+        divide(1)
+        sign_numerator(3)
+        for h in range(HALVES):
+            divide(2, columns(h, S // HALVES), "den_sum3")
+            divide(3, columns(h, S // HALVES))

@@ -24,6 +24,7 @@ LIST_ROWS = 16
 BLOCKS = S // P
 HALVES = 2
 PAIR = 2
+TERM_ORDER = (0, 1, 3, 2)
 SCALE_STEP = 8
 HALF_SIGNED = ()
 
@@ -77,8 +78,9 @@ def tile_picked_wkv8_none_p_kernel(
             nc.sync.dma_start(out=scale_table[0:P:SCALE_STEP, :].bitcast(I32), in_=x_scales[0].bitcast(I32))
 
         def place_scales():
-            for r in range(PACK):
-                nc.scalar.dma_start(
+            nc.vector.tensor_copy(x_bytes[:].bitcast(I32), picked_bytes[:].bitcast(I32))
+            for r in range(1, PACK):
+                nc.sync.dma_start(
                     out=x_bytes[r:P:QUADRANT, :].bitcast(I32), in_=picked_bytes[SCALE_STEP * r : P : QUADRANT, :].bitcast(I32)
                 )
 
@@ -157,7 +159,7 @@ def tile_picked_wkv8_none_p_kernel(
                 nc.vector.tensor_copy(x_codes[:, columns(h, S // parts)], word_table[:].bitcast(U32).indirect(entries))
 
         def key(t, parts=1):
-            keys[t] = bank(f"product{t}")
+            keys[t] = bank(f"num{TILES - 1}" if t == 0 else f"product{t}")
             for h in range(parts):
                 cols = columns(h, S // parts)
                 product(keys[t][:, cols], quant["w1"], x, columns(t, P), cols)
@@ -239,7 +241,6 @@ def tile_picked_wkv8_none_p_kernel(
         nc.gpsimd.memset(scale_table[:].bitcast(I32), 0)
         nc.vector.memset(two[:], 2.0)
         nc.scalar.copy(out=root_scale[:], in_=two[:])
-        nc.vector.memset(x_bytes[:].bitcast(I32), 0)
         make_identity(nc, ident[:])
         nc.sync.dma_start(par_sb[:], par)
         load_table("num", 0)
@@ -250,6 +251,8 @@ def tile_picked_wkv8_none_p_kernel(
         load_table("num", 2)
         load_words()
         load_table("num", 3)
+        nc.vector.tensor_copy(picked_bytes[:], scale_table[:].indirect(offs_sb[:]))
+        place_scales()
         load_table("den", 0)
         load_table("den", 1)
         load_weight("w3")
@@ -257,9 +260,7 @@ def tile_picked_wkv8_none_p_kernel(
         load_weight("w2")
         load_table("den", 3)
 
-        nc.vector.tensor_copy(picked_bytes[:], scale_table[:].indirect(offs_sb[:]))
         pick("num", 0, nc.scalar)
-        place_scales()
         for t in range(1, TILES):
             pick("num", t, nc.scalar)
         for h in range(HALVES):
@@ -270,11 +271,12 @@ def tile_picked_wkv8_none_p_kernel(
         key(0, HALVES)
         for t in range(1, TILES):
             key(t)
-        for t in range(TILES):
+        for t in range(TILES - 1):
             open_numerator(t)
         pick("den", 0, nc.vector)
         pick("den", 1, nc.vector)
         exponential(0)
+        open_numerator(TILES - 1)
         exponential(1)
         exponential(2)
         denominator(0, nc.vector)
@@ -293,7 +295,7 @@ def tile_picked_wkv8_none_p_kernel(
             round_half("w2", h)
         for h in range(HALVES):
             quantise("w2", h)
-        for t in range(TILES):
+        for t in TERM_ORDER:
             value_product(t)
         pick("den", 3, nc.vector, "rounded_w2_0")
         denominator(2, nc.gpsimd, "rounded_w2_1")
@@ -309,12 +311,12 @@ def tile_picked_wkv8_none_p_kernel(
         take_sign(3)
         take_root(3, parts=HALVES)
         square(3, parts=HALVES)
-        for t in range(TILES):
+        for t in TERM_ORDER:
             value_term(t)
         for t in (0, 1):
             sign_inverse(t)
         sign_inverse(2, parts=HALVES)
-        for t in range(TILES):
+        for t in TERM_ORDER:
             gate(t)
         divide(0)
         divide(1)

@@ -24,6 +24,7 @@ LIST_ROWS = 16
 BLOCKS = S // P
 HALVES = 2
 PAIR = 2
+LINE = 4
 TERM_ORDER = (0, 1, 3, 2)
 SCALE_STEP = 8
 HALF_SIGNED = ()
@@ -63,7 +64,7 @@ def tile_picked_wkv8_none_p_kernel(
         raw = {n: sbuf(f"raw_{n}", (P, PACK, N)) for n in weights}
         tables = {"den": den, "num": num}
         window = {(n, t): sbuf(f"{n}{t}", (P, 2 * S)) for n in tables for t in range(TILES)}
-        th = sbuf("th", (P, TILES, PAIR, PAIR, P))
+        th = sbuf("th", (P, BLOCKS, TILES, P))
 
         def load_table(n, t):
             nc.sync.dma_start(out=window[n, t][:, :S], in_=by_tile(tables[n])[t])
@@ -91,12 +92,14 @@ def tile_picked_wkv8_none_p_kernel(
             by_column = raw[n][:].rearrange("p j (m t) -> p m j t", t=TILES)
             copy(out=rounded[n, h][:].rearrange("p t m j -> p m j t"), in_=by_column[:, :, :, columns(h, PAIR)])
 
-        def round_quarters(n, h):
+        def round_in_order(n, h, copies):
             rounded[n, h] = sbuf(f"rounded_{n}_{h}", (P, PAIR, P, PACK), BF16)
-            by_column = raw[n][:].rearrange("p j (m t) -> p m j t", t=TILES)
-            for part, copy in enumerate((nc.scalar.copy, nc.vector.tensor_copy)):
-                rows = columns(part, P // HALVES)
-                copy(out=rounded[n, h][:, :, rows].rearrange("p t m j -> p m j t"), in_=by_column[:, rows, :, columns(h, PAIR)])
+            width = N // HALVES // len(copies)
+            for part, copy in enumerate(copies):
+                copy(
+                    out=rounded[n, h][:].rearrange("p a c j -> p (a c) j")[:, columns(part, width)].rearrange("p (c i) j -> p c j i", i=LINE),
+                    in_=raw[n][:, :, columns(h * len(copies) + part, width)].rearrange("p j (c i) -> p c j i", i=LINE),
+                )
 
         def round_whole(n, tag=None):
             whole = sbuf(f"rounded_{n}", (P, TILES, P, PACK), BF16, tag)
@@ -178,7 +181,12 @@ def tile_picked_wkv8_none_p_kernel(
             acc = bank(f"product{g}")
             for i in range(PAIR):
                 product(acc[:, columns(i, PAIR * P)], x, quant["w3"], columns(PAIR * half + i, P), columns(h, PAIR * P))
-            nc.scalar.activation(th[:, g].rearrange("p b t m -> p (b t m)"), acc[:], ACT.Tanh, scale=0.5)
+            nc.scalar.activation(
+                th[:, columns(half, PAIR), :, columns(h, P // HALVES)],
+                acc[:].rearrange("p (b m t) -> p b t m", b=PAIR, t=TILES),
+                ACT.Tanh,
+                scale=0.5,
+            )
 
         def take_sign(t, into=None):
             sign[t] = sbuf(f"sign{t}") if into is None else into
@@ -213,7 +221,7 @@ def tile_picked_wkv8_none_p_kernel(
         def gate(t, tag=None):
             gated[t] = sbuf(f"gated{t}", tag=tag)
             by_block = "p (b m) -> p b m"
-            gates = th[:, columns(t // PAIR, HALVES)].rearrange("p g b t m -> p (g b) t m")[:, :, t % PAIR, :]
+            gates = th[:, :, t, :]
             nc.vector.scalar_tensor_tensor(
                 gated[t][:].rearrange(by_block, m=P), gates, 1.0, num_sum[t][:].rearrange(by_block, m=P), ALU.add, ALU.mult
             )
@@ -280,8 +288,8 @@ def tile_picked_wkv8_none_p_kernel(
         exponential(1)
         exponential(2)
         denominator(0, nc.vector)
-        round_half("w3", 0)
-        round_quarters("w3", 1)
+        round_in_order("w3", 0, (nc.vector.tensor_copy,))
+        round_in_order("w3", 1, (nc.scalar.copy, nc.vector.tensor_copy))
         exponential(3, "raw_w3")
         for h in range(HALVES):
             quantise("w3", h)

@@ -88,32 +88,24 @@ def tile_picked_wkv8_none_p_kernel(
         rounded = {}
 
         def round_half(n, h, copy=nc.vector.tensor_copy, tag=None):
-            rounded[n, h] = sbuf(f"rounded_{n}_{h}", (P, PAIR, P, PACK), BF16, tag)
+            rounded[n, h] = sbuf(f"rounded_{n}_{h}", (P, PAIR * P, PACK), BF16, tag)
             by_column = raw[n][:].rearrange("p j (m t) -> p m j t", t=TILES)
-            copy(out=rounded[n, h][:].rearrange("p t m j -> p m j t"), in_=by_column[:, :, :, columns(h, PAIR)])
+            copy(out=rounded[n, h][:].rearrange("p (t m) j -> p m j t", t=PAIR), in_=by_column[:, :, :, columns(h, PAIR)])
 
-        def round_in_order(n, h, copies):
-            rounded[n, h] = sbuf(f"rounded_{n}_{h}", (P, PAIR, P, PACK), BF16)
-            width = N // HALVES // len(copies)
-            for part, copy in enumerate(copies):
-                copy(
-                    out=rounded[n, h][:].rearrange("p a c j -> p (a c) j")[:, columns(part, width)].rearrange("p (c i) j -> p c j i", i=LINE),
-                    in_=raw[n][:, :, columns(h * len(copies) + part, width)].rearrange("p j (c i) -> p c j i", i=LINE),
-                )
-
-        def round_whole(n, tag=None):
-            whole = sbuf(f"rounded_{n}", (P, TILES, P, PACK), BF16, tag)
-            nc.vector.tensor_copy(out=whole[:].rearrange("p t m j -> p m j t"), in_=raw[n][:].rearrange("p j (m t) -> p m j t", t=TILES))
-            for h in range(HALVES):
-                rounded[n, h] = whole[:, columns(h, PAIR)]
+        def round_in_order(g, copy):
+            rounded["w3", g] = sbuf(f"rounded_w3_{g}", (P, P, PACK), BF16)
+            copy(
+                out=rounded["w3", g][:].rearrange("p (c i) j -> p c j i", i=LINE),
+                in_=raw["w3"][:, :, columns(g, P)].rearrange("p j (c i) -> p c j i", i=LINE),
+            )
 
         quant = {n: (sbuf(f"codes_{n}", (P, N), U32), sbuf(f"scales_{n}", (P, N), U8)) for n in weights}
 
         def quantise(n, h):
             codes, scales = quant[n]
-            cols = columns(h, PAIR * P)
+            cols = columns(h, rounded[n, h].shape[1])
             nc.vector.quantize_mx(
-                out=codes[:, cols].bitcast(FP8X4), scales=scales[:, cols], in_=rounded[n, h][:].rearrange("p t m j -> p (t m j)")
+                out=codes[:, cols].bitcast(FP8X4), scales=scales[:, cols], in_=rounded[n, h][:].rearrange("p c j -> p (c j)")
             )
 
         def product(acc, stationary, moving, s_cols, m_cols=slice(0, S)):
@@ -177,15 +169,11 @@ def tile_picked_wkv8_none_p_kernel(
             engine.tensor_tensor(den_sum[t][:], looked_up, ek[t][:], ALU.add)
 
         def gate_values(g):
-            h, half = divmod(g, HALVES)
             acc = bank(f"product{g}")
-            for i in range(PAIR):
-                product(acc[:, columns(i, PAIR * P)], x, quant["w3"], columns(PAIR * half + i, P), columns(h, PAIR * P))
+            for b in range(BLOCKS):
+                product(acc[:, columns(b, P)], x, quant["w3"], columns(b, P), columns(g, P))
             nc.scalar.activation(
-                th[:, columns(half, PAIR), :, columns(h, P // HALVES)],
-                acc[:].rearrange("p (b m t) -> p b t m", b=PAIR, t=TILES),
-                ACT.Tanh,
-                scale=0.5,
+                th[:, :, :, columns(g, P // TILES)], acc[:].rearrange("p (b m t) -> p b t m", b=BLOCKS, t=TILES), ACT.Tanh, scale=0.5
             )
 
         def take_sign(t, into=None):
@@ -288,17 +276,19 @@ def tile_picked_wkv8_none_p_kernel(
         exponential(1)
         exponential(2)
         denominator(0, nc.vector)
-        round_in_order("w3", 0, (nc.vector.tensor_copy,))
-        round_in_order("w3", 1, (nc.scalar.copy, nc.vector.tensor_copy))
+        round_in_order(0, nc.vector.tensor_copy)
+        round_in_order(1, nc.vector.tensor_copy)
+        round_in_order(2, nc.scalar.copy)
+        quantise("w3", 0)
+        round_in_order(3, nc.vector.tensor_copy)
         exponential(3, "raw_w3")
-        for h in range(HALVES):
-            quantise("w3", h)
-        behind_w3 = sbuf("behind_w3", (P, PAIR, S), tag="rounded_w3_0")
-        take_sign(0, behind_w3[:, 0])
+        for g in range(1, TILES):
+            quantise("w3", g)
+        take_sign(0, sbuf("sign0", tag="rounded_w3_0"))
         for g in range(TILES):
             gate_values(g)
-        pick("den", 2, nc.vector, into=behind_w3[:, 1])
-        denominator(1, nc.gpsimd, "rounded_w3_1")
+        pick("den", 2, nc.vector, "rounded_w3_1")
+        denominator(1, nc.gpsimd, "rounded_w3_3")
         for h in range(HALVES):
             round_half("w2", h)
         for h in range(HALVES):

from contextlib import ExitStack

import concourse.mybir as mybir
from concourse.masks import make_identity

K, T, S, N = 512, 2048, 512, 512
FLOPS = 3 * 2 * K * N * S

F32 = mybir.dt.float32
BF16 = mybir.dt.bfloat16
I32 = mybir.dt.int32
U32 = mybir.dt.uint32
U16 = mybir.dt.uint16
U8 = mybir.dt.uint8
FP8X4 = mybir.dt.float8_e4m3fn_x4
ACT = mybir.ActivationFunctionType
ALU = mybir.AluOpType

P = 128
PACK = 4
TILES = N // P
QUADRANT = 32
LIST_ROWS = 16
BLOCKS = S // P
HALVES = 2
PAIR = 2
LINE = 4
TERM_ORDER = (0, 1, 3, 2)
SCALE_STEP = 8
HALF_SIGNED = ()


def tile_picked_wkv8_none_p_kernel(
    tc, x_words, x_scales, w1, w2, w3, num, den, offs, par, out
):
    nc = tc.nc
    with ExitStack() as ctx:
        keep = ctx.enter_context(tc.tile_pool(name="keep", bufs=1))
        psum = ctx.enter_context(tc.psum_pool(name="psum", bufs=1))

        def sbuf(name, shape=(P, S), dtype=F32, tag=None):
            return keep.tile(list(shape), dtype, name=name, tag=tag or name, align_bytes=64)

        def bank(tag):
            return psum.tile([P, S], F32, name=tag, tag=tag)

        def columns(i, width):
            return slice(i * width, (i + 1) * width)

        def by_tile(ap):
            return ap.rearrange("(p t) s -> t p s", t=TILES)

        offs_sb = keep.tile([P, S // LIST_ROWS], U16, name="offs_sb")
        par_sb = keep.tile([P, S // LIST_ROWS], U16, name="par_sb")
        word_table = sbuf("word_table", (P, T), I32)
        scale_table = sbuf("scale_table", (P, T), U8)
        x_codes = sbuf("x_codes", dtype=U32)
        x_bytes = sbuf("x_bytes", dtype=U8)
        picked_bytes = sbuf("picked_bytes", dtype=U8)
        two = sbuf("two", (P, 1))
        root_scale = sbuf("root_scale", (P, 1))
        ident = sbuf("ident", (P, P))
        weights = {"w1": w1, "w2": w2, "w3": w3}
        raw = {n: sbuf(f"raw_{n}", (P, PACK, N)) for n in weights}
        tables = {"den": den, "num": num}
        window = {(n, t): sbuf(f"{n}{t}", (P, 2 * S)) for n in tables for t in range(TILES)}
        th = sbuf("th", (P, BLOCKS, TILES, P))

        def load_table(n, t):
            nc.sync.dma_start(out=window[n, t][:, :S], in_=by_tile(tables[n])[t])

        def load_weight(n):
            nc.sync.dma_start(out=raw[n][:], in_=weights[n].rearrange("(p j) c -> p j c", j=PACK))

        def load_words():
            nc.sync.dma_start(out=word_table[:], in_=x_words[0].rearrange("p n t -> p (n t)").bitcast(I32))

        def load_scales():
            nc.sync.dma_start(out=scale_table[0:P:SCALE_STEP, :].bitcast(I32), in_=x_scales[0].bitcast(I32))

        def place_scales():
            nc.vector.tensor_copy(x_bytes[:].bitcast(I32), picked_bytes[:].bitcast(I32))
            for r in range(1, PACK):
                nc.sync.dma_start(
                    out=x_bytes[r:P:QUADRANT, :].bitcast(I32), in_=picked_bytes[SCALE_STEP * r : P : QUADRANT, :].bitcast(I32)
                )

        rounded = {}

        def round_half(n, h, copy=nc.vector.tensor_copy, tag=None):
            rounded[n, h] = sbuf(f"rounded_{n}_{h}", (P, PAIR * P, PACK), BF16, tag)
            by_column = raw[n][:].rearrange("p j (m t) -> p m j t", t=TILES)
            copy(out=rounded[n, h][:].rearrange("p (t m) j -> p m j t", t=PAIR), in_=by_column[:, :, :, columns(h, PAIR)])

        def round_in_order(g, copy):
            rounded["w3", g] = sbuf(f"rounded_w3_{g}", (P, P, PACK), BF16)
            copy(
                out=rounded["w3", g][:].rearrange("p (c i) j -> p c j i", i=LINE),
                in_=raw["w3"][:, :, columns(g, P)].rearrange("p j (c i) -> p c j i", i=LINE),
            )

        quant = {n: (sbuf(f"codes_{n}", (P, N), U32), sbuf(f"scales_{n}", (P, N), U8)) for n in weights}

        def quantise(n, h):
            codes, scales = quant[n]
            cols = columns(h, rounded[n, h].shape[1])
            nc.vector.quantize_mx(
                out=codes[:, cols].bitcast(FP8X4), scales=scales[:, cols], in_=rounded[n, h][:].rearrange("p c j -> p (c j)")
            )

        def product(acc, stationary, moving, s_cols, m_cols=slice(0, S)):
            nc.tensor.matmul_mx(
                out=acc,
                lhsT=stationary[0][:, s_cols].bitcast(FP8X4),
                lhsT_scale=stationary[1][:, s_cols],
                rhs=moving[0][:, m_cols].bitcast(FP8X4),
                rhs_scale=moving[1][:, m_cols],
                start=True,
                stop=True,
            )

        def add_turned(acc, addend, opens, closes):
            for b in range(BLOCKS):
                cols = columns(b, P)
                start, stop = opens and b == 0, closes and b == BLOCKS - 1
                nc.tensor.matmul(acc[:, cols], addend[:, cols], ident[:], start=start, stop=stop, is_transpose=True)

        def turned_back(tag, tile):
            acc = bank(tag)
            for b in range(BLOCKS):
                cols = columns(b, P)
                nc.tensor.matmul(acc[:, cols], tile[:, cols], ident[:], start=True, stop=True, is_transpose=True)
            return acc

        x = (x_codes, x_bytes)
        picked, keys, ek, den_sum, num_sum, value, term = {}, {}, {}, {}, {}, {}, {}
        root, inverse, sign, signed, gated, back = {}, {}, {}, {}, {}, {}

        def pick(n, t, engine, tag=None, into=None):
            picked[n, t] = sbuf(f"picked_{n}{t}", tag=tag) if into is None else into
            looked_up = window[n, t][:].indirect(par_sb[:])
            if engine is nc.scalar:
                nc.scalar.activation(picked[n, t][:], looked_up, ACT.Copy)
            else:
                nc.vector.tensor_copy(picked[n, t][:], looked_up)

        def open_numerator(t):
            num_sum[t] = bank(f"num{t}")
            add_turned(num_sum[t], picked["num", t], True, False)

        def pick_words(parts):
            for h in range(parts):
                entries = offs_sb[:, columns(h, S // LIST_ROWS // parts)]
                nc.vector.tensor_copy(x_codes[:, columns(h, S // parts)], word_table[:].bitcast(U32).indirect(entries))

        def key(t, parts=1):
            keys[t] = bank(f"num{TILES - 1}" if t == 0 else f"product{t}")
            for h in range(parts):
                cols = columns(h, S // parts)
                product(keys[t][:, cols], quant["w1"], x, columns(t, P), cols)

        def exponential(t, tag=None):
            ek[t] = sbuf(f"ek{t}", tag=tag)
            nc.scalar.activation(ek[t][:], keys[t][:], ACT.Exp, scale=0.5)

        def denominator(t, engine, tag=None):
            den_sum[t] = sbuf(f"den_sum{t}", tag=tag)
            looked_up = picked["den", t][:] if ("den", t) in picked else window["den", t][:].indirect(par_sb[:])
            engine.tensor_tensor(den_sum[t][:], looked_up, ek[t][:], ALU.add)

        def gate_values(g):
            acc = bank(f"product{g}")
            for b in range(BLOCKS):
                product(acc[:, columns(b, P)], x, quant["w3"], columns(b, P), columns(g, P))
            nc.scalar.activation(
                th[:, :, :, columns(g, P // TILES)], acc[:].rearrange("p (b m t) -> p b t m", b=BLOCKS, t=TILES), ACT.Tanh, scale=0.5
            )

        def take_sign(t, into=None):
            sign[t] = sbuf(f"sign{t}") if into is None else into
            nc.scalar.activation(sign[t][:], den_sum[t][:], ACT.Sign)

        def half_sign(t, tag=None):
            sign[t] = sbuf(f"sign{t}", tag=tag)
            nc.vector.tensor_scalar(sign[t][:], den_sum[t][:], 0.0, 0.5, ALU.is_ge, ALU.subtract)

        def take_root(t, tag=None, parts=1):
            root[t] = sbuf(f"root{t}", tag=tag)
            scale = 1.0 if t in HALF_SIGNED else root_scale[:]
            for h in range(parts):
                cols = columns(h, S // parts)
                nc.scalar.activation(root[t][:, cols], den_sum[t][:, cols], ACT.Abs_reciprocal_sqrt, scale=scale)

        def square(t, tag=None, parts=1):
            inverse[t] = sbuf(f"inverse{t}", tag=tag)
            for h in range(parts):
                cols = columns(h, S // parts)
                nc.scalar.activation(inverse[t][:, cols], root[t][:, cols], ACT.Square)

        def value_product(t):
            value[t] = bank(f"product{t}")
            product(value[t][:], quant["w2"], x, columns(t, P))

        def value_term(t, tag=None):
            term[t] = sbuf(f"term{t}", tag=tag)
            nc.vector.tensor_tensor(term[t][:], value[t][:], ek[t][:], ALU.mult)
            add_turned(num_sum[t], term[t], False, True)

        def gate(t, tag=None):
            gated[t] = sbuf(f"gated{t}", tag=tag)
            by_block = "p (b m) -> p b m"
            gates = th[:, :, t, :]
            nc.vector.scalar_tensor_tensor(
                gated[t][:].rearrange(by_block, m=P), gates, 1.0, num_sum[t][:].rearrange(by_block, m=P), ALU.add, ALU.mult
            )
            back[t] = turned_back(f"num{t}", gated[t])

        def sign_inverse(t, tag=None, parts=1):
            signed[t] = sbuf(f"signed{t}", tag=tag)
            for h in range(parts):
                cols = columns(h, S // parts)
                nc.gpsimd.tensor_tensor(signed[t][:, cols], inverse[t][:, cols], sign[t][:, cols], ALU.mult)

        def sign_numerator(t, tag=None):
            signed[t] = sbuf(f"signed{t}", tag=tag)
            nc.vector.tensor_tensor(signed[t][:], back[t][:], sign[t][:], ALU.mult)
            back[t], signed[t] = signed[t], inverse[t]

        result = {}

        def divide(t, cols=slice(0, S), tag=None):
            if t not in result:
                result[t] = sbuf(f"result{t}", tag=tag)
            nc.vector.tensor_tensor(result[t][:, cols], back[t][:, cols], signed[t][:, cols], ALU.mult)
            nc.sync.dma_start(out=by_tile(out)[t][:, cols], in_=result[t][:, cols])

        nc.gpsimd.memset(scale_table[:].bitcast(I32), 0)
        nc.vector.memset(two[:], 2.0)
        nc.scalar.copy(out=root_scale[:], in_=two[:])
        make_identity(nc, ident[:])
        nc.sync.dma_start(par_sb[:], par)
        load_table("num", 0)
        nc.sync.dma_start(offs_sb[:], offs)
        load_scales()
        load_table("num", 1)
        load_weight("w1")
        load_table("num", 2)
        load_words()
        load_table("num", 3)
        nc.vector.tensor_copy(picked_bytes[:], scale_table[:].indirect(offs_sb[:]))
        place_scales()
        load_table("den", 0)
        load_table("den", 1)
        load_weight("w3")
        load_table("den", 2)
        load_weight("w2")
        load_table("den", 3)

        pick("num", 0, nc.scalar)
        for t in range(1, TILES):
            pick("num", t, nc.scalar)
        for h in range(HALVES):
            round_half("w1", h)
        for h in range(HALVES):
            quantise("w1", h)
        pick_words(HALVES)
        key(0, HALVES)
        for t in range(1, TILES):
            key(t)
        for t in range(TILES - 1):
            open_numerator(t)
        pick("den", 0, nc.vector)
        pick("den", 1, nc.vector)
        exponential(0)
        open_numerator(TILES - 1)
        exponential(1)
        exponential(2)
        denominator(0, nc.vector)
        round_in_order(0, nc.vector.tensor_copy)
        round_in_order(1, nc.vector.tensor_copy)
        round_in_order(2, nc.scalar.copy)
        quantise("w3", 0)
        round_in_order(3, nc.vector.tensor_copy)
        exponential(3, "raw_w3")
        for g in range(1, TILES):
            quantise("w3", g)
        take_sign(0, sbuf("sign0", tag="rounded_w3_0"))
        for g in range(TILES):
            gate_values(g)
        pick("den", 2, nc.vector, "rounded_w3_1")
        denominator(1, nc.gpsimd, "rounded_w3_3")
        for h in range(HALVES):
            round_half("w2", h)
        for h in range(HALVES):
            quantise("w2", h)
        for t in TERM_ORDER:
            value_product(t)
        pick("den", 3, nc.vector, "rounded_w2_0")
        denominator(2, nc.gpsimd, "rounded_w2_1")
        denominator(3, nc.gpsimd)
        take_root(0, "codes_w3")
        take_root(1, "scales_w3")
        square(0)
        take_sign(1)
        square(1)
        take_root(2)
        take_sign(2)
        square(2)
        take_sign(3)
        take_root(3, parts=HALVES)
        square(3, parts=HALVES)
        for t in TERM_ORDER:
            value_term(t)
        for t in (0, 1):
            sign_inverse(t)
        sign_inverse(2, parts=HALVES)
        for t in TERM_ORDER:
            gate(t)
        divide(0)
        divide(1)
        sign_numerator(3)
        for h in range(HALVES):
            divide(2, columns(h, S // HALVES), "den_sum3")
            divide(3, columns(h, S // HALVES))
